import numpy as np, ml_dtypes
CORES = [23,119,17,113]
N = 4
BF = ml_dtypes.bfloat16
def gentries(a):
    return np.ascontiguousarray(a.reshape(8, 16, -1).transpose(0, 2, 1)).reshape(8, -1)
def gtable(e):
    e = np.asarray(e); return np.ascontiguousarray(e.reshape(8, -1, 16).transpose(0, 2, 1)).reshape(128, -1).astype(np.int32)
W, L, P, T = 4096, 256, 16, 6
def place(z, e, kap):
    return ((z * (2 * e + 1)[..., None] >> 5) + z + kap) & (W - 1)
def parts(rng):
    low = rng.random((N, 8, 1, W)) < rng.choice(np.array([0.01, 0.03, 0.06, 0.15, 0.5]), (N, 8, 1, 1))
    x = np.where(low, rng.integers(0, 256, (N, 8, 16, W)), rng.integers(64, 256, (N, 8, 16, W)))
    c = rng.integers(0, W, (N, 8, L, 16)); o = rng.integers(0, W, (N, 8, L, P))
    d = np.where(rng.random((N, 8, 1, L)) < 0.5, rng.integers(1, 49, (N, 8, 16, L)), rng.integers(1, 256, (N, 8, 16, L)))
    return x, c, o, d, rng.integers(0, 16, (N, 8, 16, 1))
def pack(x, c, o, d, w):
    return {"xt": np.ascontiguousarray(x.reshape(N, 128, W)).astype(np.float32).astype(BF), "pk": np.stack([gtable(a.reshape(8, -1)) for a in c]), "po": np.stack([gtable(a.reshape(8, -1)) for a in o]),
            "dm": np.ascontiguousarray(d.reshape(N, 128, L)).astype(np.int32), "wt": np.ascontiguousarray(w.reshape(N, 128, 1)).astype(np.int32)}
def setup_inputs(rng):
    return pack(*parts(rng))
def setup_inputs_ties(rng):
    x, c, o, d, w = parts(rng)
    v = rng.integers(8, 200, (N, 8, 16, 1))
    x = v + np.where(rng.random((N, 8, 1, W)) < 0.75, rng.integers(-1, 2, (N, 8, 1, W)), rng.integers(-1, 2, (N, 8, 16, W)))
    d = v + rng.integers(-1, 2, (N, 8, 16, L))
    few = rng.integers(0, W, 8); few[0] = 0; few[7] = W - 1
    c[:, 1::2] = few[rng.integers(0, 8, (N, 4, L, 16))]; o[:, 1::2] = few[rng.integers(0, 8, (N, 4, L, P))]
    return pack(x, c, o, d, w)
def setup_inputs_corners(rng):
    x, c, o, d, w = parts(rng)
    d = rng.choice(np.array([1, 2, 4, 5, 6, 8, 9, 10, 128, 246, 247, 248, 251, 252, 255]), (N, 8, 16, L))
    d[:, :, :, :8] = 1; d[:, :, :, L - 8:] = 255
    x[:, 0] = x[:, 0, :, :1]
    c[:, 1] = c[:, 1, :, :1]; o[:, 1] = o[:, 1, :, :1]
    o[:, 2] = np.concatenate([c[:, 2, :, ::-1]] * (P // 16), axis=2)
    w[:, 3] = 0; w[:, 4] = 15; w[:, 5] = 0; w[:, 5, 15] = rng.integers(1, 16, (N, 1))
    x[:, 6] = 255 * rng.integers(0, 2, (N, 1, W))
    x[:, 7] = rng.integers(0, 256, (N, 16, W)); c[:, 7] = (W - 1) * rng.integers(0, 2, (N, L, 16)); o[:, 7] = (W - 1) * rng.integers(0, 2, (N, L, P))
    q = int(rng.integers(0, N)); x[q] = x[q, :, :, :1]
    return pack(x, c, o, d, w)
def setup_inputs_ends(rng):
    kind = rng.integers(0, 4, (N, 8, 1, W)); hole = rng.integers(0, 16, (N, 8, 1, W))
    x = np.where(kind == 0, 0, np.where(kind == 1, 1, np.where(kind == 2, rng.integers(0, 2, (N, 8, 16, W)), np.arange(16).reshape(16, 1) != hole)))
    w = rng.integers(0, 2, (N, 8, 16, 1)); w[:, 6] = 0; w[:, 7] = 1; w = 15 * w
    kd = rng.integers(0, 4, (N, 8, 1, L)); d = np.where(kd == 0, 0, np.where(kd == 1, 1, rng.integers(0, 2, (N, 8, 16, L))))
    d[:, :, :, L - 1] = 1; d[:, :, :, L - 2] = 0; d = 1 + 254 * d
    c = (W - 1) * rng.integers(0, 2, (N, 8, L, 16)); o = (W - 1) * rng.integers(0, 2, (N, 8, L, P))
    c[:, :, L - 2:] = 0; c[:, :, L - 2:, 15] = W - 1; c[:, :, L - 1, 2] = W - 1
    o[:, :, L - 2:] = W - 1; o[:, :, L - 2:, P - 1] = 0; o[:, :, L - 1, 1] = 0
    c[0, :, :, 7] = W - 1; o[0, :, :, P - 1] = 0; c[0, 3, 5] = 0
    c[N - 1, :, :, 15] = W - 1; o[N - 1, :, :, P - 1] = 0
    m = rng.random((8, L, 1)) < 0.5; c[1] = np.where(m, 0, W - 1); o[1] = np.where(m, o[1], W - 1)
    e = np.add.reduce(w * d, axis=2) & 1023
    p = place(np.full((N, 8, L, 1), W - 1), e, 0)[..., 0]
    tail = int(np.argmax(place(np.arange(W)[None, :], np.zeros(1, np.int64), 0)[0]))
    for q in (0, 1, N - 1):
        for g in range(8): x[q, g][:, p[q, g]] = 1
        x[q, :, :, 0] = 0
    for q in (0, N - 1):
        c[q, 6, L - 2:, 15] = tail; x[q, 6, :, W - 1] = 1
    return pack(255 * x, c, o, d, w)
def setup_inputs_lull(rng):
    x, c, o, d, w = parts(rng)
    q = int(rng.integers(0, N)); p = (q - 1) % N
    x[q] = np.maximum(x[q], 1); x[:, :, :, :32] = 255; x[p, :, :, :32] = 0; x[q, :, :, :32] = 0
    c[p] = 0; o[q, :, :, P - 2:] = 0; o[q] = rng.permuted(o[q], axis=2)
    still = rng.permutation(8 * L)[:int(rng.integers(1, 32))]; c[q, still // L, still % L] = 0
    return pack(x, c, o, d, w)
def setup_inputs_spread(rng):
    x = np.minimum((np.exp2(8 * rng.random((N, 8, 1, W))) * (0.5 + 0.5 * rng.random((N, 8, 16, W)))).astype(np.int64), 255) * (rng.random((N, 8, 1, W)) > 0.0625)
    c = np.minimum((W * rng.random((N, 8, L, 16)) ** 4).astype(np.int64), W - 1); o = np.minimum((W * rng.random((N, 8, L, P)) ** 4).astype(np.int64), W - 1)
    d = np.minimum(np.maximum(np.exp2(8 * rng.random((N, 8, 16, L))).astype(np.int64), 1), 255)
    w = rng.integers(0, 16, (N, 8, 16, 1)) * (rng.random((N, 8, 16, 1)) < 0.4)
    return pack(x, c, o, d, w)
def check_inputs(d):
    bad = []
    for k, lo, hi in (("xt", 0, 255), ("pk", 0, W - 1), ("po", 0, W - 1), ("dm", 1, 255), ("wt", 0, 15)):
        v = np.asarray(d[k]).astype(np.float64)
        if not np.all((v >= lo) & (v <= hi) & (v == np.floor(v))): bad.append("range of " + k)
    return bad
def picks(x, z, e, kap):
    return np.take(x, place(z, e, kap) + (W * np.arange(8 * N)).reshape(N, 8, 1, 1), axis=0)
def reference(xt, pk, po, dm, wt):
    x = np.ascontiguousarray(xt.astype(np.float32).astype(np.int32).reshape(8 * N, 16, W).transpose(0, 2, 1)).reshape(-1, 16)
    c = np.stack([gentries(a) for a in pk]).astype(np.int64).reshape(N, 8, L, 16)
    o = np.stack([gentries(a) for a in po]).astype(np.int64).reshape(N, 8, L, P)
    D = np.ascontiguousarray(dm.astype(np.int32).reshape(N, 8, 16, L).transpose(0, 1, 3, 2))
    w = wt.astype(np.int32).reshape(N, 8, 1, 16)
    kap = np.zeros((N, 1, 1, 1), np.int64); left = []
    for t in range(T):
        if t > 0: c = np.roll(c, 1, axis=0)
        e = (np.add.reduce(w * D, axis=3) & 1023).astype(np.int64)
        a = picks(x, c, e, kap); b = picks(x, o, e, kap)
        if t >= N:
            m = left[t - N]; y = picks(x, m, e, kap); gone = (m != c)[..., None]
            up = np.max(np.where(gone, -1, a), axis=3) >= np.max(np.where(gone, y, -1), axis=3)
            D = np.minimum(np.maximum(np.where(up, D + 8, D - 8), 1), 255)
        sa = np.add.reduce(np.minimum(a, D[:, :, :, None, :]), axis=4); sb = np.add.reduce(np.minimum(b, D[:, :, :, None, :]), axis=4)
        k = np.argmax(sa, axis=3)[..., None]; j = np.argmin(sb, axis=3)[..., None]
        swap = np.take_along_axis(sa, k, 3) > np.take_along_axis(sb, j, 3)
        ck = np.take_along_axis(c, k, 3); oj = np.take_along_axis(o, j, 3)
        np.put_along_axis(c, k, np.where(swap, oj, ck), 3); np.put_along_axis(o, j, np.where(swap, ck, oj), 3)
        xk = np.take_along_axis(a, k[..., None], 3)[:, :, :, 0]
        D = np.where(swap & (xk >= D), np.maximum(D - 4, 1), D)
        kap = np.add.reduce(swap.reshape(N, -1).astype(np.int64), axis=1).reshape(N, 1, 1, 1) & 31
        left.append(c)
    return {"yc": np.stack([gtable(v.reshape(8, -1)) for v in c]).astype(np.float32), "yo": np.stack([gtable(v.reshape(8, -1)) for v in o]).astype(np.float32),
            "yd": np.ascontiguousarray(D.transpose(0, 1, 3, 2)).reshape(N, 128, L).astype(np.float32)}

@@ -1,0 +1,648 @@
+from concourse.mybir import AluOpType as A, ActivationFunctionType as F, AxisListType as AX
+
+W = 4096
+ZC = 4128
+NT = 6
+NR, NM = 3, 6
+NK, NW, N1 = 3, 2, 2
+LC = 8
+GV = 2
+LEAD = 6
+SCRATCH = {
+    "xt_s": ("sbuf", [128, 4144], "bfloat16"),
+    "wti": ("sbuf", [128, 1], "int32"), "wtf": ("sbuf", [128, 1], "float32"),
+    "dmi": ("sbuf", [128, 8, 32], "int32"),
+    "ci0": ("sbuf", [128, 256], "int32"), "ci1": ("sbuf", [128, 256], "int32"),
+    "cf0": ("sbuf", [128, 256], "float32"), "cf1": ("sbuf", [128, 256], "float32"),
+    "tt0": ("sbuf", [128, 8, 32], "float32"), "tt1": ("sbuf", [128, 8, 32], "float32"),
+    "ywO0": ("sbuf", [128, 128], "float32"), "ywC0": ("sbuf", [128, 128], "float32"),
+    "ywO1": ("sbuf", [128, 128], "float32"), "ywC1": ("sbuf", [128, 128], "float32"),
+    "yO": ("sbuf", [128, 8, 32], "float32"), "yC": ("sbuf", [128, 8, 32], "float32"),
+    "yd_s": ("sbuf", [128, 8, 32], "float32"),
+    "on": ("sbuf", [128, 128], "float32"), "onb": ("sbuf", [128, 128], "bfloat16"),
+    "idf": ("sbuf", [128, 128], "float32"), "idb": ("sbuf", [128, 128], "bfloat16"),
+    "idn": ("sbuf", [128, 128], "bfloat16"), "idm": ("sbuf", [128, 128], "bfloat16"),
+    "shu": ("sbuf", [128, 128], "float32"), "shd": ("sbuf", [128, 128], "float32"),
+    "l00": ("sbuf", [128, 128], "float32"), "l01": ("sbuf", [128, 128], "float32"),
+    "l10": ("sbuf", [128, 128], "float32"), "l11": ("sbuf", [128, 128], "float32"),
+    "blk": ("sbuf", [128, 8], "float32"), "bs": ("sbuf", [128, 8], "float32"), "bw": ("sbuf", [128, 8], "float32"),
+    "pi": ("sbuf", [128, 12], "int32"),
+    "mh": ("sbuf", [128, 4], "float32"), "mh1": ("sbuf", [128, 4], "float32"),
+    "b16i": ("sbuf", [128, 16], "int32"), "b16": ("sbuf", [128, 16], "uint16"), "b8": ("sbuf", [128, 4], "uint16"),
+    "con": ("sbuf", [128, 128], "bfloat16"),
+    "sr": ("sbuf", [128, 2048], "bfloat16"), "wr": ("sbuf", [128, 2048], "bfloat16"),
+    "mkm": ("sbuf", [128, 256], "float32"), "mka": ("sbuf", [128, 128], "float32"),
+    "kc": ("sbuf", [128, 8], "float32"), "kn": ("sbuf", [128, 8], "int32"), "kt": ("sbuf", [128, 8], "float32"),
+}
+for _h in "01":
+    SCRATCH.update({
+        "o" + _h: ("sbuf", [128, 128], "float32"),
+        "d" + _h: ("sbuf", [128, 128], "bfloat16"),
+        "e" + _h: ("sbuf", [128, 8], "float32"), "ei" + _h: ("sbuf", [128, 8], "int32"),
+        "drep" + _h: ("psum", [128, 8, 64], "float32"),
+        "bkO" + _h: ("psum", [128, 512], "float32"), "bkC" + _h: ("psum", [128, 512], "float32"),
+        "cps" + _h: ("psum", [128, 512], "float32"),
+        "ks" + _h: ("sbuf", [128, 256], "float32"),
+        "oh" + _h: ("sbuf", [128, 256], "float32"), "sel" + _h: ("sbuf", [128, 256], "float32"),
+        "rs" + _h: ("sbuf", [128, 256], "float32"), "tz" + _h: ("sbuf", [128, 256], "float32"),
+        "sm" + _h: ("sbuf", [128, 80], "float32"),
+        "si" + _h: ("sbuf", [128, 32], "int32"),
+        "sw" + _h: ("sbuf", [128, 8], "bfloat16"),
+        "xo" + _h: ("sbuf", [128, 8], "uint16"),
+        "u" + _h: ("sbuf", [128, 128], "bfloat16"),
+        "aq" + _h: ("sbuf", [128, 48], "int32"),
+        "ai" + _h: ("sbuf", [128, 48], "int32"), "vv" + _h: ("sbuf", [128, 3, 16], "float32"),
+        "rb" + _h: ("sbuf", [128, 3, 16], "float32"),
+        "gg" + _h: ("sbuf", [128, 48], "float32"), "ne" + _h: ("sbuf", [128, 64], "float32"),
+        "so" + _h: ("sbuf", [128, 48], "uint16"), "sf" + _h: ("sbuf", [128, 48], "float32"),
+        "yg" + _h: ("sbuf", [128, 768], "bfloat16"), "xgi" + _h: ("sbuf", [128, 3, 8, 16], "bfloat16"),
+        "bb" + _h: ("sbuf", [128, 8, 16], "bfloat16"), "up" + _h: ("sbuf", [128, 8, 16], "float32"),
+    })
+    for _l in "OC":
+        SCRATCH.update({
+            "fq" + _l + _h: ("sbuf", [128, 128], "int32"), "f" + _l + _h: ("sbuf", [128, 128], "uint16"),
+            "x" + _l + _h: ("sbuf", [128, 4, 512], "bfloat16"), "mn" + _l + _h: ("sbuf", [128, 8, 256], "bfloat16"),
+            "r" + _l + _h: ("sbuf", [128, 128], "float32"),
+        })
+    SCRATCH["ld" + _h] = ("sbuf", [128, 192 * NT], "float32")
+SEMAPHORES = (["sv", "ss", "sp", "sg", "sent", "lxt", "lwr", "lwt", "ldm", "lpo", "lpk", "oc", "oo", "od"]
+              + ["ar%d%d" % (t, h) for t in range(1, NT) for h in range(2)])
+
+
+def rank_program(g, core, T, topo):
+    rank = T.rank_of(core)
+    if rank is None:
+        return
+    nxt = T.cores[(rank + 1) % len(T.cores)]
+    prv = T.cores[(rank - 1) % len(T.cores)]
+    rid, pid = topo.addr(nxt)[0], topo.addr(nxt)[1]
+    mask = topo.mask(core, nxt)
+    nout, nin = len(topo.engines(core, nxt)), len(topo.engines(prv, core))
+    Q = {"v": g.vector, "s": g.scalar, "p": g.tensor, "g": g, "y": g.sync}
+    S = {"v": T.sem.sv, "s": T.sem.ss, "p": T.sem.sp, "g": T.sem.sg}
+    cnt = {q: 0 for q in Q}
+    known = {q: {} for q in Q}
+    clk, last_w, reads, banks = {}, {}, {}, {}
+
+    def need(q, dep):
+        q2, n = dep
+        if known[q].get(q2, 0) >= n:
+            return
+        Q[q].wait_ge(S[q2], n)
+        known[q][q2] = n
+        for a, m in clk.get(dep, {}).items():
+            if known[q].get(a, 0) < m:
+                known[q][a] = m
+
+    def sync(q, R, Wr, B=()):
+        deps = {}
+        def add(d):
+            if q == "p" and d[0] == "p":
+                return
+            deps[d[0]] = max(deps.get(d[0], 0), d[1])
+        for k in R:
+            if k in last_w:
+                add(last_w[k])
+        for k in Wr:
+            if k in last_w:
+                add(last_w[k])
+            for d in reads.get(k, {}).items():
+                add(d)
+        for b in B:
+            for d in banks.get(b, {}).items():
+                if d[0] != q:
+                    add(d)
+        for d in sorted(deps.items(), key=lambda z: (z[0] == q, z[0])):
+            need(q, d)
+
+    def note(q, n, R, Wr, B=()):
+        for k in R:
+            reads.setdefault(k, {})[q] = n
+        for k in Wr:
+            last_w[k] = (q, n)
+            reads[k] = {}
+        for b in B:
+            banks.setdefault(b, {})[q] = n
+        clk[(q, n)] = dict(known[q])
+
+    buf = [None]
+
+    def later(q, fn):
+        if buf[0] is None:
+            fn()
+        else:
+            buf[0].append((q, fn))
+
+    def seq(*fns):
+        old, buf[0] = buf[0], []
+        for fn in fns:
+            fn[0](*fn[1:])
+        out, buf[0] = buf[0], old
+        return out
+
+    def run(L):
+        for z in L:
+            later(z[0], z[1])
+
+    def split(L, n):
+        k = 0
+        for i, z in enumerate(L):
+            if z[0] == "v":
+                k += 1
+                if k > n:
+                    return L[:i], L[i:]
+        return L, []
+
+    def till_sent(L):
+        i = [z[0] for z in L].index("g") + 1 if "g" in [z[0] for z in L] else 0
+        return L[:i], L[i:]
+
+    def weave(*Ls):
+        items = []
+        for j, L in enumerate(Ls):
+            nv, k = max(1, sum(1 for z in L if z[0] == "v")), 0
+            for i, z in enumerate(L):
+                if z[0] == "v":
+                    k += 1
+                items.append(((k - 0.5) / nv if k else 0.0, j, i, z))
+        run([z[3] for z in sorted(items, key=lambda z: z[:3])])
+
+    def op(q, name, args, R, Wr, B=(), kw=None):
+        later(q, lambda: op_now(q, name, args, R, Wr, B, kw))
+
+    def op_now(q, name, args, R, Wr, B, kw):
+        sync(q, R, Wr, B)
+        cnt[q] += 1
+        m = {"v": {"tt": g.vector.tensor_tensor, "ts": g.vector.tensor_scalar, "cp": g.vector.tensor_copy,
+                   "ms": g.vector.memset, "red": g.vector.tensor_reduce, "scan": g.vector.tensor_tensor_scan,
+                   "tr": g.vector.transpose},
+             "s": {"act": g.scalar.activation}, "p": {"mm": g.tensor.matmul},
+             "g": {"iota": g.iota, "aff": g.affine_select}}[q][name]
+        m(*args, **(kw or {})).then_inc(S[q], 1)
+        note(q, cnt[q], R, Wr, B)
+
+    def v(name, args, R, Wr, B=(), **kw):
+        op("v", name, args, R, Wr, B, kw)
+
+    def load(q, sem, out, in_, keys):
+        Q[q].dma_start(out, in_).then_inc(T.sem[sem], 16)
+        S[sem] = T.sem[sem]
+        for k in keys:
+            last_w[k] = (sem, 16)
+
+    load("y", "lwt", T.wti[:], T.wt[:], ["wti"])
+    load("y", "ldm", T.dmi[:], T.dm[:], ["dmi"])
+    load("s", "lxt", T.xt_s[:, 0:W], T.xt[:], ["xt.m"])
+    load("y", "lpo", T.ci0[:], T.po[:], ["ci0"])
+    load("y", "lpk", T.ci1[:], T.pk[:], ["ci1"])
+    load("s", "lwr", T.xt_s[:, W:W + 32], T.xt[:, 0:32], ["xt.w"])
+    XTK = ["xt.m", "xt.w", "xt.z"]
+    xtab = T.xt_s[:, 0:4144]
+
+    v("ms", (T.on[:], 1.0), [], ["on"])
+    v("ms", (T.wr[:], 0.0), [], ["wr"])
+    op("g", "aff", (T.blk[:], T.on[:, 0:8], [[-16, 8]], A.is_ge, 0.0, 0, 1), ["on"], ["blk"])
+    op("g", "aff", (T.blk[:], T.blk[:], [[16, 8]], A.is_ge, 0.0, 15, -1), ["blk"], ["blk"])
+    op("g", "iota", (T.pi[:, 0:4], [[0, 4]], 0, 1), [], ["pi"])
+    op("g", "iota", (T.b16i[:], [[1, 16]], 0, 0), [], ["b16i"])
+    op("g", "aff", (T.idf[:], T.on[:], [[-1, 128]], A.is_equal, 0.0, 0, 1), ["on"], ["idf"])
+    op("g", "aff", (T.shu[:], T.on[:], [[1, 128]], A.is_equal, 0.0, -16, -1), ["on"], ["shu"])
+    op("g", "aff", (T.shd[:], T.on[:], [[1, 128]], A.is_equal, 0.0, 16, -1), ["on"], ["shd"])
+    op("g", "iota", (T.con[:, 0:64], [[0, 4], [16, 16]], 4, 0), [], ["con.o"], kw={"allow_small_or_imprecise_dtypes": True})
+    op("g", "iota", (T.con[:, 64:128], [[0, 4], [-16, 16]], 244, 0), [], ["con.c"], kw={"allow_small_or_imprecise_dtypes": True})
+    v("ms", (T.onb[:], 1.0), [], ["onb"])
+    v("cp", (T.wtf[:], T.wti[:]), ["wti"], ["wtf"])
+    for h in range(2):
+        v("cp", (T["d%d" % h][:], T.dmi[:, :, 16 * h:16 * h + 16]), ["dmi"], ["d%d" % h])
+    v("ts", (T.bw[:], T.blk[:], T.wtf[:, 0:1], 2.0, A.mult, A.mult), ["blk", "wtf"], ["bw"])
+    for q in range(8):
+        v("ts", (T.wr[:, 16 * q:16 * q + 15 * 129 + 1:129], T.onb[:, 0:16], T.bw[:, q:q + 1], None, A.mult),
+          ["onb", "bw"] + (["wr"] if q == 0 else []), ["wr.%d" % q])
+    WRK = ["wr.%d" % q for q in range(8)]
+    v("cp", (T.cf0[:], T.ci0[:]), ["ci0"], ["cf0"])
+    v("ms", (T.kc[:, 0:1], 0.0), [], ["kc0"])
+    v("cp", (T.b16[:], T.b16i[:]), ["b16i"], ["b16"])
+    v("ts", (T.pi[:, 4:8], T.pi[:, 0:4], 16, None, A.bitwise_and), ["pi"], ["pj"])
+    v("ts", (T.pi[:, 8:12], T.pi[:, 0:4], 7, None, A.bitwise_and), ["pi"], ["p7"])
+    v("ts", (T.mh[:], T.pi[:, 4:8], 0.0, None, A.is_equal), ["pj"], ["mh"])
+    v("ts", (T.mh1[:], T.mh[:], -1.0, 1.0, A.mult, A.add), ["mh"], ["mh1"])
+    for nm, src, m in (("l00", "idf", "mh"), ("l01", "shu", "mh"), ("l10", "shd", "mh1"), ("l11", "idf", "mh1")):
+        v("ts", (T[nm][:], T[src][:], T[m][:, 0:1], None, A.mult), [src, m], [nm])
+
+    def e_sum(h):
+        ep = T["cps%d" % h][:, 256:264]
+        for r in range(16):
+            op("p", "mm", (ep, T.wr[:, 128 * r:128 * r + 128], T["d%d" % h][:, r:128:16], r == 0, r == 15),
+               WRK + ["d%d" % h], ["ep%d" % h], ["cps%d" % h])
+
+    def e_fin(h):
+        v("cp", (T["ei%d" % h][:], T["cps%d" % h][:, 256:264]), ["ep%d" % h], ["ei%d" % h], ["cps%d" % h])
+        v("ts", (T["ei%d" % h][:], T["ei%d" % h][:], 2047, None, A.bitwise_and), ["ei%d" % h], ["ei%d" % h])
+        v("ts", (T["e%d" % h][:], T["ei%d" % h][:], 33.0, None, A.add), ["ei%d" % h], ["e%d" % h])
+
+    def d_rep(h, src="d"):
+        for j in range(4):
+            op("p", "mm", (T["drep%d" % h][:, :, 16 * j:16 * j + 16], T.idb[:], T["%s%d" % (src, h)][:], True, True),
+               ["idb", "%s%d" % (src, h)], ["drep%d" % h], ["drep%d" % h])
+
+    def cards(l, h, t):
+        return (T["o%d" % h][:], "o%d" % h) if l == "O" else (T["ld%d" % h][:, 192 * t:192 * t + 128], "ld%d%d" % (t, h))
+
+    def c_ps(l, h, t):
+        ap, key = cards(l, h, t)
+        c0 = 0 if l == "O" else 128
+        op("p", "mm", (T["cps%d" % h][:, c0:c0 + 128], T.idf[:], ap, True, True), ["idf", key],
+           ["cp%s%d" % (l, h)], ["cps%d" % h])
+
+    def f_pre(l, h, t):
+        ap, key = cards(l, h, t)
+        n = "fq%s%d" % (l, h)
+        v("tt", (T[n][:], T["e%d" % h][:, 0:8].indirect(T.b16[:, 0:8]), ap, A.mult), ["b16", "e%d" % h, key], [n])
+        v("ts", (T[n][:], T[n][:], 5, 4095, A.arith_shift_right, A.bitwise_and), [n], [n])
+
+    def f_add(l, h, t):
+        n = "f%s%d" % (l, h)
+        v("ts", (T[n][:], T["fq%s%d" % (l, h)][:], T.kc[:, t:t + 1], None, A.add), ["fq%s%d" % (l, h), "kc%d" % t], [n])
+
+    def gather(l, h, lo=0, hi=4):
+        for p in range(lo, hi):
+            op("s", "act", (T["x%s%d" % (l, h)][:, p, :], xtab.indirect(T["f%s%d" % (l, h)][:, 32 * p:32 * p + 32]), F.Copy),
+               XTK + ["f%s%d" % (l, h)], ["x%s%d.%d" % (l, h, p)])
+
+    def against(l, h, fn, lo=0, hi=4, step=4):
+        for p in range(lo, hi, step):
+            for bb in range(2):
+                for kq in range(4):
+                    c0 = 256 * bb + 64 * kq
+                    b0, b1 = 2 * p + bb, 2 * (p + step)
+                    v("tt", (T["mn%s%d" % (l, h)][:, b0:b1:2, 64 * kq:64 * kq + 64],
+                             T["x%s%d" % (l, h)][:, p:p + step, c0:c0 + 64],
+                             T["drep%d" % h][:, b0:b1:2, :], fn),
+                      ["x%s%d.%d" % (l, h, i) for i in range(p, p + step)] + ["drep%d" % h],
+                      ["mn%s%d.%d.%d.%d" % (l, h, i, bb, kq) for i in range(p, p + step)], ["drep%d" % h])
+
+    def mn_keys(l, h, lo, hi):
+        return ["mn%s%d.%d.%d.%d" % (l, h, i, bb, kq) for i in range(lo, hi) for bb in range(2) for kq in range(4)]
+
+    def score(l, h, c):
+        bk = "bk%s%d" % (l, h)
+        out = T[bk][:, 64 * c:64 * c + 64]
+        c0 = 0 if l == "O" else 64
+        op("p", "mm", (out, T.onb[0:1, :], T.con[0:1, c0:c0 + 64], True, False),
+           ["onb", "con.o" if l == "O" else "con.c"], ["k" + l + "%d.%d" % (h, c)], [bk])
+        K = mn_keys(l, h, 2 * c, 2 * c + 2)
+        for r in range(16):
+            op("p", "mm", (out, T.sr[:, 128 * r:128 * r + 128], T["mn%s%d" % (l, h)][:, 4 * c:4 * c + 4, r:256:16], False, r == 15),
+               SRK + K, ["k" + l + "%d.%d" % (h, c)], [bk])
+
+    def mins(l, h, step):
+        if step == 4:
+            against(l, h, A.min)
+            score(l, h, 0)
+            score(l, h, 1)
+        else:
+            for c in range(2):
+                against(l, h, A.min, 2 * c, 2 * c + 2, step if c else 2)
+                score(l, h, c)
+
+    def kkeys(l, h):
+        return ["k%s%d.0" % (l, h), "k%s%d.1" % (l, h)]
+
+    def scan(l, h):
+        if l == "O":
+            a = (T["rO%d" % h][:], T.mka[:], T["bkO%d" % h][:, 0:128], 0.0, A.add, A.min)
+        else:
+            a = (T["rC%d" % h][:], T.mkm[:, 0:128], T["bkC%d" % h][:, 0:128], 0.0, A.mult, A.max)
+        v("scan", a, kkeys(l, h) + ["mka" if l == "O" else "mkm"], ["r%s%d" % (l, h)], ["bk%s%d" % (l, h)])
+
+    def k_copy(l, h):
+        c0 = 0 if l == "O" else 128
+        op("s", "act", (T["ks%d" % h][:, c0:c0 + 128], T["bk%s%d" % (l, h)][:, 0:128], F.Copy), kkeys(l, h),
+           ["ks%d.%s" % (h, l)], ["bk%s%d" % (l, h)])
+
+    def thr(h):
+        v("ts", (T["sm%d" % h][:, 0:8], T["rO%d" % h][:, 15:128:16], 256.0, None, A.add), ["rO%d" % h], ["thr%d" % h])
+
+    def swap(h):
+        v("tt", (T["sw%d" % h][:], T["rC%d" % h][:, 15:128:16], T["sm%d" % h][:, 0:8], A.is_ge),
+          ["rC%d" % h, "thr%d" % h], ["sw%d" % h])
+
+    def count(t):
+        for h in range(2):
+            op("p", "mm", (T.cps1[:, 272:280], T.onb[:], T["sw%d" % h][:], h == 0, h == 1), ["onb", "sw%d" % h], ["cnt"], ["cps1"])
+
+    def k_fin(t):
+        c = t + 1
+        v("red", (T.kt[:, c:c + 1], T.cps1[:, 272:280], AX.X, A.add), ["cnt"], ["kt%d" % c], ["cps1"])
+        v("ts", (T.kn[:, c:c + 1], T.kt[:, c:c + 1], -15.5, 0.03125, A.add, A.mult), ["kt%d" % c], ["kn%d" % c])
+        v("ts", (T.kc[:, c:c + 1], T.kn[:, c:c + 1], -32.0, T.kt[:, c:c + 1], A.mult, A.add), ["kn%d" % c, "kt%d" % c], ["kc%d" % c])
+
+    def rest(t, h):
+        last = t == NT - 1
+        sm, si, H = T["sm%d" % h], T["si%d" % h], "%d" % h
+        cps = T["cps%d" % h]
+        v("tt", (sm[:, 8:16], T["rO" + H][:, 15:128:16], T["sw" + H][:], A.mult), ["rO" + H, "sw" + H], ["kmO" + H])
+        v("tt", (sm[:, 16:24], T["rC" + H][:, 15:128:16], T["sw" + H][:], A.mult), ["rC" + H, "sw" + H], ["kmC" + H])
+        rec = 1 <= t <= 4
+        if rec:
+            v("cp", (si[:, 0:8], T["rC" + H][:, 15:128:16]), ["rC" + H], ["ra" + H])
+        v("tt", (T["oh" + H][:], sm[:, 8:24].indirect(T.b16[:, 0:16]), T["ks" + H][:], A.is_equal),
+          ["b16", "kmO" + H, "kmC" + H, "ks" + H + ".O", "ks" + H + ".C"], ["oh" + H])
+        if rec:
+            v("ts", (si[:, 8:16], si[:, 0:8], 240, None, A.bitwise_and), ["ra" + H], ["rb" + H])
+        v("tt", (T["sel" + H][:], T["oh" + H][:], cps[:, 0:256], A.mult), ["oh" + H, "cpO" + H, "cpC" + H], ["sel" + H], ["cps" + H])
+        if rec:
+            v("ts", (sm[:, 56:64], si[:, 8:16], 256.0, 1.0, A.mult, A.add), ["rb" + H], ["rc" + H])
+        v("scan", (T["rs" + H][:], T.mkm[:], T["sel" + H][:], 0.0, A.mult, A.add), ["mkm", "sel" + H], ["rs" + H])
+        if rec:
+            v("tt", (sm[:, 64:72], sm[:, 56:64], T["sw" + H][:], A.mult), ["rc" + H, "sw" + H], ["rd" + H])
+        oj, ck = T["rs" + H][:, 15:128:16], T["rs" + H][:, 143:256:16]
+        lk, l0 = "ld%d%d" % (t, h), 192 * t
+
+        def send():
+            w = 128 + 16 * t
+            sync("g", [lk, lk + "r"] + [lk + "r.%s%d" % (c, t) for c in "ab"], [])
+            g.remote_dma(T["ld" + H][:, l0 + 192:l0 + 192 + w], T["ld" + H][:, l0:l0 + w], T.sem["ar%d%d" % (t + 1, h)],
+                         T.sem.sent, pid, rid, mask)
+
+        def exchange():
+            v("tt", (sm[:, 24:32], ck, oj, A.subtract), ["rs" + H], ["dlO" + H])
+            v("tt", (sm[:, 32:40], oj, ck, A.subtract), ["rs" + H], ["dlC" + H])
+            if rec:
+                c0 = l0 + 128 + 16 * (t - 1)
+                v("tt", (T["ld" + H][:, c0:c0 + 8], sm[:, 64:72], ck, A.add), ["rd" + H, "rs" + H], [lk + "r.a%d" % t])
+                v("tt", (T["ld" + H][:, c0 + 8:c0 + 16], sm[:, 64:72], oj, A.add), ["rd" + H, "rs" + H], [lk + "r.b%d" % t])
+            v("tt", (T["tz" + H][:], sm[:, 24:40].indirect(T.b16[:, 0:16]), T["oh" + H][:], A.mult),
+              ["b16", "dlO" + H, "dlC" + H, "oh" + H], ["tz" + H])
+            cout = T["ywC" + H][:] if last else T["ld" + H][:, l0:l0 + 128]
+            oout = T["ywO" + H][:] if last else T["o" + H][:]
+            v("tt", (cout, T["tz" + H][:, 128:256], cps[:, 128:256], A.add), ["tz" + H, "cpC" + H],
+              ["ywC" + H if last else lk], ["cps" + H])
+            if not last:
+                later("g", send)
+            v("tt", (oout, T["tz" + H][:, 0:128], cps[:, 0:128], A.add), ["tz" + H, "cpO" + H],
+              ["ywO" + H if last else "o" + H], ["cps" + H])
+            if not last and h:
+                c_ps("O", h, t)
+
+        exch = seq((exchange,))
+        dem = seq((v, "tt", (si[:, 16:24], ck, T["e" + H][:, 0:8], A.mult), ["rs" + H, "e" + H], ["q1" + H]),
+                  (v, "ts", (sm[:, 40:48], T["sw" + H][:], -8192.0, 8192.0, A.mult, A.add), ["sw" + H], ["pen" + H]),
+                  (v, "ts", (si[:, 24:32], si[:, 16:24], 5, 4095, A.arith_shift_right, A.bitwise_and), ["q1" + H], ["q2" + H]),
+                  (v, "tt", (sm[:, 48:56], si[:, 24:32], sm[:, 40:48], A.add), ["q2" + H, "pen" + H], ["q3" + H]),
+                  (v, "ts", (T["xo" + H][:], sm[:, 48:56], T.kc[:, t:t + 1], float(ZC), A.add, A.min),
+                   ["q3" + H, "kc%d" % t], ["xo" + H]))
+        weave(exch, dem)
+        v("tt", (T["u" + H][:], xtab.indirect(T["xo" + H][:, 0:8]), T["d" + H][:], A.is_ge), XTK + ["xo" + H, "d" + H], ["u" + H])
+        op("p", "mm", (cps[:, 384:512], T.idb[:], T["d" + H][:], True, False), ["idb", "d" + H], ["dp" + H], ["cps" + H])
+        op("p", "mm", (cps[:, 384:512], T.idn[:], T["u" + H][:], False, True), ["idn", "u" + H], ["dp" + H], ["cps" + H])
+        if last:
+            v("ts", (T.yd_s[:, :, 16 * h:16 * h + 16], cps[:, 384:512], 1.0, None, A.max), ["dp" + H], ["yd." + H], ["cps" + H])
+            return
+        v("ts", (T["d" + H][:], cps[:, 384:512], 1.0, None, A.max), ["dp" + H], ["d" + H], ["cps" + H])
+        e_sum(h)
+        if t + 1 < 4 and h:
+            d_rep(h)
+
+    def next_pool(t, h):
+        e_fin(h)
+        f_pre("O", h, t)
+
+    def arrive(t, h):
+        sem = "ar%d%d" % (t, h)
+
+        def landed():
+            S[sem] = T.sem[sem]
+            last_w["ld%d%d" % (t, h)] = (sem, nin)
+            last_w["ld%d%dr" % (t, h)] = (sem, nin)
+        later("x", landed)
+        c_ps("C", h, t)
+        f_pre("C", h, t)
+
+    def slots_in(t, h):
+        L, rk, c0 = T["ld%d" % h], ["ld%d%dr" % (t, h)], 192 * t + 128 + 16 * (t - 4)
+        v("cp", (T["rb%d" % h][:, :, :], L[:, c0:c0 + 48]), rk, ["rb%d" % h])
+        v("ts", (T["gg%d" % h][:], L[:, c0:c0 + 48], 0.5, None, A.is_ge), rk, ["gg%d" % h])
+
+    def slots(t, h):
+        H, L = "%d" % h, T["ld%d" % h]
+        rk = "ld%d%dr" % (t, h)
+        c0 = 192 * t + 128 + 16 * (t - 4)
+        rb, ne, vv = T["rb" + H], T["ne" + H], T["vv" + H]
+        def k(*i):
+            return ["ne%s%d" % (H, j) for j in i]
+        def n(i, j):
+            return ne[:, 8 * i:8 * j]
+        v("ts", (T["ai" + H][:], L[:, c0:c0 + 48], -1.0, None, A.add), [rk], ["ai" + H])
+        v("tt", (n(1, 3), rb[:, 1:3, 8:16], rb[:, 0:2, 0:8], A.not_equal), ["rb" + H], k(1, 2))
+        v("tt", (n(4, 6), rb[:, 1:3, 0:8], rb[:, 0:2, 8:16], A.not_equal), ["rb" + H], k(4, 5))
+        v("ts", (T["ai" + H][:], T["ai" + H][:], 4095, None, A.bitwise_and), ["ai" + H], ["ai" + H])
+        v("tt", (n(0, 1), rb[:, 2, 0:8], rb[:, 0, 8:16], A.not_equal), ["rb" + H], k(0))
+        v("tt", (n(3, 4), rb[:, 2, 8:16], rb[:, 0, 0:8], A.not_equal), ["rb" + H], k(3))
+        v("tt", (n(6, 7), n(5, 6), n(1, 2), A.is_ge), k(5, 1), k(6))
+        v("tt", (n(7, 8), n(2, 3), n(4, 5), A.is_ge), k(2, 4), k(7))
+        v("tt", (vv[:, 0:2, 8:16], n(4, 6), n(0, 2), A.mult), k(4, 5, 0, 1), ["vv%s0" % H])
+        v("tt", (vv[:, 0:2, 0:8], n(1, 3), n(3, 5), A.mult), k(1, 2, 3, 4), ["vv%s1" % H])
+        v("tt", (vv[:, 2, 0:8], n(0, 1), n(6, 7), A.mult), k(0, 6), ["vv%s2" % H])
+        v("tt", (vv[:, 2, 8:16], n(3, 4), n(7, 8), A.mult), k(3, 7), ["vv%s3" % H])
+        v("tt", (T["aq" + H][:], T["e" + H][:, 0:8].indirect(T.b8[:, 0:3]), T["ai" + H][:], A.mult),
+          ["b8", "e" + H, "ai" + H], ["aq" + H])
+        VV = ["vv%s%d" % (H, i) for i in range(4)]
+        v("tt", (vv[:, :, :], vv[:, :, :], T["gg" + H][:], A.mult), VV + ["gg" + H], ["vv" + H] + VV)
+        v("ts", (T["aq" + H][:], T["aq" + H][:], 5, 4095, A.arith_shift_right, A.bitwise_and), ["aq" + H], ["aq" + H])
+
+    def slots_k(t, h):
+        H = "%d" % h
+        v("ts", (T["sf" + H][:], T["aq" + H][:], T.kc[:, t:t + 1], -float(ZC), A.add, A.add), ["aq" + H, "kc%d" % t], ["sf" + H])
+        v("tt", (T["sf" + H][:], T["sf" + H][:], T["vv" + H][:, :, :], A.mult), ["sf" + H, "vv" + H], ["sf" + H])
+        v("ts", (T["so" + H][:], T["sf" + H][:], float(ZC), None, A.add), ["sf" + H], ["so" + H])
+        op("s", "act", (T["yg" + H][:], xtab.indirect(T["so" + H][:, 0:48]), F.Copy), XTK + ["so" + H], ["yg" + H])
+
+    def step2a(h):
+        H = "%d" % h
+        y, bb, xg = T["yg" + H], T["bb" + H], T["xgi" + H]
+        v("tt", (bb[:, :, :], y[:, 0:128], y[:, 256:384], A.max), ["yg" + H], ["bb" + H])
+        v("tt", (bb[:, :, :], bb[:, :, :], y[:, 512:640], A.max), ["bb" + H, "yg" + H], ["bb" + H])
+        d_rep(h, "bb")
+        against("C", h, A.is_ge, 0, 4, 2)
+        for i in range(3):
+            v("tt", (xg[:, i, :, :], y[:, 256 * i + 128:256 * i + 256], T["drep" + H][:, :, 0:16], A.is_ge),
+              ["drep" + H, "yg" + H], ["xg%s%d" % (H, i)], ["drep" + H])
+        out = T["bkC" + H][:, 0:128]
+        for i in range(3):
+            op("p", "mm", (out, T.idm[:], xg[:, i, :, :], i == 0, False), ["idm", "xg%s%d" % (H, i)], kkeys("C", h), ["bkC" + H])
+        for k in range(16):
+            op("p", "mm", (out, T.idb[:], T["mnC" + H][:, 0:8, 16 * k:16 * k + 16], False, k == 15),
+               ["idb"] + ["mnC%s.%d.%d.%d" % (H, p, q, k // 4) for p in range(4) for q in range(2)], kkeys("C", h), ["bkC" + H])
+
+    def step2b(h):
+        H = "%d" % h
+        u, d = T["up" + H], T["d" + H]
+        U = ["up" + H]
+        v("ts", (u[:, :, :], T["bkC" + H][:, 0:128], 0.5, 16.0, A.is_ge, A.mult), kkeys("C", h), U, ["bkC" + H])
+        v("tt", (u[:, :, :], u[:, :, :], d[:], A.add), U + ["d" + H], U)
+        v("ts", (u[:, :, :], u[:, :, :], -8.0, 1.0, A.add, A.max), U, U)
+        v("ts", (d[:], u[:, :, :], 255.0, None, A.min), U, ["d" + H])
+        d_rep(h)
+
+    def turn(i, srckey, T_in, dest):
+        tt = T["tt%d" % i]
+        for b in range(8):
+            v("tr", (tt[:, b, :], T_in(b)), srckey, ["tt%d.%d" % (i, b)])
+        K = ["tt%d.%d" % (i, b) for b in range(8)]
+        for q in range(2):
+            bk = "bk%s%d" % ("OC"[i], q)
+            for s_ in range(2):
+                op("p", "mm", (T[bk][:, 0:128], T["l%d%d" % (q, s_)][:], tt[:, :, 16 * s_:16 * s_ + 16], s_ == 0, s_ == 1),
+                   ["l%d%d" % (q, s_)] + K, kkeys("OC"[i], q), [bk])
+            out, keys = dest(q)
+            op("s", "act", (out, T[bk][:, 0:128], F.Copy), kkeys("OC"[i], q), keys, [bk])
+
+    def turn_out(l, h):
+        tt, K = T["tt%d" % (l == "C")], ["to%s%d.%d" % (l, h, b) for b in range(4)]
+        for b in range(4):
+            v("tr", (tt[:, 4 * h + b, :], T["yw%s%d" % (l, h)][:, 32 * b:32 * b + 32]), ["yw%s%d" % (l, h)], [K[b]])
+        bk = "bk%s%d" % (l, h)
+        for q in range(2):
+            out = T[bk][:, 64 * q:64 * q + 64]
+            for s_ in range(2):
+                op("p", "mm", (out, T["l%d%d" % (q, s_)][:], tt[:, 4 * h:4 * h + 4, 16 * s_:16 * s_ + 16], s_ == 0, s_ == 1),
+                   ["l%d%d" % (q, s_)] + K, ["k%s%d.%d" % (l, h, q)], [bk])
+        for q in range(2):
+            op("s", "act", (T["y" + l][:, q:8:2, 16 * h:16 * h + 16], T[bk][:, 64 * q:64 * q + 64], F.Copy),
+               ["k%s%d.%d" % (l, h, q)], ["y%s%d%d" % (l, h, q)], [bk])
+
+    SRK = ["sr.%d" % q for q in range(8)]
+    e_sum(0)
+    e_sum(1)
+    turn(0, ["cf0"], lambda b: T.cf0[:, 32 * b:32 * b + 32], lambda q: (T["o%d" % q][:], ["o%d" % q]))
+    v("ms", (T.xt_s[:, ZC:ZC + 16], -1.0), [], ["xt.z"])
+    v("ts", (T.bs[:], T.blk[:], 512.0, None, A.mult), ["blk"], ["bs"])
+    v("ms", (T.sr[:], 0.0), [], ["sr"])
+    v("cp", (T.cf1[:], T.ci1[:]), ["ci1"], ["cf1"])
+    turn(1, ["cf1"], lambda b: T.cf1[:, 32 * b:32 * b + 32], lambda q: (T["ld%d" % q][:, 0:128], ["ld0%d" % q]))
+    for q in range(8):
+        op("s", "act", (T.sr[:, 16 * q:16 * q + 15 * 129 + 1:129], T.onb[:, 0:16], F.Copy, 0.0, T.bs[:, q:q + 1]),
+           ["onb", "bs"] + (["sr"] if q == 0 else []), ["sr.%d" % q])
+    v("cp", (T.idb[:], T.idf[:]), ["idf"], ["idb"])
+    next_pool(0, 0)
+    f_add("O", 0, 0)
+    gather("O", 0)
+    e_fin(1)
+    for h in range(2):
+        d_rep(h)
+        c_ps("O", h, 0)
+        c_ps("C", h, 0)
+    f_pre("C", 0, 0)
+    f_add("C", 0, 0)
+    gather("C", 0, 0, 4 - GV)
+    f_pre("O", 1, 0)
+    f_add("O", 1, 0)
+    gather("O", 1)
+    v("ms", (T.mkm[:], 1.0), [], ["mkm"])
+    v("ms", (T.mka[:], 0.0), [], ["mka"])
+    v("ms", (T.mkm[:, 0:256:16], 0.0), [], ["mkm"])
+    v("ms", (T.mka[:, 0:128:16], 8388608.0), [], ["mka"])
+    v("ts", (T.idn[:], T.idb[:], -4.0, None, A.mult), ["idb"], ["idn"])
+    v("ts", (T.idm[:], T.idb[:], -1.0, None, A.mult), ["idb"], ["idm"])
+    v("cp", (T.b8[:], T.pi[:, 8:12]), ["p7"], ["b8"])
+    f_pre("C", 1, 0)
+    f_add("C", 1, 0)
+    for p in range(4 - GV, 4):
+        v("cp", (T.xC0[:, p, :], xtab.indirect(T.fC0[:, 32 * p:32 * p + 32])), XTK + ["fC0"], ["xC0.%d" % p])
+
+    R = []
+    for t in range(NT):
+        two, more = t >= 4, t < NT - 1
+        kch = []
+        if t > 0:
+            kch = seq((k_fin, t - 1), (f_add, "C" if two else "O", 0, t), (gather, "C" if two else "O", 0))
+        r1, R = split(R, NK)
+        run(r1)
+        if two:
+            run(seq((arrive, t, 0), (slots_in, t, 0)))
+        r1, R = split(R, NW)
+        weave(kch, r1)
+        n1 = seq((next_pool, t - 1, 1), (f_add, "O", 1, t)) if t > 0 else []
+        if t > 0 and not two:
+            r0, R = split(R, N1)
+            run(r0)
+            r1, R = split(R, 3)
+            weave(seq((arrive, t, 0), (f_add, "C", 0, t)), r1)
+            gather("C", 0)
+        if not two:
+            r0, R = split(R, NR)
+            run(r0)
+            m0, m1 = split(seq((mins, "O", 0, 2)), NM)
+            weave(R, m0)
+            run(m1)
+            m0, m1 = split(seq((mins, "C", 0, 2)), 8)
+            weave(n1, m0)
+            if t > 0:
+                gather("O", 1)
+            weave(m1, seq((scan, "O", 0), (thr, 0)))
+            k_copy("O", 0)
+            m0, m1 = split(seq((mins, "O", 1, 2)), LEAD)
+            weave(seq((arrive, t, 1), (f_add, "C", 1, t)) if t > 0 else [], m0)
+            run(seq((scan, "C", 0), (swap, 0), (k_copy, "C", 0), (gather, "C", 1)))
+            weave(seq((rest, t, 0)), m1)
+            c0, c1 = split(seq((mins, "C", 1, 2)), 8)
+            run(c0)
+            m0, m1 = split(c1, LC)
+            run(m0)
+            weave(seq((next_pool, t, 0)), seq((scan, "O", 1), (thr, 1)), m1)
+        else:
+            weave(seq((slots, t, 0), (slots_k, t, 0), (f_add, "O", 0, t)), R)
+            gather("O", 0)
+            sa, sb = split(seq((step2a, 0)), 2)
+            run(sa)
+            run(n1)
+            run(sb)
+            run(seq((arrive, t, 1), (slots_in, t, 1), (f_add, "C", 1, t), (gather, "C", 1)))
+            run(seq((slots, t, 1)))
+            weave(seq((slots_k, t, 1)), seq((step2b, 0)))
+            m0, m1 = split(seq((mins, "C", 0, 4)), 4)
+            run(m0 + m1)
+            sa, sb = split(seq((step2a, 1)), 2)
+            run(sa)
+            run(seq((mins, "O", 0, 4)))
+            run(seq((scan, "C", 0), (k_copy, "C", 0)))
+            run(sb)
+            run(seq((scan, "O", 0), (k_copy, "O", 0), (thr, 0), (swap, 0)))
+            ra, rb = split(seq((rest, t, 0)), 10)
+            gather("O", 1)
+            run(ra)
+            m0, m1 = split(seq((step2b, 1), (mins, "O", 1, 2), (mins, "C", 1, 2)), 4 + 16)
+            weave(rb, m0)
+            c0, c1 = split(m1, 8)
+            run(c0 + c1)
+            run(seq((scan, "O", 1), (thr, 1)))
+            if more:
+                run(seq((next_pool, t, 0)))
+        k_copy("O", 1)
+        scan("C", 1)
+        swap(1)
+        k_copy("C", 1)
+        if more:
+            count(t)
+            c_ps("O", 0, t)
+            if t + 1 < 4:
+                d_rep(0)
+        R = seq((rest, t, 1))
+
+    r0, R = split(R, 15)
+    weave(r0, seq((turn_out, "C", 0), (turn_out, "O", 0)))
+    weave(seq((turn_out, "C", 1), (turn_out, "O", 1)), R)
+    for l, y, sem in (("C", T.yc, "oc"), ("O", T.yo, "oo")):
+        sync("y", ["y%s%d%d" % (l, h, q) for h in range(2) for q in range(2)], [])
+        g.sync.dma_start(y[:], T["y" + l][:]).then_inc(T.sem[sem], 16)
+    sync("s", ["yd.0", "yd.1"], [])
+    g.scalar.dma_start(T.yd[:], T.yd_s[:]).then_inc(T.sem.od, 16)
+    for q in "vspg":
+        g.wait_ge(S[q], cnt[q])
+    g.wait_ge(T.sem.sent, nout * 2 * (NT - 1))
+    for sem in ("lxt", "lwr", "lwt", "ldm", "lpo", "lpk", "oc", "oo", "od"):
+        g.wait_ge(T.sem[sem], 16)
+    for t in range(1, NT):
+        for h in range(2):
+            g.wait_ge(T.sem["ar%d%d" % (t, h)], nin)

@@ -1,72 +1,67 @@
 from concourse.mybir import AluOpType as A, ActivationFunctionType as F, AxisListType as AX
 
 W = 4096
-ZC = 4128
 NT = 6
-NR, NM = 3, 6
-NK, NW, N1 = 3, 2, 2
-LC = 8
-GV = 2
-LEAD = 6
+X0 = 528
+WIN = X0 - 16
+XW = X0 + W + 32
+FLOOR = -2560.0
+M32, M64, M2K = 1.5 * 2 ** 28, 1.5 * 2 ** 29, 1.5 * 2 ** 34
+CR = {"key": (0, 256), "c2k": (256, 384), "c4k": (384, 512), "u": (512, 640), "u5": (640, 768), "s1": (768, 896),
+      "s33": (896, 1024), "big": (1024, 1408), "xo": (1408, 1416), "cnt": (1416, 1424), "off": (1424, 1448)}
+VG = {0: [("O", 0, 1), ("O", 0, 3), ("C", 0, 1), ("C", 0, 3), ("O", 1, 1)],
+      1: [("C", 1, 3)], 2: []}
+SCMP = [1, 3]
+ZQ = "s"
+SLACK = 0.0
+PASSES = 6
 SCRATCH = {
-    "xt_s": ("sbuf", [128, 4144], "bfloat16"),
+    "xt_s": ("sbuf", [128, XW], "bfloat16"),
     "wti": ("sbuf", [128, 1], "int32"), "wtf": ("sbuf", [128, 1], "float32"),
-    "dmi": ("sbuf", [128, 8, 32], "int32"),
-    "ci0": ("sbuf", [128, 256], "int32"), "ci1": ("sbuf", [128, 256], "int32"),
-    "cf0": ("sbuf", [128, 256], "float32"), "cf1": ("sbuf", [128, 256], "float32"),
-    "tt0": ("sbuf", [128, 8, 32], "float32"), "tt1": ("sbuf", [128, 8, 32], "float32"),
-    "ywO0": ("sbuf", [128, 128], "float32"), "ywC0": ("sbuf", [128, 128], "float32"),
-    "ywO1": ("sbuf", [128, 128], "float32"), "ywC1": ("sbuf", [128, 128], "float32"),
-    "yO": ("sbuf", [128, 8, 32], "float32"), "yC": ("sbuf", [128, 8, 32], "float32"),
-    "yd_s": ("sbuf", [128, 8, 32], "float32"),
-    "on": ("sbuf", [128, 128], "float32"), "onb": ("sbuf", [128, 128], "bfloat16"),
-    "idf": ("sbuf", [128, 128], "float32"), "idb": ("sbuf", [128, 128], "bfloat16"),
-    "idn": ("sbuf", [128, 128], "bfloat16"), "idm": ("sbuf", [128, 128], "bfloat16"),
-    "shu": ("sbuf", [128, 128], "float32"), "shd": ("sbuf", [128, 128], "float32"),
-    "l00": ("sbuf", [128, 128], "float32"), "l01": ("sbuf", [128, 128], "float32"),
-    "l10": ("sbuf", [128, 128], "float32"), "l11": ("sbuf", [128, 128], "float32"),
-    "blk": ("sbuf", [128, 8], "float32"), "bs": ("sbuf", [128, 8], "float32"), "bw": ("sbuf", [128, 8], "float32"),
-    "pi": ("sbuf", [128, 12], "int32"),
-    "mh": ("sbuf", [128, 4], "float32"), "mh1": ("sbuf", [128, 4], "float32"),
-    "b16i": ("sbuf", [128, 16], "int32"), "b16": ("sbuf", [128, 16], "uint16"), "b8": ("sbuf", [128, 4], "uint16"),
-    "con": ("sbuf", [128, 128], "bfloat16"),
-    "sr": ("sbuf", [128, 2048], "bfloat16"), "wr": ("sbuf", [128, 2048], "bfloat16"),
-    "mkm": ("sbuf", [128, 256], "float32"), "mka": ("sbuf", [128, 128], "float32"),
-    "kc": ("sbuf", [128, 8], "float32"), "kn": ("sbuf", [128, 8], "int32"), "kt": ("sbuf", [128, 8], "float32"),
+    "dmi": ("sbuf", [128, 256], "int32"), "poi": ("sbuf", [128, 256], "int32"), "pki": ("sbuf", [128, 256], "int32"),
+    "yO": ("sbuf", [128, 256], "float32"), "yC": ("sbuf", [128, 256], "float32"), "yD": ("sbuf", [128, 256], "float32"),
+    "on": ("sbuf", [128, 384], "bfloat16"), "cr": ("sbuf", [128, 1448], "bfloat16"),
+    "blk8": ("sbuf", [128, 8], "bfloat16"), "b64": ("sbuf", [128, 8], "bfloat16"),
+    "blk": ("sbuf", [128, 128], "bfloat16"), "w2": ("sbuf", [128, 128], "bfloat16"),
+    "idb": ("sbuf", [128, 128], "bfloat16"), "idm": ("sbuf", [128, 128], "bfloat16"),
+    "idn": ("sbuf", [128, 128], "bfloat16"), "id16": ("sbuf", [128, 128], "bfloat16"),
+    "c512": ("sbuf", [128, 128], "bfloat16"), "nbk": ("sbuf", [128, 128], "bfloat16"),
+    "tri": ("sbuf", [128, 640], "bfloat16"),
+    "et": ("sbuf", [128, 168], "bfloat16"), "em": ("sbuf", [128, 384], "bfloat16"),
+    "xr": ("sbuf", [128, 2048], "bfloat16"), "sr": ("sbuf", [128, 2048], "bfloat16"), "sk": ("sbuf", [128, 2048], "bfloat16"),
+    "pi": ("sbuf", [128, 8], "int32"), "pf": ("sbuf", [128, 8], "float32"),
+    "mkm": ("sbuf", [128, 128], "float32"), "mka": ("sbuf", [128, 128], "float32"),
+    "kc": ("sbuf", [128, 16], "float32"),
+    "key": ("psum", [128, 512], "float32"), "wu": ("psum", [128, 512], "float32"),
+    "misc": ("psum", [128, 512], "float32"), "p7": ("psum", [128, 512], "float32"),
 }
 for _h in "01":
     SCRATCH.update({
-        "o" + _h: ("sbuf", [128, 128], "float32"),
-        "d" + _h: ("sbuf", [128, 128], "bfloat16"),
-        "e" + _h: ("sbuf", [128, 8], "float32"), "ei" + _h: ("sbuf", [128, 8], "int32"),
-        "drep" + _h: ("psum", [128, 8, 64], "float32"),
-        "bkO" + _h: ("psum", [128, 512], "float32"), "bkC" + _h: ("psum", [128, 512], "float32"),
-        "cps" + _h: ("psum", [128, 512], "float32"),
-        "ks" + _h: ("sbuf", [128, 256], "float32"),
-        "oh" + _h: ("sbuf", [128, 256], "float32"), "sel" + _h: ("sbuf", [128, 256], "float32"),
-        "rs" + _h: ("sbuf", [128, 256], "float32"), "tz" + _h: ("sbuf", [128, 256], "float32"),
-        "sm" + _h: ("sbuf", [128, 80], "float32"),
-        "si" + _h: ("sbuf", [128, 32], "int32"),
-        "sw" + _h: ("sbuf", [128, 8], "bfloat16"),
-        "xo" + _h: ("sbuf", [128, 8], "uint16"),
-        "u" + _h: ("sbuf", [128, 128], "bfloat16"),
-        "aq" + _h: ("sbuf", [128, 48], "int32"),
-        "ai" + _h: ("sbuf", [128, 48], "int32"), "vv" + _h: ("sbuf", [128, 3, 16], "float32"),
-        "rb" + _h: ("sbuf", [128, 3, 16], "float32"),
-        "gg" + _h: ("sbuf", [128, 48], "float32"), "ne" + _h: ("sbuf", [128, 64], "float32"),
-        "so" + _h: ("sbuf", [128, 48], "uint16"), "sf" + _h: ("sbuf", [128, 48], "float32"),
-        "yg" + _h: ("sbuf", [128, 768], "bfloat16"), "xgi" + _h: ("sbuf", [128, 3, 8, 16], "bfloat16"),
-        "bb" + _h: ("sbuf", [128, 8, 16], "bfloat16"), "up" + _h: ("sbuf", [128, 8, 16], "float32"),
+        "drep" + _h: ("psum", [128, 512], "float32"), "cps" + _h: ("psum", [128, 512], "float32"),
+        "o" + _h: ("sbuf", [128, 128], "float16"), "ld" + _h: ("sbuf", [128, 128 * NT], "float16"),
+        "d" + _h: ("sbuf", [128, 128], "bfloat16"), "e" + _h: ("sbuf", [128, 128], "float32"),
+        "eq" + _h: ("sbuf", [128, 128], "float32"),
+        "r" + _h: ("sbuf", [128, 256], "float32"), "tq" + _h: ("sbuf", [128, 16], "float32"),
+        "z" + _h: ("sbuf", [128, 56], "bfloat16"), "zs" + _h: ("sbuf", [128, 128], "bfloat16"),
+        "sel" + _h: ("sbuf", [128, 256], "float16"), "vv" + _h: ("sbuf", [128, 256], "float32"),
+        "xo" + _h: ("sbuf", [128, 8], "uint16"), "u" + _h: ("sbuf", [128, 128], "bfloat16"),
+        "gn" + _h: ("sbuf", [128, 128], "bfloat16"), "fqM" + _h: ("sbuf", [128, 128], "int32"),
+        "fm" + _h: ("sbuf", [128, 128], "float16"), "cl" + _h: ("sbuf", [128, 384], "float16"),
+        "sf" + _h: ("sbuf", [128, 24], "float32"), "so" + _h: ("sbuf", [128, 24], "uint16"),
+        "yy" + _h: ("sbuf", [128, 384], "bfloat16"), "up" + _h: ("sbuf", [128, 128], "bfloat16"),
+        "ge" + _h: ("sbuf", [128, 2048], "bfloat16"),
     })
     for _l in "OC":
         SCRATCH.update({
             "fq" + _l + _h: ("sbuf", [128, 128], "int32"), "f" + _l + _h: ("sbuf", [128, 128], "uint16"),
-            "x" + _l + _h: ("sbuf", [128, 4, 512], "bfloat16"), "mn" + _l + _h: ("sbuf", [128, 8, 256], "bfloat16"),
-            "r" + _l + _h: ("sbuf", [128, 128], "float32"),
+            "x" + _l + _h: ("sbuf", [128, 2064], "bfloat16"), "mn" + _l + _h: ("sbuf", [128, 2048], "bfloat16"),
         })
-    SCRATCH["ld" + _h] = ("sbuf", [128, 192 * NT], "float32")
-SEMAPHORES = (["sv", "ss", "sp", "sg", "sent", "lxt", "lwr", "lwt", "ldm", "lpo", "lpk", "oc", "oo", "od"]
+LOADS = ["lwt", "ldm0", "lpo0", "lxt", "lpk0", "ldm1", "lpo1", "lpk1"]
+STORES = ["s%s%d" % (l, h) for l in "OCD" for h in range(2)]
+SEMAPHORES = (["sv", "ss", "sp", "sg", "sent"] + LOADS + STORES
               + ["ar%d%d" % (t, h) for t in range(1, NT) for h in range(2)])
+
+CYC, PCYC, GATHER, HOP, DMA, FAR = 0.83, 0.5, 1.56, 120.0, 2500.0, 3500.0
 
 
 def rank_program(g, core, T, topo):
@@ -80,568 +75,460 @@ def rank_program(g, core, T, topo):
     nout, nin = len(topo.engines(core, nxt)), len(topo.engines(prv, core))
     Q = {"v": g.vector, "s": g.scalar, "p": g.tensor, "g": g, "y": g.sync}
     S = {"v": T.sem.sv, "s": T.sem.ss, "p": T.sem.sp, "g": T.sem.sg}
-    cnt = {q: 0 for q in Q}
-    known = {q: {} for q in Q}
-    clk, last_w, reads, banks = {}, {}, {}, {}
 
-    def need(q, dep):
-        q2, n = dep
-        if known[q].get(q2, 0) >= n:
-            return
-        Q[q].wait_ge(S[q2], n)
-        known[q][q2] = n
-        for a, m in clk.get(dep, {}).items():
-            if known[q].get(a, 0) < m:
-                known[q][a] = m
+    ops, acc = [], {}
 
-    def sync(q, R, Wr, B=()):
-        deps = {}
-        def add(d):
-            if q == "p" and d[0] == "p":
-                return
-            deps[d[0]] = max(deps.get(d[0], 0), d[1])
-        for k in R:
-            if k in last_w:
-                add(last_w[k])
-        for k in Wr:
-            if k in last_w:
-                add(last_w[k])
-            for d in reads.get(k, {}).items():
-                add(d)
-        for b in B:
-            for d in banks.get(b, {}).items():
-                if d[0] != q:
-                    add(d)
-        for d in sorted(deps.items(), key=lambda z: (z[0] == q, z[0])):
-            need(q, d)
+    def a(name, lo=0, hi=None, step=1, P=128):
+        hi = SCRATCH[name][1][1] if hi is None else hi
+        cols = range(lo, hi, step)
+        bits = ((1 << hi) - (1 << lo)) if step == 1 else sum(1 << c for c in cols)
+        return {"ap": T[name][0:P, lo:hi:step], "rw": [(name, bits)], "n": len(cols), "b": name}
 
-    def note(q, n, R, Wr, B=()):
-        for k in R:
-            reads.setdefault(k, {})[q] = n
-        for k in Wr:
-            last_w[k] = (q, n)
-            reads[k] = {}
-        for b in B:
-            banks.setdefault(b, {})[q] = n
-        clk[(q, n)] = dict(known[q])
+    def ind(win, off):
+        return {"ap": win["ap"].indirect(off["ap"]), "rw": win["rw"] + off["rw"], "n": 16 * off["n"], "b": win["b"], "ind": 1}
 
-    buf = [None]
+    def add(q, calls, R, Wr, cost, sem=None, tail=0.0, after=None):
+        i, deps = len(ops), set()
+        Rl = [z for x in R if isinstance(x, dict) for z in x["rw"]]
+        Wl = [z for x in Wr for z in x["rw"]]
+        for n, bits in Rl:
+            deps.update(j for j, b, w in acc.get(n, []) if w and b & bits)
+        for n, bits in Wl:
+            deps.update(j for j, b, w in acc.get(n, []) if b & bits)
+        for n, bits in Wl:
+            acc[n] = [(j, b & ~bits, w) for j, b, w in acc.get(n, []) if b & ~bits] + [(i, bits, True)]
+        for n, bits in Rl:
+            acc.setdefault(n, []).append((i, bits, False))
+        deps.discard(i)
+        ops.append({"q": q, "calls": calls, "deps": deps, "cost": cost, "sem": sem, "tail": tail,
+                    "after": set() if after is None else {after},
+                    "banks": {n for n, b in Rl + Wl if SCRATCH[n][0] == "psum"}})
+        return i
 
-    def later(q, fn):
-        if buf[0] is None:
-            fn()
-        else:
-            buf[0].append((q, fn))
+    def u(x):
+        return x["ap"] if isinstance(x, dict) else x
 
-    def seq(*fns):
-        old, buf[0] = buf[0], []
-        for fn in fns:
-            fn[0](*fn[1:])
-        out, buf[0] = buf[0], old
-        return out
+    def two(*xs):
+        return all(SCRATCH[x["b"]][2] in ("bfloat16", "float16", "uint16") for x in xs)
 
-    def run(L):
-        for z in L:
-            later(z[0], z[1])
+    def cost(q, out, ins, per):
+        if any("ind" in x for x in ins):
+            return (50 if q == "v" else 65) + out["n"] * GATHER * CYC
+        return max(64, max(x["n"] for x in [out] + ins) * per) * CYC
 
-    def split(L, n):
-        k = 0
-        for i, z in enumerate(L):
-            if z[0] == "v":
-                k += 1
-                if k > n:
-                    return L[:i], L[i:]
-        return L, []
+    def tt(out, x, y, op, after=None):
+        per = 1 if "psum" in (SCRATCH[x["b"]][0], SCRATCH[y["b"]][0]) else 2
+        return add("v", [lambda: g.vector.tensor_tensor(u(out), u(x), u(y), op)], [x, y], [out], cost("v", out, [x], per), after=after)
 
-    def till_sent(L):
-        i = [z[0] for z in L].index("g") + 1 if "g" in [z[0] for z in L] else 0
-        return L[:i], L[i:]
+    def ts(out, x, s1, s2, *op):
+        return add("v", [lambda: g.vector.tensor_scalar(u(out), u(x), u(s1), u(s2), *op)], [x, s1, s2], [out],
+                   cost("v", out, [x], 0.5 if two(out, x) else 1))
 
-    def weave(*Ls):
-        items = []
-        for j, L in enumerate(Ls):
-            nv, k = max(1, sum(1 for z in L if z[0] == "v")), 0
-            for i, z in enumerate(L):
-                if z[0] == "v":
-                    k += 1
-                items.append(((k - 0.5) / nv if k else 0.0, j, i, z))
-        run([z[3] for z in sorted(items, key=lambda z: z[:3])])
+    def cp(out, x, q="v", after=None):
+        if q == "s":
+            return act(out, x, F.Copy, after=after)
+        return add("v", [lambda: g.vector.tensor_copy(u(out), u(x))], [x], [out], cost("v", out, [x], 0.5 if two(out, x) else 1), after=after)
 
-    def op(q, name, args, R, Wr, B=(), kw=None):
-        later(q, lambda: op_now(q, name, args, R, Wr, B, kw))
+    def ms(out, c):
+        return add("v", [lambda: g.vector.memset(u(out), c)], [], [out], cost("v", out, [], 0.5 if two(out) else 1))
 
-    def op_now(q, name, args, R, Wr, B, kw):
-        sync(q, R, Wr, B)
-        cnt[q] += 1
-        m = {"v": {"tt": g.vector.tensor_tensor, "ts": g.vector.tensor_scalar, "cp": g.vector.tensor_copy,
-                   "ms": g.vector.memset, "red": g.vector.tensor_reduce, "scan": g.vector.tensor_tensor_scan,
-                   "tr": g.vector.transpose},
-             "s": {"act": g.scalar.activation}, "p": {"mm": g.tensor.matmul},
-             "g": {"iota": g.iota, "aff": g.affine_select}}[q][name]
-        m(*args, **(kw or {})).then_inc(S[q], 1)
-        note(q, cnt[q], R, Wr, B)
+    def scan(out, d0, d1, op0, op1):
+        return add("v", [lambda: g.vector.tensor_tensor_scan(u(out), u(d0), u(d1), 0.0, op0, op1)], [d0, d1], [out], cost("v", out, [d1], 1))
 
-    def v(name, args, R, Wr, B=(), **kw):
-        op("v", name, args, R, Wr, B, kw)
+    def act(out, x, f, bias=0.0, scale=1.0, after=None):
+        return add("s", [lambda: g.scalar.activation(u(out), u(x), f, bias, scale)], [x], [out], cost("s", out, [x], 1), after=after)
 
-    def load(q, sem, out, in_, keys):
-        Q[q].dma_start(out, in_).then_inc(T.sem[sem], 16)
-        S[sem] = T.sem[sem]
-        for k in keys:
-            last_w[k] = (sem, 16)
+    def mm(*groups):
+        calls, R, Wr, c = [], [], [], 0
+        for grp in groups:
+            for i, (o, l, r) in enumerate(grp):
+                calls.append(lambda o=o, l=l, r=r, st=(i == 0), sp=(i == len(grp) - 1): g.tensor.matmul(u(o), u(l), u(r), st, sp))
+                R += [l, r]
+                Wr.append(o)
+                c += max(min(64, l["n"]), r["n"])
+        return add("p", calls, R, Wr, c * PCYC)
 
-    load("y", "lwt", T.wti[:], T.wt[:], ["wti"])
-    load("y", "ldm", T.dmi[:], T.dm[:], ["dmi"])
-    load("s", "lxt", T.xt_s[:, 0:W], T.xt[:], ["xt.m"])
-    load("y", "lpo", T.ci0[:], T.po[:], ["ci0"])
-    load("y", "lpk", T.ci1[:], T.pk[:], ["ci1"])
-    load("s", "lwr", T.xt_s[:, W:W + 32], T.xt[:, 0:32], ["xt.w"])
-    XTK = ["xt.m", "xt.w", "xt.z"]
-    xtab = T.xt_s[:, 0:4144]
+    def row(out, name, n=None, K=1):
+        lo, hi = CR[name]
+        return (out, a("on", 0, 128, 1, K), a("cr", lo, hi if n is None else lo + n, 1, K))
 
-    v("ms", (T.on[:], 1.0), [], ["on"])
-    v("ms", (T.wr[:], 0.0), [], ["wr"])
-    op("g", "aff", (T.blk[:], T.on[:, 0:8], [[-16, 8]], A.is_ge, 0.0, 0, 1), ["on"], ["blk"])
-    op("g", "aff", (T.blk[:], T.blk[:], [[16, 8]], A.is_ge, 0.0, 15, -1), ["blk"], ["blk"])
-    op("g", "iota", (T.pi[:, 0:4], [[0, 4]], 0, 1), [], ["pi"])
-    op("g", "iota", (T.b16i[:], [[1, 16]], 0, 0), [], ["b16i"])
-    op("g", "aff", (T.idf[:], T.on[:], [[-1, 128]], A.is_equal, 0.0, 0, 1), ["on"], ["idf"])
-    op("g", "aff", (T.shu[:], T.on[:], [[1, 128]], A.is_equal, 0.0, -16, -1), ["on"], ["shu"])
-    op("g", "aff", (T.shd[:], T.on[:], [[1, 128]], A.is_equal, 0.0, 16, -1), ["on"], ["shd"])
-    op("g", "iota", (T.con[:, 0:64], [[0, 4], [16, 16]], 4, 0), [], ["con.o"], kw={"allow_small_or_imprecise_dtypes": True})
-    op("g", "iota", (T.con[:, 64:128], [[0, 4], [-16, 16]], 244, 0), [], ["con.c"], kw={"allow_small_or_imprecise_dtypes": True})
-    v("ms", (T.onb[:], 1.0), [], ["onb"])
-    v("cp", (T.wtf[:], T.wti[:]), ["wti"], ["wtf"])
+    def iota(out, pattern, base, cm):
+        kw = {} if SCRATCH[out["b"]][2] == "int32" else {"allow_small_or_imprecise_dtypes": True}
+        return add("g", [lambda: g.iota(u(out), pattern, base, cm, **kw)], [], [out], 130 + 2 * out["n"] * CYC)
+
+    def aff(out, x, pattern, op, fill, base, cm):
+        return add("g", [lambda: g.affine_select(u(out), u(x), pattern, op, fill, base, cm)], [x], [out], 170 + 2 * out["n"] * CYC)
+
+    def load(sem, out, src, t):
+        return add("y", [lambda: g.sync.dma_start(u(out), src)], [], [out], 60, sem=(sem, 16), tail=t,
+                   after=len(ops) - 1 if ops else None)
+
+    def store(q, sem, dst, x):
+        return add(q, [lambda: Q[q].dma_start(dst, u(x))], [x], [], 60, sem=(sem, 16), tail=DMA)
+
+    load("lwt", a("wti"), T.wt[:], DMA)
+    load("ldm0", a("dmi", 0, 128), T.dm[:, 0:128], DMA)
+    load("lpo0", a("poi", 0, 128), T.po[:, 0:128], DMA + 300)
+    load("lxt", a("xt_s", X0, X0 + W), T.xt[:], DMA + 5500)
+    load("lpk0", a("pki", 0, 128), T.pk[:, 0:128], DMA + 5800)
+    load("ldm1", a("dmi", 128, 256), T.dm[:, 128:256], DMA + 6100)
+    load("lpo1", a("poi", 128, 256), T.po[:, 128:256], DMA + 6400)
+    load("lpk1", a("pki", 128, 256), T.pk[:, 128:256], DMA + 6700)
+
+    on, idb, blk, blk8 = a("on", 0, 128), a("idb"), a("blk"), a("blk8")
+    ms(a("on"), 1.0)
+    aff(blk, on, [[-16, 8], [0, 16]], A.is_ge, 0.0, 0, 1)
+    aff(blk, blk, [[16, 8], [0, 16]], A.is_ge, 0.0, 15, -1)
+    aff(idb, on, [[-1, 128]], A.is_equal, 0.0, 0, 1)
+    iota(a("cr", *CR["s1"], 1, 2), [[0, 128]], -1024, 1025)
+    iota(a("cr", 0, 128, 1, 1), [[0, 8], [1, 16]], 64, 0)
+    iota(a("cr", 128, 256, 1, 1), [[0, 8], [-1, 16]], 63, 0)
+    iota(a("cr", *CR["xo"], 1, 1), [[256, 8]], 0, 0)
+    iota(a("pi", 0, 4), [[0, 4]], 0, 1)
+    for name, c in (("c2k", 2048.0), ("s33", 33.0), ("u", -30720.0), ("cnt", 16.25 / 8), ("c4k", 4096.0), ("u5", -28672.0),
+                    ("big", -8192.0), ("off", -16 * FLOOR)):
+        ms(a("cr", *CR[name], 1, 32), c)
+    ms(a("cr", CR["off"][0] + 8, CR["off"][0] + 16, 1, 32), -15 * FLOOR - 2048)
+    ms(a("xt_s", 0, X0), -1.0)
+    cp(a("wtf"), a("wti"))
+    ts(a("w2"), blk, a("wtf"), 2.0, A.mult, A.mult)
+    cp(blk8, a("blk", 0, 128, 16))
+    ts(a("b64"), blk8, 64.0, None, A.mult)
+    for name, c in (("idm", -1.0), ("idn", -4.0), ("id16", 16.0)):
+        ts(a(name), idb, c, None, A.mult)
+    ms(a("mkm"), 1.0)
+    ms(a("mkm", 0, 128, 16), 0.0)
+    ms(a("mka"), 0.0)
+    ms(a("mka", 0, 128, 16), 8388608.0)
     for h in range(2):
-        v("cp", (T["d%d" % h][:], T.dmi[:, :, 16 * h:16 * h + 16]), ["dmi"], ["d%d" % h])
-    v("ts", (T.bw[:], T.blk[:], T.wtf[:, 0:1], 2.0, A.mult, A.mult), ["blk", "wtf"], ["bw"])
-    for q in range(8):
-        v("ts", (T.wr[:, 16 * q:16 * q + 15 * 129 + 1:129], T.onb[:, 0:16], T.bw[:, q:q + 1], None, A.mult),
-          ["onb", "bw"] + (["wr"] if q == 0 else []), ["wr.%d" % q])
-    WRK = ["wr.%d" % q for q in range(8)]
-    v("cp", (T.cf0[:], T.ci0[:]), ["ci0"], ["cf0"])
-    v("ms", (T.kc[:, 0:1], 0.0), [], ["kc0"])
-    v("cp", (T.b16[:], T.b16i[:]), ["b16i"], ["b16"])
-    v("ts", (T.pi[:, 4:8], T.pi[:, 0:4], 16, None, A.bitwise_and), ["pi"], ["pj"])
-    v("ts", (T.pi[:, 8:12], T.pi[:, 0:4], 7, None, A.bitwise_and), ["pi"], ["p7"])
-    v("ts", (T.mh[:], T.pi[:, 4:8], 0.0, None, A.is_equal), ["pj"], ["mh"])
-    v("ts", (T.mh1[:], T.mh[:], -1.0, 1.0, A.mult, A.add), ["mh"], ["mh1"])
-    for nm, src, m in (("l00", "idf", "mh"), ("l01", "shu", "mh"), ("l10", "shd", "mh1"), ("l11", "idf", "mh1")):
-        v("ts", (T[nm][:], T[src][:], T[m][:, 0:1], None, A.mult), [src, m], [nm])
+        ms(a("z%d" % h, 40, 56), 1.0)
+        ms(a("xC%d" % h, 2048, 2064), -1.0)
+    ts(a("pi", 4, 8), a("pi", 0, 4), 15, None, A.bitwise_and)
+    cp(a("pf", 0, 1), a("pi", 4, 5))
+    ts(a("pf", 1, 2), a("pi", 4, 5), -1.0, -1.0, A.mult, A.add)
+    tt(a("pf", 2, 4), a("pf", 0, 2), a("pf", 0, 2), A.mult)
+    ts(a("pf", 4, 5), a("pi", 4, 5), 16.0, 4095.0, A.mult, A.add)
+    ms(a("et"), 0.0)
+    for i in range(2):
+        for c0, s1, s2 in ((8 * i, a("pf", i, i + 1), -8192.0), (16 + 8 * i, 1.0, 4096.0), (32, 1.0, -4096.0),
+                           (40, a("pf", 2 + i, 3 + i), 4096.0), (48, 1.0, 4096.0)):
+            ts(a("et", 56 * i + c0, 56 * i + c0 + 8), blk8, s1, s2, A.mult, A.mult)
+    ts(a("et", 120, 128), blk8, -1.0, None, A.mult)
+    ts(a("et", 144, 152), blk8, -4096.0, None, A.mult)
+    mm(*[[(a("p7", 128 * i, 128 * i + 128, 1, 56), a("et", 56 * i, 56 * i + 56), idb)] for i in range(3)])
+    cp(a("em", 0, 384, 1, 56), a("p7", 0, 384, 1, 56), "s")
+    for r in range(16):
+        aff(a("xr", 128 * r, 128 * r + 128, 1, 56), a("em", 256, 384, 1, 56), [[0, 8], [1, 16]], A.is_equal, 0.0, -r, 0)
 
-    def e_sum(h):
-        ep = T["cps%d" % h][:, 256:264]
+    def late_constants():
+        cp(a("xt_s", X0 + W, XW), a("xt_s", X0, X0 + 32), "s")
+        ms(a("c512"), 512.0)
+        ts(a("nbk"), blk, -8192.0, None, A.mult)
         for r in range(16):
-            op("p", "mm", (ep, T.wr[:, 128 * r:128 * r + 128], T["d%d" % h][:, r:128:16], r == 0, r == 15),
-               WRK + ["d%d" % h], ["ep%d" % h], ["cps%d" % h])
-
-    def e_fin(h):
-        v("cp", (T["ei%d" % h][:], T["cps%d" % h][:, 256:264]), ["ep%d" % h], ["ei%d" % h], ["cps%d" % h])
-        v("ts", (T["ei%d" % h][:], T["ei%d" % h][:], 2047, None, A.bitwise_and), ["ei%d" % h], ["ei%d" % h])
-        v("ts", (T["e%d" % h][:], T["ei%d" % h][:], 33.0, None, A.add), ["ei%d" % h], ["e%d" % h])
-
-    def d_rep(h, src="d"):
-        for j in range(4):
-            op("p", "mm", (T["drep%d" % h][:, :, 16 * j:16 * j + 16], T.idb[:], T["%s%d" % (src, h)][:], True, True),
-               ["idb", "%s%d" % (src, h)], ["drep%d" % h], ["drep%d" % h])
+            aff(a("sr", 128 * r, 128 * r + 128), blk, [[0, 8], [1, 16]], A.is_equal, 0.0, -r, 0)
+            aff(a("sk", 128 * r, 128 * r + 128), a("c512"), [[-16, 8], [0, 16]], A.is_equal, 0.0, -r, 1)
+        aff(a("tri", 384, 512), a("nbk"), [[1, 128]], A.is_gt, 0.0, 0, -1)
+        aff(a("tri", 512, 640), a("nbk"), [[-1, 128]], A.is_gt, 0.0, 0, 1)
+        for s, (c0, fill) in enumerate(((384, 8192.0), (384, 16384.0), (512, 8192.0))):
+            aff(a("tri", 128 * s, 128 * s + 128), a("tri", c0, c0 + 128), [[1, 128]], A.not_equal, fill, 0, -1)
 
     def cards(l, h, t):
-        return (T["o%d" % h][:], "o%d" % h) if l == "O" else (T["ld%d" % h][:, 192 * t:192 * t + 128], "ld%d%d" % (t, h))
+        return a("o%d" % h) if l == "O" else a("ld%d" % h, 128 * t, 128 * t + 128)
 
-    def c_ps(l, h, t):
-        ap, key = cards(l, h, t)
-        c0 = 0 if l == "O" else 128
-        op("p", "mm", (T["cps%d" % h][:, c0:c0 + 128], T.idf[:], ap, True, True), ["idf", key],
-           ["cp%s%d" % (l, h)], ["cps%d" % h])
+    def half(l):
+        return (0, 128) if l == "O" else (128, 256)
 
-    def f_pre(l, h, t):
-        ap, key = cards(l, h, t)
-        n = "fq%s%d" % (l, h)
-        v("tt", (T[n][:], T["e%d" % h][:, 0:8].indirect(T.b16[:, 0:8]), ap, A.mult), ["b16", "e%d" % h, key], [n])
-        v("ts", (T[n][:], T[n][:], 5, 4095, A.arith_shift_right, A.bitwise_and), [n], [n])
+    def c_ps(l, h, t, c="c2k"):
+        out = a("cps%d" % h, *half(l))
+        mm([row(out, c), (out, idb, cards(l, h, t))])
 
-    def f_add(l, h, t):
-        n = "f%s%d" % (l, h)
-        v("ts", (T[n][:], T["fq%s%d" % (l, h)][:], T.kc[:, t:t + 1], None, A.add), ["fq%s%d" % (l, h), "kc%d" % t], [n])
+    def e_of(h):
+        H = "%d" % h
+        s1, s2 = a("cps" + H, 256, 384), a("cps" + H, 384, 512)
+        mm([row(s1, "s1", K=2), (s1, a("w2"), a("d" + H))], [row(s2, "s33"), (s2, a("w2"), a("d" + H))])
+        ts(a("eq" + H), s1, M2K, M2K, A.add, A.subtract)
+        tt(a("e" + H), s2, a("eq" + H), A.subtract)
 
-    def gather(l, h, lo=0, hi=4):
-        for p in range(lo, hi):
-            op("s", "act", (T["x%s%d" % (l, h)][:, p, :], xtab.indirect(T["f%s%d" % (l, h)][:, 32 * p:32 * p + 32]), F.Copy),
-               XTK + ["f%s%d" % (l, h)], ["x%s%d.%d" % (l, h, p)])
+    def d_rep(h):
+        mm(*[[(a("drep%d" % h, j, 512, 4), idb, a("d%d" % h))] for j in range(4)])
 
-    def against(l, h, fn, lo=0, hi=4, step=4):
-        for p in range(lo, hi, step):
-            for bb in range(2):
-                for kq in range(4):
-                    c0 = 256 * bb + 64 * kq
-                    b0, b1 = 2 * p + bb, 2 * (p + step)
-                    v("tt", (T["mn%s%d" % (l, h)][:, b0:b1:2, 64 * kq:64 * kq + 64],
-                             T["x%s%d" % (l, h)][:, p:p + step, c0:c0 + 64],
-                             T["drep%d" % h][:, b0:b1:2, :], fn),
-                      ["x%s%d.%d" % (l, h, i) for i in range(p, p + step)] + ["drep%d" % h],
-                      ["mn%s%d.%d.%d.%d" % (l, h, i, bb, kq) for i in range(p, p + step)], ["drep%d" % h])
+    def f_pre(src, fq, h):
+        tt(fq, src, a("e%d" % h), A.mult)
+        ts(fq, fq, 5, 4095, A.arith_shift_right, A.bitwise_and)
 
-    def mn_keys(l, h, lo, hi):
-        return ["mn%s%d.%d.%d.%d" % (l, h, i, bb, kq) for i in range(lo, hi) for bb in range(2) for kq in range(4)]
-
-    def score(l, h, c):
-        bk = "bk%s%d" % (l, h)
-        out = T[bk][:, 64 * c:64 * c + 64]
-        c0 = 0 if l == "O" else 64
-        op("p", "mm", (out, T.onb[0:1, :], T.con[0:1, c0:c0 + 64], True, False),
-           ["onb", "con.o" if l == "O" else "con.c"], ["k" + l + "%d.%d" % (h, c)], [bk])
-        K = mn_keys(l, h, 2 * c, 2 * c + 2)
-        for r in range(16):
-            op("p", "mm", (out, T.sr[:, 128 * r:128 * r + 128], T["mn%s%d" % (l, h)][:, 4 * c:4 * c + 4, r:256:16], False, r == 15),
-               SRK + K, ["k" + l + "%d.%d" % (h, c)], [bk])
-
-    def mins(l, h, step):
-        if step == 4:
-            against(l, h, A.min)
-            score(l, h, 0)
-            score(l, h, 1)
+    def with_k(out, x, t):
+        if t == 0:
+            ts(out, x, 16.0, None, A.add)
         else:
-            for c in range(2):
-                against(l, h, A.min, 2 * c, 2 * c + 2, step if c else 2)
-                score(l, h, c)
+            ts(out, x, a("kc", 2 * t, 2 * t + 1), a("kc", 2 * t + 1, 2 * t + 2), A.add, A.subtract)
 
-    def kkeys(l, h):
-        return ["k%s%d.0" % (l, h), "k%s%d.1" % (l, h)]
+    last = {"s": None, "v": None}
 
-    def scan(l, h):
+    def gather(l, h, t, first=False):
+        n = "%s%d" % (l, h)
+        for lo, hi in ((0, 32), (32, 128)) if first else ((0, 128),):
+            with_k(a("f" + n, lo, hi), a("fq" + n, lo, hi), t)
+        win = a("xt_s", WIN, XW if t else X0 + W)
+        for c in range(4):
+            q = "v" if (l, h, c) in VG[min(t, 1) if t < 4 else 2] else "s"
+            i = cp(a("x" + n, 512 * c, 512 * c + 512), ind(win, a("f" + n, 32 * c, 32 * c + 32)), q, last["s"] if q == "s" else None)
+            if q == "s":
+                last["s"] = i
+
+    def mins(l, h, parts):
+        n, lo = "%s%d" % (l, h), 0
+        for w in parts:
+            for j in range(4):
+                last["v"] = tt(a("mn" + n, 16 * lo + j, 16 * (lo + w), 4), a("x" + n, 16 * lo + j, 16 * (lo + w), 4),
+                               a("drep%d" % h, 4 * lo, 4 * (lo + w)), A.min, last["v"])
+            lo += w
+        c0 = 256 * h + half(l)[0]
+        out = a("key", c0, c0 + 128)
+        mm([(out, a("on", 0, 128, 1, 1), a("cr", *half(l), 1, 1))]
+           + [(a("key", c0 + k, c0 + 128, 16), a("mn" + n, k, 2048, 16), a("b64")) for k in range(16)])
         if l == "O":
-            a = (T["rO%d" % h][:], T.mka[:], T["bkO%d" % h][:, 0:128], 0.0, A.add, A.min)
+            scan(a("r%d" % h, 0, 128), a("mka"), out, A.add, A.min)
         else:
-            a = (T["rC%d" % h][:], T.mkm[:, 0:128], T["bkC%d" % h][:, 0:128], 0.0, A.mult, A.max)
-        v("scan", a, kkeys(l, h) + ["mka" if l == "O" else "mkm"], ["r%s%d" % (l, h)], ["bk%s%d" % (l, h)])
-
-    def k_copy(l, h):
-        c0 = 0 if l == "O" else 128
-        op("s", "act", (T["ks%d" % h][:, c0:c0 + 128], T["bk%s%d" % (l, h)][:, 0:128], F.Copy), kkeys(l, h),
-           ["ks%d.%s" % (h, l)], ["bk%s%d" % (l, h)])
-
-    def thr(h):
-        v("ts", (T["sm%d" % h][:, 0:8], T["rO%d" % h][:, 15:128:16], 256.0, None, A.add), ["rO%d" % h], ["thr%d" % h])
+            scan(a("r%d" % h, 128, 256), a("mkm"), out, A.mult, A.max)
 
     def swap(h):
-        v("tt", (T["sw%d" % h][:], T["rC%d" % h][:, 15:128:16], T["sm%d" % h][:, 0:8], A.is_ge),
-          ["rC%d" % h, "thr%d" % h], ["sw%d" % h])
+        tt(a("z%d" % h, 32, 40), a("r%d" % h, 143, 256, 16), a("r%d" % h, 15, 128, 16), A.is_gt)
 
     def count(t):
-        for h in range(2):
-            op("p", "mm", (T.cps1[:, 272:280], T.onb[:], T["sw%d" % h][:], h == 0, h == 1), ["onb", "sw%d" % h], ["cnt"], ["cps1"])
+        out, c = a("misc", 136, 144), 2 * t + 2
+        mm([row(out, "cnt")] + [(out, on, a("z%d" % h, 32, 40)) for h in range(2)])
+        add("v", [lambda: g.vector.tensor_reduce(u(a("kc", c, c + 1)), u(out), AX.X, A.add)], [out], [a("kc", c, c + 1)], 64 * CYC)
+        ts(a("kc", c + 1, c + 2), a("kc", c, c + 1), M32, M32 + 32, A.add, A.subtract)
 
-    def k_fin(t):
-        c = t + 1
-        v("red", (T.kt[:, c:c + 1], T.cps1[:, 272:280], AX.X, A.add), ["cnt"], ["kt%d" % c], ["cps1"])
-        v("ts", (T.kn[:, c:c + 1], T.kt[:, c:c + 1], -15.5, 0.03125, A.add, A.mult), ["kt%d" % c], ["kn%d" % c])
-        v("ts", (T.kc[:, c:c + 1], T.kn[:, c:c + 1], -32.0, T.kt[:, c:c + 1], A.mult, A.add), ["kn%d" % c, "kt%d" % c], ["kc%d" % c])
-
-    def rest(t, h):
-        last = t == NT - 1
-        sm, si, H = T["sm%d" % h], T["si%d" % h], "%d" % h
-        cps = T["cps%d" % h]
-        v("tt", (sm[:, 8:16], T["rO" + H][:, 15:128:16], T["sw" + H][:], A.mult), ["rO" + H, "sw" + H], ["kmO" + H])
-        v("tt", (sm[:, 16:24], T["rC" + H][:, 15:128:16], T["sw" + H][:], A.mult), ["rC" + H, "sw" + H], ["kmC" + H])
-        rec = 1 <= t <= 4
-        if rec:
-            v("cp", (si[:, 0:8], T["rC" + H][:, 15:128:16]), ["rC" + H], ["ra" + H])
-        v("tt", (T["oh" + H][:], sm[:, 8:24].indirect(T.b16[:, 0:16]), T["ks" + H][:], A.is_equal),
-          ["b16", "kmO" + H, "kmC" + H, "ks" + H + ".O", "ks" + H + ".C"], ["oh" + H])
-        if rec:
-            v("ts", (si[:, 8:16], si[:, 0:8], 240, None, A.bitwise_and), ["ra" + H], ["rb" + H])
-        v("tt", (T["sel" + H][:], T["oh" + H][:], cps[:, 0:256], A.mult), ["oh" + H, "cpO" + H, "cpC" + H], ["sel" + H], ["cps" + H])
-        if rec:
-            v("ts", (sm[:, 56:64], si[:, 8:16], 256.0, 1.0, A.mult, A.add), ["rb" + H], ["rc" + H])
-        v("scan", (T["rs" + H][:], T.mkm[:], T["sel" + H][:], 0.0, A.mult, A.add), ["mkm", "sel" + H], ["rs" + H])
-        if rec:
-            v("tt", (sm[:, 64:72], sm[:, 56:64], T["sw" + H][:], A.mult), ["rc" + H, "sw" + H], ["rd" + H])
-        oj, ck = T["rs" + H][:, 15:128:16], T["rs" + H][:, 143:256:16]
-        lk, l0 = "ld%d%d" % (t, h), 192 * t
-
-        def send():
-            w = 128 + 16 * t
-            sync("g", [lk, lk + "r"] + [lk + "r.%s%d" % (c, t) for c in "ab"], [])
-            g.remote_dma(T["ld" + H][:, l0 + 192:l0 + 192 + w], T["ld" + H][:, l0:l0 + w], T.sem["ar%d%d" % (t + 1, h)],
-                         T.sem.sent, pid, rid, mask)
-
-        def exchange():
-            v("tt", (sm[:, 24:32], ck, oj, A.subtract), ["rs" + H], ["dlO" + H])
-            v("tt", (sm[:, 32:40], oj, ck, A.subtract), ["rs" + H], ["dlC" + H])
-            if rec:
-                c0 = l0 + 128 + 16 * (t - 1)
-                v("tt", (T["ld" + H][:, c0:c0 + 8], sm[:, 64:72], ck, A.add), ["rd" + H, "rs" + H], [lk + "r.a%d" % t])
-                v("tt", (T["ld" + H][:, c0 + 8:c0 + 16], sm[:, 64:72], oj, A.add), ["rd" + H, "rs" + H], [lk + "r.b%d" % t])
-            v("tt", (T["tz" + H][:], sm[:, 24:40].indirect(T.b16[:, 0:16]), T["oh" + H][:], A.mult),
-              ["b16", "dlO" + H, "dlC" + H, "oh" + H], ["tz" + H])
-            cout = T["ywC" + H][:] if last else T["ld" + H][:, l0:l0 + 128]
-            oout = T["ywO" + H][:] if last else T["o" + H][:]
-            v("tt", (cout, T["tz" + H][:, 128:256], cps[:, 128:256], A.add), ["tz" + H, "cpC" + H],
-              ["ywC" + H if last else lk], ["cps" + H])
-            if not last:
-                later("g", send)
-            v("tt", (oout, T["tz" + H][:, 0:128], cps[:, 0:128], A.add), ["tz" + H, "cpO" + H],
-              ["ywO" + H if last else "o" + H], ["cps" + H])
-            if not last and h:
+    def exchange(t, h):
+        H, end = "%d" % h, t == NT - 1
+        z, zs, best = "z" + H, a("zs" + H, 0, 128, 1, 56), a("r" + H, 15, 256, 16)
+        ts(a("tq" + H), best, M64, M64, A.add, A.subtract)
+        tt(a(z, 0, 16), best, a("tq" + H), A.subtract)
+        tt(a(z, 16, 32), a(z, 0, 16), a(z, 0, 16), A.mult)
+        mm([(a("misc", 0, 128, 1, 56), a(z), idb)])
+        cp(zs, a("misc", 0, 128, 1, 56), ZQ)
+        em = {l: a("em", *half(l), 1, 56) for l in "OC"}
+        if end:
+            for l in "OC":
+                c_ps(l, h, t, "c4k")
+        mm(*[[(a("wu", *half(l)), idb, cards(l, h, t)), (a("wu", *half(l)), em[l], zs)] for l in "OC"])
+        ts(a("sel" + H), a("wu", 0, 256), 2048.0, None, A.min)
+        for l, m in ("CO", "OC"):
+            out = a("wu", 256 + half(l)[0], 256 + half(l)[1])
+            mm([row(out, "u5" if end else "u"), (out, em[l], zs), (out, blk, a("sel" + H, *half(m)))])
+            tt(a("vv" + H, *half(l)), a("cps" + H, *half(l)), a("sel" + H, *half(l)), A.subtract)
+            new = a("y" + l, 128 * h, 128 * h + 128) if end else cards(l, h, t)
+            tt(new, out, a("vv" + H, *half(l)), A.min)
+            if end:
+                store("y", "s%s%d" % (l, h), T["y" + l.lower()][:, 128 * h:128 * h + 128], new)
+            elif l == "C":
+                send(t, h)
+            else:
                 c_ps("O", h, t)
-
-        exch = seq((exchange,))
-        dem = seq((v, "tt", (si[:, 16:24], ck, T["e" + H][:, 0:8], A.mult), ["rs" + H, "e" + H], ["q1" + H]),
-                  (v, "ts", (sm[:, 40:48], T["sw" + H][:], -8192.0, 8192.0, A.mult, A.add), ["sw" + H], ["pen" + H]),
-                  (v, "ts", (si[:, 24:32], si[:, 16:24], 5, 4095, A.arith_shift_right, A.bitwise_and), ["q1" + H], ["q2" + H]),
-                  (v, "tt", (sm[:, 48:56], si[:, 24:32], sm[:, 40:48], A.add), ["q2" + H, "pen" + H], ["q3" + H]),
-                  (v, "ts", (T["xo" + H][:], sm[:, 48:56], T.kc[:, t:t + 1], float(ZC), A.add, A.min),
-                   ["q3" + H, "kc%d" % t], ["xo" + H]))
-        weave(exch, dem)
-        v("tt", (T["u" + H][:], xtab.indirect(T["xo" + H][:, 0:8]), T["d" + H][:], A.is_ge), XTK + ["xo" + H, "d" + H], ["u" + H])
-        op("p", "mm", (cps[:, 384:512], T.idb[:], T["d" + H][:], True, False), ["idb", "d" + H], ["dp" + H], ["cps" + H])
-        op("p", "mm", (cps[:, 384:512], T.idn[:], T["u" + H][:], False, True), ["idn", "u" + H], ["dp" + H], ["cps" + H])
-        if last:
-            v("ts", (T.yd_s[:, :, 16 * h:16 * h + 16], cps[:, 384:512], 1.0, None, A.max), ["dp" + H], ["yd." + H], ["cps" + H])
+        xo, dp, d = a("misc", 128, 136), a("misc", 256, 384), a("d" + H)
+        mm([row(xo, "xo")] + [(xo, a("xr", 128 * r, 128 * r + 128, 1, 56), a("zs" + H, r, 128, 16, 56)) for r in range(16)])
+        ts(a("xo" + H), xo, a("pf", 4, 5), 2048.0, A.add, A.min)
+        tt(a("u" + H), ind(a("xC" + H), a("xo" + H)), d, A.is_ge)
+        mm([(dp, idb, d), (dp, a("idn"), a("u" + H))])
+        if end:
+            new = a("yD", 128 * h, 128 * h + 128)
+            ts(new, dp, 1.0, None, A.max)
+            store("s" if h else "y", "sD%d" % h, T.yd[:, 128 * h:128 * h + 128], new)
             return
-        v("ts", (T["d" + H][:], cps[:, 384:512], 1.0, None, A.max), ["dp" + H], ["d" + H], ["cps" + H])
-        e_sum(h)
-        if t + 1 < 4 and h:
+        ts(d, dp, 1.0, None, A.max)
+        e_of(h)
+        if t + 1 < 4:
             d_rep(h)
+        f_pre(a("cps" + H, 0, 128), a("fqO" + H), h)
 
-    def next_pool(t, h):
-        e_fin(h)
-        f_pre("O", h, t)
+    def send(t, h):
+        src, dst = cards("C", h, t), cards("C", h, t + 1)
+        sem = "ar%d%d" % (t + 1, h)
+        i = add("g", [lambda: g.remote_dma(u(dst), u(src), T.sem[sem], T.sem.sent, pid, rid, mask)], [src], [], 60, sem=("sent", 0))
+        add("x", [], [], [dst], 0, sem=(sem, nin), tail=FAR + (2000 if t + h == 0 else 0), after=i)
 
     def arrive(t, h):
-        sem = "ar%d%d" % (t, h)
-
-        def landed():
-            S[sem] = T.sem[sem]
-            last_w["ld%d%d" % (t, h)] = (sem, nin)
-            last_w["ld%d%dr" % (t, h)] = (sem, nin)
-        later("x", landed)
         c_ps("C", h, t)
-        f_pre("C", h, t)
-
-    def slots_in(t, h):
-        L, rk, c0 = T["ld%d" % h], ["ld%d%dr" % (t, h)], 192 * t + 128 + 16 * (t - 4)
-        v("cp", (T["rb%d" % h][:, :, :], L[:, c0:c0 + 48]), rk, ["rb%d" % h])
-        v("ts", (T["gg%d" % h][:], L[:, c0:c0 + 48], 0.5, None, A.is_ge), rk, ["gg%d" % h])
+        f_pre(a("cps%d" % h, 128, 256), a("fqC%d" % h), h)
 
     def slots(t, h):
-        H, L = "%d" % h, T["ld%d" % h]
-        rk = "ld%d%dr" % (t, h)
-        c0 = 192 * t + 128 + 16 * (t - 4)
-        rb, ne, vv = T["rb" + H], T["ne" + H], T["vv" + H]
-        def k(*i):
-            return ["ne%s%d" % (H, j) for j in i]
-        def n(i, j):
-            return ne[:, 8 * i:8 * j]
-        v("ts", (T["ai" + H][:], L[:, c0:c0 + 48], -1.0, None, A.add), [rk], ["ai" + H])
-        v("tt", (n(1, 3), rb[:, 1:3, 8:16], rb[:, 0:2, 0:8], A.not_equal), ["rb" + H], k(1, 2))
-        v("tt", (n(4, 6), rb[:, 1:3, 0:8], rb[:, 0:2, 8:16], A.not_equal), ["rb" + H], k(4, 5))
-        v("ts", (T["ai" + H][:], T["ai" + H][:], 4095, None, A.bitwise_and), ["ai" + H], ["ai" + H])
-        v("tt", (n(0, 1), rb[:, 2, 0:8], rb[:, 0, 8:16], A.not_equal), ["rb" + H], k(0))
-        v("tt", (n(3, 4), rb[:, 2, 8:16], rb[:, 0, 0:8], A.not_equal), ["rb" + H], k(3))
-        v("tt", (n(6, 7), n(5, 6), n(1, 2), A.is_ge), k(5, 1), k(6))
-        v("tt", (n(7, 8), n(2, 3), n(4, 5), A.is_ge), k(2, 4), k(7))
-        v("tt", (vv[:, 0:2, 8:16], n(4, 6), n(0, 2), A.mult), k(4, 5, 0, 1), ["vv%s0" % H])
-        v("tt", (vv[:, 0:2, 0:8], n(1, 3), n(3, 5), A.mult), k(1, 2, 3, 4), ["vv%s1" % H])
-        v("tt", (vv[:, 2, 0:8], n(0, 1), n(6, 7), A.mult), k(0, 6), ["vv%s2" % H])
-        v("tt", (vv[:, 2, 8:16], n(3, 4), n(7, 8), A.mult), k(3, 7), ["vv%s3" % H])
-        v("tt", (T["aq" + H][:], T["e" + H][:, 0:8].indirect(T.b8[:, 0:3]), T["ai" + H][:], A.mult),
-          ["b8", "e" + H, "ai" + H], ["aq" + H])
-        VV = ["vv%s%d" % (H, i) for i in range(4)]
-        v("tt", (vv[:, :, :], vv[:, :, :], T["gg" + H][:], A.mult), VV + ["gg" + H], ["vv" + H] + VV)
-        v("ts", (T["aq" + H][:], T["aq" + H][:], 5, 4095, A.arith_shift_right, A.bitwise_and), ["aq" + H], ["aq" + H])
-
-    def slots_k(t, h):
         H = "%d" % h
-        v("ts", (T["sf" + H][:], T["aq" + H][:], T.kc[:, t:t + 1], -float(ZC), A.add, A.add), ["aq" + H, "kc%d" % t], ["sf" + H])
-        v("tt", (T["sf" + H][:], T["sf" + H][:], T["vv" + H][:, :, :], A.mult), ["sf" + H, "vv" + H], ["sf" + H])
-        v("ts", (T["so" + H][:], T["sf" + H][:], float(ZC), None, A.add), ["sf" + H], ["so" + H])
-        op("s", "act", (T["yg" + H][:], xtab.indirect(T["so" + H][:, 0:48]), F.Copy), XTK + ["so" + H], ["yg" + H])
+        m, gn, mp, df = cards("C", h, t - 4), a("gn" + H), a("p7", 0, 128), a("p7", 128, 256)
+        mm([row(mp, "c2k"), (mp, idb, m)], [(df, idb, m), (df, a("idm"), cards("C", h, t))])
+        ts(gn, df, 0.0, None, A.not_equal)
+        f_pre(mp, a("fqM" + H), h)
+        ts(a("fm" + H), a("fqM" + H), -2048.0, None, A.add)
+        grp = [row(a("p7", 128, 512), "big")]
+        for s in range(3):
+            out = a("p7", 128 + 128 * s, 256 + 128 * s)
+            grp += [(out, idb, a("fm" + H)), (out, a("tri", 128 * s, 128 * s + 128), gn)]
+        mm(grp)
+        ts(a("cl" + H), a("p7", 128, 512), FLOOR, 2048.0, A.max, A.min)
+        out = a("misc", 144 + 24 * h, 168 + 24 * h)
+        mm([row(out, "off")] + [(out, a("sr", 128 * r, 128 * r + 128), a("cl" + H, r, 384, 16)) for r in range(16)])
 
-    def step2a(h):
-        H = "%d" % h
-        y, bb, xg = T["yg" + H], T["bb" + H], T["xgi" + H]
-        v("tt", (bb[:, :, :], y[:, 0:128], y[:, 256:384], A.max), ["yg" + H], ["bb" + H])
-        v("tt", (bb[:, :, :], bb[:, :, :], y[:, 512:640], A.max), ["bb" + H, "yg" + H], ["bb" + H])
-        d_rep(h, "bb")
-        against("C", h, A.is_ge, 0, 4, 2)
-        for i in range(3):
-            v("tt", (xg[:, i, :, :], y[:, 256 * i + 128:256 * i + 256], T["drep" + H][:, :, 0:16], A.is_ge),
-              ["drep" + H, "yg" + H], ["xg%s%d" % (H, i)], ["drep" + H])
-        out = T["bkC" + H][:, 0:128]
-        for i in range(3):
-            op("p", "mm", (out, T.idm[:], xg[:, i, :, :], i == 0, False), ["idm", "xg%s%d" % (H, i)], kkeys("C", h), ["bkC" + H])
-        for k in range(16):
-            op("p", "mm", (out, T.idb[:], T["mnC" + H][:, 0:8, 16 * k:16 * k + 16], False, k == 15),
-               ["idb"] + ["mnC%s.%d.%d.%d" % (H, p, q, k // 4) for p in range(4) for q in range(2)], kkeys("C", h), ["bkC" + H])
+    def best_gone(t, h):
+        H, win = "%d" % h, a("xt_s")
+        with_k(a("so" + H), a("misc", 144 + 24 * h, 168 + 24 * h), t)
+        cp(a("yy" + H, 0, 128), ind(win, a("so" + H, 0, 8)))
+        for s in (1, 2):
+            tt(a("yy" + H, 128 * s, 128 * s + 128), ind(win, a("so" + H, 8 * s, 8 * s + 8)), a("yy" + H, 128 * s - 128, 128 * s), A.max)
 
-    def step2b(h):
+    def step2(t, h):
         H = "%d" % h
-        u, d = T["up" + H], T["d" + H]
-        U = ["up" + H]
-        v("ts", (u[:, :, :], T["bkC" + H][:, 0:128], 0.5, 16.0, A.is_ge, A.mult), kkeys("C", h), U, ["bkC" + H])
-        v("tt", (u[:, :, :], u[:, :, :], d[:], A.add), U + ["d" + H], U)
-        v("ts", (u[:, :, :], u[:, :, :], -8.0, 1.0, A.add, A.max), U, U)
-        v("ts", (d[:], u[:, :, :], 255.0, None, A.min), U, ["d" + H])
+        B, gn, d = a("yy" + H, 256, 384), a("gn" + H), a("d" + H)
+        for j in range(4):
+            bank = (("drep0", "drep1"), ("drep1", "p7"))[h][j % 2]
+            x, ge = a("xC" + H, j, 2048, 4), a("ge" + H, j, 2048, 4)
+            parts = [[(a(bank, q, 512, 4), idb, B), (a(bank, q, 512, 4), a("sk", 128 * (4 * q + j), 128 * (4 * q + j) + 128), gn)]
+                     for q in range(4)]
+            if j in SCMP:
+                mm([(a(bank), a("idm"), x)] + [z for p in parts for z in p])
+                act(ge, a(bank), F.Relu, 1.0, -1.0)
+            else:
+                mm(*parts)
+                tt(ge, x, a(bank), A.is_ge)
+        n, dp = a("misc", 384, 512), a("misc", 256, 384)
+        mm([(n, idb, a("ge" + H, k, 2048, 16)) for k in range(16)])
+        ts(a("up" + H), n, 0.5, 0.5, A.is_ge, A.subtract)
+        mm([(dp, idb, d), (dp, a("id16"), a("up" + H))])
+        ts(d, dp, 1.0, 255.0, A.max, A.min)
         d_rep(h)
 
-    def turn(i, srckey, T_in, dest):
-        tt = T["tt%d" % i]
-        for b in range(8):
-            v("tr", (tt[:, b, :], T_in(b)), srckey, ["tt%d.%d" % (i, b)])
-        K = ["tt%d.%d" % (i, b) for b in range(8)]
-        for q in range(2):
-            bk = "bk%s%d" % ("OC"[i], q)
-            for s_ in range(2):
-                op("p", "mm", (T[bk][:, 0:128], T["l%d%d" % (q, s_)][:], tt[:, :, 16 * s_:16 * s_ + 16], s_ == 0, s_ == 1),
-                   ["l%d%d" % (q, s_)] + K, kkeys("OC"[i], q), [bk])
-            out, keys = dest(q)
-            op("s", "act", (out, T[bk][:, 0:128], F.Copy), kkeys("OC"[i], q), keys, [bk])
-
-    def turn_out(l, h):
-        tt, K = T["tt%d" % (l == "C")], ["to%s%d.%d" % (l, h, b) for b in range(4)]
-        for b in range(4):
-            v("tr", (tt[:, 4 * h + b, :], T["yw%s%d" % (l, h)][:, 32 * b:32 * b + 32]), ["yw%s%d" % (l, h)], [K[b]])
-        bk = "bk%s%d" % (l, h)
-        for q in range(2):
-            out = T[bk][:, 64 * q:64 * q + 64]
-            for s_ in range(2):
-                op("p", "mm", (out, T["l%d%d" % (q, s_)][:], tt[:, 4 * h:4 * h + 4, 16 * s_:16 * s_ + 16], s_ == 0, s_ == 1),
-                   ["l%d%d" % (q, s_)] + K, ["k%s%d.%d" % (l, h, q)], [bk])
-        for q in range(2):
-            op("s", "act", (T["y" + l][:, q:8:2, 16 * h:16 * h + 16], T[bk][:, 64 * q:64 * q + 64], F.Copy),
-               ["k%s%d.%d" % (l, h, q)], ["y%s%d%d" % (l, h, q)], [bk])
-
-    SRK = ["sr.%d" % q for q in range(8)]
-    e_sum(0)
-    e_sum(1)
-    turn(0, ["cf0"], lambda b: T.cf0[:, 32 * b:32 * b + 32], lambda q: (T["o%d" % q][:], ["o%d" % q]))
-    v("ms", (T.xt_s[:, ZC:ZC + 16], -1.0), [], ["xt.z"])
-    v("ts", (T.bs[:], T.blk[:], 512.0, None, A.mult), ["blk"], ["bs"])
-    v("ms", (T.sr[:], 0.0), [], ["sr"])
-    v("cp", (T.cf1[:], T.ci1[:]), ["ci1"], ["cf1"])
-    turn(1, ["cf1"], lambda b: T.cf1[:, 32 * b:32 * b + 32], lambda q: (T["ld%d" % q][:, 0:128], ["ld0%d" % q]))
-    for q in range(8):
-        op("s", "act", (T.sr[:, 16 * q:16 * q + 15 * 129 + 1:129], T.onb[:, 0:16], F.Copy, 0.0, T.bs[:, q:q + 1]),
-           ["onb", "bs"] + (["sr"] if q == 0 else []), ["sr.%d" % q])
-    v("cp", (T.idb[:], T.idf[:]), ["idf"], ["idb"])
-    next_pool(0, 0)
-    f_add("O", 0, 0)
-    gather("O", 0)
-    e_fin(1)
     for h in range(2):
+        H = "%d" % h
+        cp(a("d" + H), a("dmi", 128 * h, 128 * h + 128))
+        ts(a("o" + H), a("poi", 128 * h, 128 * h + 128), -2048.0, None, A.add)
+        ts(cards("C", h, 0), a("pki", 128 * h, 128 * h + 128), -2048.0, None, A.add)
+        e_of(h)
         d_rep(h)
         c_ps("O", h, 0)
-        c_ps("C", h, 0)
-    f_pre("C", 0, 0)
-    f_add("C", 0, 0)
-    gather("C", 0, 0, 4 - GV)
-    f_pre("O", 1, 0)
-    f_add("O", 1, 0)
-    gather("O", 1)
-    v("ms", (T.mkm[:], 1.0), [], ["mkm"])
-    v("ms", (T.mka[:], 0.0), [], ["mka"])
-    v("ms", (T.mkm[:, 0:256:16], 0.0), [], ["mkm"])
-    v("ms", (T.mka[:, 0:128:16], 8388608.0), [], ["mka"])
-    v("ts", (T.idn[:], T.idb[:], -4.0, None, A.mult), ["idb"], ["idn"])
-    v("ts", (T.idm[:], T.idb[:], -1.0, None, A.mult), ["idb"], ["idm"])
-    v("cp", (T.b8[:], T.pi[:, 8:12]), ["p7"], ["b8"])
-    f_pre("C", 1, 0)
-    f_add("C", 1, 0)
-    for p in range(4 - GV, 4):
-        v("cp", (T.xC0[:, p, :], xtab.indirect(T.fC0[:, 32 * p:32 * p + 32])), XTK + ["fC0"], ["xC0.%d" % p])
-
-    R = []
+        f_pre(a("cps" + H, 0, 128), a("fqO" + H), h)
     for t in range(NT):
-        two, more = t >= 4, t < NT - 1
-        kch = []
-        if t > 0:
-            kch = seq((k_fin, t - 1), (f_add, "C" if two else "O", 0, t), (gather, "C" if two else "O", 0))
-        r1, R = split(R, NK)
-        run(r1)
-        if two:
-            run(seq((arrive, t, 0), (slots_in, t, 0)))
-        r1, R = split(R, NW)
-        weave(kch, r1)
-        n1 = seq((next_pool, t - 1, 1), (f_add, "O", 1, t)) if t > 0 else []
-        if t > 0 and not two:
-            r0, R = split(R, N1)
-            run(r0)
-            r1, R = split(R, 3)
-            weave(seq((arrive, t, 0), (f_add, "C", 0, t)), r1)
-            gather("C", 0)
-        if not two:
-            r0, R = split(R, NR)
-            run(r0)
-            m0, m1 = split(seq((mins, "O", 0, 2)), NM)
-            weave(R, m0)
-            run(m1)
-            m0, m1 = split(seq((mins, "C", 0, 2)), 8)
-            weave(n1, m0)
-            if t > 0:
-                gather("O", 1)
-            weave(m1, seq((scan, "O", 0), (thr, 0)))
-            k_copy("O", 0)
-            m0, m1 = split(seq((mins, "O", 1, 2)), LEAD)
-            weave(seq((arrive, t, 1), (f_add, "C", 1, t)) if t > 0 else [], m0)
-            run(seq((scan, "C", 0), (swap, 0), (k_copy, "C", 0), (gather, "C", 1)))
-            weave(seq((rest, t, 0)), m1)
-            c0, c1 = split(seq((mins, "C", 1, 2)), 8)
-            run(c0)
-            m0, m1 = split(c1, LC)
-            run(m0)
-            weave(seq((next_pool, t, 0)), seq((scan, "O", 1), (thr, 1)), m1)
+        if t < 4:
+            for h in range(2):
+                gather("O", h, t, h == 0)
+                arrive(t, h)
+                gather("C", h, t)
+                mins("O", h, (64, 64))
+                mins("C", h, (64, 32, 32) if h else (64, 64))
+                swap(h)
+                if h == 0:
+                    exchange(t, 0)
         else:
-            weave(seq((slots, t, 0), (slots_k, t, 0), (f_add, "O", 0, t)), R)
-            gather("O", 0)
-            sa, sb = split(seq((step2a, 0)), 2)
-            run(sa)
-            run(n1)
-            run(sb)
-            run(seq((arrive, t, 1), (slots_in, t, 1), (f_add, "C", 1, t), (gather, "C", 1)))
-            run(seq((slots, t, 1)))
-            weave(seq((slots_k, t, 1)), seq((step2b, 0)))
-            m0, m1 = split(seq((mins, "C", 0, 4)), 4)
-            run(m0 + m1)
-            sa, sb = split(seq((step2a, 1)), 2)
-            run(sa)
-            run(seq((mins, "O", 0, 4)))
-            run(seq((scan, "C", 0), (k_copy, "C", 0)))
-            run(sb)
-            run(seq((scan, "O", 0), (k_copy, "O", 0), (thr, 0), (swap, 0)))
-            ra, rb = split(seq((rest, t, 0)), 10)
-            gather("O", 1)
-            run(ra)
-            m0, m1 = split(seq((step2b, 1), (mins, "O", 1, 2), (mins, "C", 1, 2)), 4 + 16)
-            weave(rb, m0)
-            c0, c1 = split(m1, 8)
-            run(c0 + c1)
-            run(seq((scan, "O", 1), (thr, 1)))
-            if more:
-                run(seq((next_pool, t, 0)))
-        k_copy("O", 1)
-        scan("C", 1)
-        swap(1)
-        k_copy("C", 1)
-        if more:
+            for h in range(2):
+                if h:
+                    arrive(t, h)
+                    slots(t, h)
+                gather("C", h, t, h == 0)
+                best_gone(t, h)
+                gather("O", h, t)
+                step2(t, h)
+            for h in range(2):
+                mins("C", h, (128,))
+                mins("O", h, (128,))
+                swap(h)
+                if h == 0:
+                    exchange(t, 0)
+        if t < NT - 1:
             count(t)
-            c_ps("O", 0, t)
-            if t + 1 < 4:
-                d_rep(0)
-        R = seq((rest, t, 1))
+        if t == 0:
+            late_constants()
+        if 3 <= t < NT - 1:
+            arrive(t + 1, 0)
+            slots(t + 1, 0)
+        exchange(t, 1)
 
-    r0, R = split(R, 15)
-    weave(r0, seq((turn_out, "C", 0), (turn_out, "O", 0)))
-    weave(seq((turn_out, "C", 1), (turn_out, "O", 1)), R)
-    for l, y, sem in (("C", T.yc, "oc"), ("O", T.yo, "oo")):
-        sync("y", ["y%s%d%d" % (l, h, q) for h in range(2) for q in range(2)], [])
-        g.sync.dma_start(y[:], T["y" + l][:]).then_inc(T.sem[sem], 16)
-    sync("s", ["yd.0", "yd.1"], [])
-    g.scalar.dma_start(T.yd[:], T.yd_s[:]).then_inc(T.sem.od, 16)
-    for q in "vspg":
+    n = len(ops)
+    pred, succ = [{} for _ in range(n)], [{} for _ in range(n)]
+    for i, o in enumerate(ops):
+        for j in o["deps"] | o["after"]:
+            lag = 0.0
+            if j in o["deps"] and o["q"] != "x" and not o["q"] == ops[j]["q"] == "p":
+                lag = ops[j]["tail"] + HOP
+            pred[i][j] = succ[j][i] = lag
+
+    def place(before, behind, weight, release):
+        left = [len(b) for b in before]
+        ready = {i: release[i] for i in range(n) if left[i] == 0}
+        free, ends, bank, order, extra = {q: 0.0 for q in "vspgyx"}, [0.0] * n, {}, [], {}
+        while ready:
+            st = {}
+            for i, t0 in ready.items():
+                o = ops[i]
+                st[i] = max([t0, free[o["q"]]] + [ends[j] + HOP for b in o["banks"] for q, j in bank.get(b, {}).items() if q != o["q"]])
+            i0 = min(st, key=st.get)
+            i = max((k for k in st if ops[k]["q"] == ops[i0]["q"] and st[k] <= st[i0] + SLACK), key=lambda k: weight[k])
+            o = ops[i]
+            extra[i] = set()
+            for b in o["banks"]:
+                extra[i] |= {j for q, j in bank.setdefault(b, {}).items() if q != o["q"]}
+                bank[b][o["q"]] = i
+            ends[i] = st[i] + o["cost"]
+            if o["q"] != "x":
+                free[o["q"]] = ends[i]
+            order.append(i)
+            del ready[i]
+            for k in behind[i]:
+                left[k] -= 1
+                if left[k] == 0:
+                    ready[k] = max([release[k]] + [ends[j] + lag for j, lag in before[k].items()])
+        return order, ends, extra
+
+    tails, zero = [o["tail"] for o in ops], [0.0] * n
+    weight = [0.0] * n
+    for i in range(n - 1, -1, -1):
+        weight[i] = ops[i]["cost"] + max([tails[i]] + [weight[k] + lag for k, lag in succ[i].items()])
+    best = None
+    for _ in range(PASSES):
+        order, ends, extra = place(pred, succ, weight, zero)
+        total = max(e + t for e, t in zip(ends, tails))
+        if best is None or total < best[0]:
+            best = (total, order, ends, extra)
+        weight = place(succ, pred, ends, tails)[1]
+    total, order, done, extra = best
+    for i in order:
+        ops[i]["deps"] = ops[i]["deps"] | extra[i]
+
+    pos, known, clock, waits, seen = {}, {q: {} for q in "vspgyx"}, {}, {}, {q: 0 for q in "vspgyx"}
+    for i in order:
+        o = ops[i]
+        q = o["q"]
+        seen[q] += 1
+        pos[i] = (o["sem"][0], 1) if o["sem"] else (q, seen[q])
+        waits[i] = []
+        for j in sorted(o["deps"], key=lambda j: -done[j]):
+            c, m = pos[j]
+            if q != "x" and not (q == c == "p") and known[q].get(c, 0) < m:
+                waits[i].append(j)
+                known[q][c] = m
+                for c2, m2 in clock[j].items():
+                    known[q][c2] = max(known[q].get(c2, 0), m2)
+        clock[i] = dict(known[q]) if q != "x" else {}
+    final = {ops[i]["q"]: i for i in order if not ops[i]["sem"]}
+    wanted = {j for w in waits.values() for j in w} | set(final.values())
+    cnt, val = {q: 0 for q in S}, {}
+    for i in order:
+        o = ops[i]
+        q = o["q"]
+        for j in waits[i]:
+            Q[q].wait_ge(*val[j])
+        call = None
+        for fn in o["calls"]:
+            call = fn()
+        if o["sem"]:
+            val[i] = (T.sem[o["sem"][0]], o["sem"][1])
+            if o["sem"][1] and call is not None:
+                call.then_inc(*val[i])
+        elif i in wanted:
+            cnt[q] += 1
+            call.then_inc(S[q], 1)
+            val[i] = (S[q], cnt[q])
+    for q in S:
         g.wait_ge(S[q], cnt[q])
     g.wait_ge(T.sem.sent, nout * 2 * (NT - 1))
-    for sem in ("lxt", "lwr", "lwt", "ldm", "lpo", "lpk", "oc", "oo", "od"):
+    for sem in LOADS + STORES:
         g.wait_ge(T.sem[sem], 16)
     for t in range(1, NT):
         for h in range(2):

@@ -9,19 +9,27 @@ FLOOR = -2560.0
 M32, M64, M2K = 1.5 * 2 ** 28, 1.5 * 2 ** 29, 1.5 * 2 ** 34
 CR = {"key": (0, 256), "c2k": (256, 384), "c4k": (384, 512), "u": (512, 640), "u5": (640, 768), "s1": (768, 896),
       "s33": (896, 1024), "big": (1024, 1408), "xo": (1408, 1416), "cnt": (1416, 1424), "off": (1424, 1448)}
-VG = {0: [("O", 0, 1), ("O", 0, 3), ("C", 0, 1), ("C", 0, 3), ("O", 1, 1)],
-      1: [("C", 1, 3)], 2: []}
-SCMP = [1, 3]
+VG = {0: [("O", 0, 1), ("C", 0, 1)],
+      1: [("O", 0, 0)], 2: []}
+SMIN = {"O": [1], "C": [1]}
+ORDER2 = [("C", 0), ("O", 0), ("C", 1), ("O", 1)]
+YQ = "v"
+SCMP = [[], [3]]
 ZQ = "s"
 SLACK = 0.0
 PASSES = 6
+BANKS = [["drep0", "drep1", "drep0", "drep1"], ["drep1", "p7", "drep1", "p7"]]
+ML = ["CO", "CO"]
+PO = [(64, 64), (64, 64)]
+PC = [(64, 64), (64, 32, 32)]
+P2 = (128,)
 SCRATCH = {
     "xt_s": ("sbuf", [128, XW], "bfloat16"),
     "wti": ("sbuf", [128, 1], "int32"), "wtf": ("sbuf", [128, 1], "float32"),
     "dmi": ("sbuf", [128, 256], "int32"), "poi": ("sbuf", [128, 256], "int32"), "pki": ("sbuf", [128, 256], "int32"),
     "yO": ("sbuf", [128, 256], "float32"), "yC": ("sbuf", [128, 256], "float32"), "yD": ("sbuf", [128, 256], "float32"),
     "on": ("sbuf", [128, 384], "bfloat16"), "cr": ("sbuf", [128, 1448], "bfloat16"),
-    "blk8": ("sbuf", [128, 8], "bfloat16"), "b64": ("sbuf", [128, 8], "bfloat16"),
+    "blk8": ("sbuf", [128, 8], "bfloat16"), "b64": ("sbuf", [128, 16], "bfloat16"),
     "blk": ("sbuf", [128, 128], "bfloat16"), "w2": ("sbuf", [128, 128], "bfloat16"),
     "idb": ("sbuf", [128, 128], "bfloat16"), "idm": ("sbuf", [128, 128], "bfloat16"),
     "idn": ("sbuf", [128, 128], "bfloat16"), "id16": ("sbuf", [128, 128], "bfloat16"),
@@ -48,7 +56,7 @@ for _h in "01":
         "gn" + _h: ("sbuf", [128, 128], "bfloat16"), "fqM" + _h: ("sbuf", [128, 128], "int32"),
         "fm" + _h: ("sbuf", [128, 128], "float16"), "cl" + _h: ("sbuf", [128, 384], "float16"),
         "sf" + _h: ("sbuf", [128, 24], "float32"), "so" + _h: ("sbuf", [128, 24], "uint16"),
-        "yy" + _h: ("sbuf", [128, 384], "bfloat16"), "up" + _h: ("sbuf", [128, 128], "bfloat16"),
+        "yy" + _h: ("sbuf", [128, 384], "bfloat16"), "up" + _h: ("sbuf", [128, 256], "bfloat16"),
         "ge" + _h: ("sbuf", [128, 2048], "bfloat16"),
     })
     for _l in "OC":
@@ -102,7 +110,7 @@ def rank_program(g, core, T, topo):
         deps.discard(i)
         ops.append({"q": q, "calls": calls, "deps": deps, "cost": cost, "sem": sem, "tail": tail,
                     "after": set() if after is None else {after},
-                    "banks": {n for n, b in Rl + Wl if SCRATCH[n][0] == "psum"}})
+                    "banks": {n for n, b in Rl + Wl if n in SCRATCH and SCRATCH[n][0] == "psum"}})
         return i
 
     def u(x):
@@ -138,15 +146,17 @@ def rank_program(g, core, T, topo):
     def act(out, x, f, bias=0.0, scale=1.0, after=None):
         return add("s", [lambda: g.scalar.activation(u(out), u(x), f, bias, scale)], [x], [out], cost("s", out, [x], 1), after=after)
 
-    def mm(*groups):
+    def mm(*groups, opens=True, closes=True):
         calls, R, Wr, c = [], [], [], 0
         for grp in groups:
             for i, (o, l, r) in enumerate(grp):
-                calls.append(lambda o=o, l=l, r=r, st=(i == 0), sp=(i == len(grp) - 1): g.tensor.matmul(u(o), u(l), u(r), st, sp))
+                st, sp = opens and i == 0, closes and i == len(grp) - 1
+                calls.append(lambda o=o, l=l, r=r, st=st, sp=sp: g.tensor.matmul(u(o), u(l), u(r), st, sp))
                 R += [l, r]
                 Wr.append(o)
                 c += max(min(64, l["n"]), r["n"])
-        return add("p", calls, R, Wr, c * PCYC)
+        lock = {"rw": [("open " + Wr[0]["b"], 1)]}
+        return add("p", calls, R + [lock], Wr + [lock] * (not (opens and closes)), c * PCYC)
 
     def row(out, name, n=None, K=1):
         lo, hi = CR[name]
@@ -193,7 +203,8 @@ def rank_program(g, core, T, topo):
     cp(a("wtf"), a("wti"))
     ts(a("w2"), blk, a("wtf"), 2.0, A.mult, A.mult)
     cp(blk8, a("blk", 0, 128, 16))
-    ts(a("b64"), blk8, 64.0, None, A.mult)
+    ts(a("b64", 0, 8), blk8, 64.0, None, A.mult)
+    ts(a("b64", 8, 16), blk8, -64.0, None, A.mult)
     for name, c in (("idm", -1.0), ("idn", -4.0), ("id16", 16.0)):
         ts(a(name), idb, c, None, A.mult)
     ms(a("mkm"), 1.0)
@@ -275,17 +286,29 @@ def rank_program(g, core, T, topo):
             if q == "s":
                 last["s"] = i
 
-    def mins(l, h, parts):
-        n, lo = "%s%d" % (l, h), 0
+    def mins(l, h, parts, by_s=()):
+        n, lo, d = "%s%d" % (l, h), 0, a("d%d" % h)
+        js = [j for j in range(4) if j not in by_s]
+        for j in by_s:
+            bank = ("p7", "drep0")[j % 2]
+            mm([(a(bank), a("idm"), a("x" + n, j, 2048, 4))] + [(a(bank, q, 512, 4), idb, d) for q in range(4)])
+            act(a("mn" + n, j, 2048, 4), a(bank), F.Relu)
         for w in parts:
-            for j in range(4):
-                last["v"] = tt(a("mn" + n, 16 * lo + j, 16 * (lo + w), 4), a("x" + n, 16 * lo + j, 16 * (lo + w), 4),
-                               a("drep%d" % h, 4 * lo, 4 * (lo + w)), A.min, last["v"])
+            for j in js:
+                tt(a("mn" + n, 16 * lo + j, 16 * (lo + w), 4), a("x" + n, 16 * lo + j, 16 * (lo + w), 4),
+                   a("drep%d" % h, 4 * lo, 4 * (lo + w)), A.min)
             lo += w
         c0 = 256 * h + half(l)[0]
         out = a("key", c0, c0 + 128)
-        mm([(out, a("on", 0, 128, 1, 1), a("cr", *half(l), 1, 1))]
-           + [(a("key", c0 + k, c0 + 128, 16), a("mn" + n, k, 2048, 16), a("b64")) for k in range(16)])
+        for i, j in enumerate(js[:1] + list(by_s) + js[1:]):
+            grp = [(out, a("on", 0, 128, 1, 1), a("cr", *half(l), 1, 1))] * (i == 0)
+            for k in range(j, 16, 4):
+                key = a("key", c0 + k, c0 + 128, 16)
+                if j in by_s:
+                    grp += [(key, d, a("b64", 0, 8)), (key, a("mn" + n, k, 2048, 16), a("b64", 8, 16))]
+                else:
+                    grp += [(key, a("mn" + n, k, 2048, 16), a("b64", 0, 8))]
+            mm(grp, opens=i == 0, closes=i == 3)
         if l == "O":
             scan(a("r%d" % h, 0, 128), a("mka"), out, A.add, A.min)
         else:
@@ -371,29 +394,29 @@ def rank_program(g, core, T, topo):
     def best_gone(t, h):
         H, win = "%d" % h, a("xt_s")
         with_k(a("so" + H), a("misc", 144 + 24 * h, 168 + 24 * h), t)
-        cp(a("yy" + H, 0, 128), ind(win, a("so" + H, 0, 8)))
+        cp(a("yy" + H, 0, 128), ind(win, a("so" + H, 0, 8)), YQ)
         for s in (1, 2):
             tt(a("yy" + H, 128 * s, 128 * s + 128), ind(win, a("so" + H, 8 * s, 8 * s + 8)), a("yy" + H, 128 * s - 128, 128 * s), A.max)
 
     def step2(t, h):
         H = "%d" % h
         B, gn, d = a("yy" + H, 256, 384), a("gn" + H), a("d" + H)
+        n, lo, hi = a("cps" + H, 256, 384), a("up" + H, 0, 128), a("up" + H, 128, 256)
+        ts(lo, d, -8.0, 1.0, A.add, A.max)
+        ts(hi, d, 8.0, 255.0, A.add, A.min)
         for j in range(4):
-            bank = (("drep0", "drep1"), ("drep1", "p7"))[h][j % 2]
+            bank = BANKS[h][j]
             x, ge = a("xC" + H, j, 2048, 4), a("ge" + H, j, 2048, 4)
             parts = [[(a(bank, q, 512, 4), idb, B), (a(bank, q, 512, 4), a("sk", 128 * (4 * q + j), 128 * (4 * q + j) + 128), gn)]
                      for q in range(4)]
-            if j in SCMP:
+            if j in SCMP[h]:
                 mm([(a(bank), a("idm"), x)] + [z for p in parts for z in p])
                 act(ge, a(bank), F.Relu, 1.0, -1.0)
             else:
                 mm(*parts)
                 tt(ge, x, a(bank), A.is_ge)
-        n, dp = a("misc", 384, 512), a("misc", 256, 384)
-        mm([(n, idb, a("ge" + H, k, 2048, 16)) for k in range(16)])
-        ts(a("up" + H), n, 0.5, 0.5, A.is_ge, A.subtract)
-        mm([(dp, idb, d), (dp, a("id16"), a("up" + H))])
-        ts(d, dp, 1.0, 255.0, A.max, A.min)
+            mm([(n, idb, lo)] * (j == 0) + [(n, a("id16"), a("ge" + H, k, 2048, 16)) for k in range(j, 16, 4)], opens=j == 0, closes=j == 3)
+        tt(d, n, hi, A.min)
         d_rep(h)
 
     for h in range(2):
@@ -411,23 +434,21 @@ def rank_program(g, core, T, topo):
                 gather("O", h, t, h == 0)
                 arrive(t, h)
                 gather("C", h, t)
-                mins("O", h, (64, 64))
-                mins("C", h, (64, 32, 32) if h else (64, 64))
+                mins("O", h, PO[h])
+                mins("C", h, PC[h])
                 swap(h)
                 if h == 0:
                     exchange(t, 0)
         else:
+            arrive(t, 1)
+            slots(t, 1)
+            for l, h in ORDER2:
+                gather(l, h, t, (l, h) == ORDER2[0])
             for h in range(2):
-                if h:
-                    arrive(t, h)
-                    slots(t, h)
-                gather("C", h, t, h == 0)
                 best_gone(t, h)
-                gather("O", h, t)
                 step2(t, h)
-            for h in range(2):
-                mins("C", h, (128,))
-                mins("O", h, (128,))
+                for l in ML[h]:
+                    mins(l, h, P2, SMIN[l] if h else ())
                 swap(h)
                 if h == 0:
                     exchange(t, 0)

@@ -1,3 +1,4 @@
+import numpy as np
 from concourse.mybir import AluOpType as A, ActivationFunctionType as F, AxisListType as AX
 
 W = 4096
@@ -8,37 +9,45 @@ XW = X0 + W + 32
 FLOOR = -2560.0
 M32, M64, M2K = 1.5 * 2 ** 28, 1.5 * 2 ** 29, 1.5 * 2 ** 34
 CR = {"key": (0, 256), "c2k": (256, 384), "c4k": (384, 512), "u": (512, 640), "u5": (640, 768), "s1": (768, 896),
-      "s33": (896, 1024), "big": (1024, 1408), "xo": (1408, 1416), "cnt": (1416, 1424), "off": (1424, 1448)}
-VG = {0: [("O", 0, 1), ("C", 0, 1)],
-      1: [("O", 0, 0)], 2: []}
-SMIN = {"O": [1], "C": [1]}
-ORDER2 = [("C", 0), ("O", 0), ("C", 1), ("O", 1)]
-YQ = "v"
-SCMP = [[], [3]]
-ZQ = "s"
+      "s33": (896, 1024), "big": (1024, 1408), "xo": (1408, 1416), "cnt": (1416, 1424), "off": (1424, 1448),
+      "m2k": (1448, 1576), "n2k": (1576, 1704), "m32": (1704, 1712), "n32": (1712, 1720), "l32": (1720, 1728)}
+VG = {0: [], 1: [], 2: []}
+NF = [{"O0": 1, "C0": 1}] * 4 + [{}] * 2
+SMIN = [{}] * 4 + [{"O0": {1: "wu"}, "O1": {1: "drep0"}, "C1": {1: "p7"}}] * 2
+ORDER2 = [("O", 0, (0,)), ("C", 0, (0, 1, 2, 3)), ("O", 0, (1, 2, 3)), ("O", 1, (0, 1)), ("C", 1, (0, 1, 2, 3)), ("O", 1, (2, 3))]
+YQ = "vv"
+SCMP = [[], []]
+ZQ = "v"
 SLACK = 0.0
-PASSES = 6
-BANKS = [["drep0", "drep1", "drep0", "drep1"], ["drep1", "p7", "drep1", "p7"]]
+PASSES, ROUNDS, ALLOW, SEED = 6, 30000, 120.0, 0
+PLAN = {}
+STEP = 17
+OLD2 = 0
+DS = 0
+KP, EP = 1, 1
+ON_S = [["", ""]] * 6
+BANKS = [["drep0", "drep1", "key", "drep1"], ["drep1", "p7", "drep0", "p7"]]
 ML = ["CO", "CO"]
-PO = [(64, 64), (64, 64)]
-PC = [(64, 64), (64, 32, 32)]
-P2 = (128,)
+PC = (64, 32, 32)
+P2 = (64, 64)
 SCRATCH = {
     "xt_s": ("sbuf", [128, XW], "bfloat16"),
     "wti": ("sbuf", [128, 1], "int32"), "wtf": ("sbuf", [128, 1], "float32"),
     "dmi": ("sbuf", [128, 256], "int32"), "poi": ("sbuf", [128, 256], "int32"), "pki": ("sbuf", [128, 256], "int32"),
     "yO": ("sbuf", [128, 256], "float32"), "yC": ("sbuf", [128, 256], "float32"), "yD": ("sbuf", [128, 256], "float32"),
-    "on": ("sbuf", [128, 384], "bfloat16"), "cr": ("sbuf", [128, 1448], "bfloat16"),
+    "on": ("sbuf", [128, 384], "bfloat16"), "cr": ("sbuf", [128, 1728], "bfloat16"),
     "blk8": ("sbuf", [128, 8], "bfloat16"), "b64": ("sbuf", [128, 16], "bfloat16"),
-    "blk": ("sbuf", [128, 128], "bfloat16"), "w2": ("sbuf", [128, 128], "bfloat16"),
+    "blk": ("sbuf", [128, 128], "bfloat16"), "w2": ("sbuf", [128, 128], "bfloat16"), "w2n": ("sbuf", [128, 128], "bfloat16"),
     "idb": ("sbuf", [128, 128], "bfloat16"), "idm": ("sbuf", [128, 128], "bfloat16"),
     "idn": ("sbuf", [128, 128], "bfloat16"), "id16": ("sbuf", [128, 128], "bfloat16"),
     "c512": ("sbuf", [128, 128], "bfloat16"), "nbk": ("sbuf", [128, 128], "bfloat16"),
     "tri": ("sbuf", [128, 640], "bfloat16"),
     "et": ("sbuf", [128, 168], "bfloat16"), "em": ("sbuf", [128, 384], "bfloat16"),
-    "xr": ("sbuf", [128, 2048], "bfloat16"), "sr": ("sbuf", [128, 2048], "bfloat16"), "sk": ("sbuf", [128, 2048], "bfloat16"),
-    "pi": ("sbuf", [128, 8], "int32"), "pf": ("sbuf", [128, 8], "float32"),
+    "rr": ("sbuf", [128, 16], "float32"), "e4": ("sbuf", [128, 512], "bfloat16"),
+    "xr": ("sbuf", [128, 512], "bfloat16"), "sr": ("sbuf", [128, 2048], "bfloat16"), "sk": ("sbuf", [128, 2048], "bfloat16"),
+    "pi": ("sbuf", [128, 24], "int32"), "pf": ("sbuf", [128, 8], "float32"),
     "mkm": ("sbuf", [128, 128], "float32"), "mka": ("sbuf", [128, 128], "float32"),
+    "ds0": ("sbuf", [128, 2048], "bfloat16"), "ds1": ("sbuf", [128, 2048], "bfloat16"),
     "kc": ("sbuf", [128, 16], "float32"),
     "key": ("psum", [128, 512], "float32"), "wu": ("psum", [128, 512], "float32"),
     "misc": ("psum", [128, 512], "float32"), "p7": ("psum", [128, 512], "float32"),
@@ -52,24 +61,27 @@ for _h in "01":
         "r" + _h: ("sbuf", [128, 256], "float32"), "tq" + _h: ("sbuf", [128, 16], "float32"),
         "z" + _h: ("sbuf", [128, 56], "bfloat16"), "zs" + _h: ("sbuf", [128, 128], "bfloat16"),
         "sel" + _h: ("sbuf", [128, 256], "float16"), "vv" + _h: ("sbuf", [128, 256], "float32"),
+        "z4" + _h: ("sbuf", [128, 32], "bfloat16"),
         "xo" + _h: ("sbuf", [128, 8], "uint16"), "u" + _h: ("sbuf", [128, 128], "bfloat16"),
         "gn" + _h: ("sbuf", [128, 128], "bfloat16"), "fqM" + _h: ("sbuf", [128, 128], "int32"),
         "fm" + _h: ("sbuf", [128, 128], "float16"), "cl" + _h: ("sbuf", [128, 384], "float16"),
-        "sf" + _h: ("sbuf", [128, 24], "float32"), "so" + _h: ("sbuf", [128, 24], "uint16"),
+        "y3" + _h: ("sbuf", [128, 384], "bfloat16"), "so" + _h: ("sbuf", [128, 24], "uint16"),
         "yy" + _h: ("sbuf", [128, 384], "bfloat16"), "up" + _h: ("sbuf", [128, 256], "bfloat16"),
         "ge" + _h: ("sbuf", [128, 2048], "bfloat16"),
     })
     for _l in "OC":
         SCRATCH.update({
             "fq" + _l + _h: ("sbuf", [128, 128], "int32"), "f" + _l + _h: ("sbuf", [128, 128], "uint16"),
-            "x" + _l + _h: ("sbuf", [128, 2064], "bfloat16"), "mn" + _l + _h: ("sbuf", [128, 2048], "bfloat16"),
+            "x" + _l + _h: ("sbuf", [128, 2064], "bfloat16"), "mn" + _l + _h: ("sbuf", [128, 2064], "bfloat16"),
         })
 LOADS = ["lwt", "ldm0", "lpo0", "lxt", "lpk0", "ldm1", "lpo1", "lpk1"]
 STORES = ["s%s%d" % (l, h) for l in "OCD" for h in range(2)]
 SEMAPHORES = (["sv", "ss", "sp", "sg", "sent"] + LOADS + STORES
               + ["ar%d%d" % (t, h) for t in range(1, NT) for h in range(2)])
 
-CYC, PCYC, GATHER, HOP, DMA, FAR = 0.83, 0.5, 1.56, 120.0, 2500.0, 3500.0
+CYC, PCYC, GATHER, HOP, DMA, FAR = 0.83, 0.45, 1.45, 200.0, 2500.0, 3300.0
+SFIX, SLATE, PMIN = 60.0, 60.0, 72
+CASES = [(1.0, 1.3, 210.0, 3300.0), (1.35, 1.9, 200.0, 3600.0)]
 
 
 def rank_program(g, core, T, topo):
@@ -86,11 +98,11 @@ def rank_program(g, core, T, topo):
 
     ops, acc = [], {}
 
-    def a(name, lo=0, hi=None, step=1, P=128):
+    def a(name, lo=0, hi=None, step=1, P=128, p0=0):
         hi = SCRATCH[name][1][1] if hi is None else hi
         cols = range(lo, hi, step)
         bits = ((1 << hi) - (1 << lo)) if step == 1 else sum(1 << c for c in cols)
-        return {"ap": T[name][0:P, lo:hi:step], "rw": [(name, bits)], "n": len(cols), "b": name}
+        return {"ap": T[name][p0:p0 + P, lo:hi:step], "rw": [(name, bits)], "n": len(cols), "b": name}
 
     def ind(win, off):
         return {"ap": win["ap"].indirect(off["ap"]), "rw": win["rw"] + off["rw"], "n": 16 * off["n"], "b": win["b"], "ind": 1}
@@ -108,7 +120,7 @@ def rank_program(g, core, T, topo):
         for n, bits in Rl:
             acc.setdefault(n, []).append((i, bits, False))
         deps.discard(i)
-        ops.append({"q": q, "calls": calls, "deps": deps, "cost": cost, "sem": sem, "tail": tail,
+        ops.append({"q": q, "gathered": sum(x["n"] for x in R if isinstance(x, dict) and "ind" in x), "calls": calls, "deps": deps, "cost": cost, "sem": sem, "tail": tail,
                     "after": set() if after is None else {after},
                     "banks": {n for n, b in Rl + Wl if n in SCRATCH and SCRATCH[n][0] == "psum"}})
         return i
@@ -144,7 +156,8 @@ def rank_program(g, core, T, topo):
         return add("v", [lambda: g.vector.tensor_tensor_scan(u(out), u(d0), u(d1), 0.0, op0, op1)], [d0, d1], [out], cost("v", out, [d1], 1))
 
     def act(out, x, f, bias=0.0, scale=1.0, after=None):
-        return add("s", [lambda: g.scalar.activation(u(out), u(x), f, bias, scale)], [x], [out], cost("s", out, [x], 1), after=after)
+        return add("s", [lambda: g.scalar.activation(u(out), u(x), f, bias, scale)], [x], [out],
+                   cost("s", out, [x], 1) + (0 if "ind" in x else SFIX), tail=SLATE, after=after)
 
     def mm(*groups, opens=True, closes=True):
         calls, R, Wr, c = [], [], [], 0
@@ -154,9 +167,13 @@ def rank_program(g, core, T, topo):
                 calls.append(lambda o=o, l=l, r=r, st=st, sp=sp: g.tensor.matmul(u(o), u(l), u(r), st, sp))
                 R += [l, r]
                 Wr.append(o)
-                c += max(min(64, l["n"]), r["n"])
+                c += max(PMIN, r["n"])
         lock = {"rw": [("open " + Wr[0]["b"], 1)]}
         return add("p", calls, R + [lock], Wr + [lock] * (not (opens and closes)), c * PCYC)
+
+    def steps(grp):
+        for i in range(0, len(grp), STEP):
+            mm(grp[i:i + STEP], opens=i == 0, closes=i + STEP >= len(grp))
 
     def row(out, name, n=None, K=1):
         lo, hi = CR[name]
@@ -190,18 +207,21 @@ def rank_program(g, core, T, topo):
     aff(blk, on, [[-16, 8], [0, 16]], A.is_ge, 0.0, 0, 1)
     aff(blk, blk, [[16, 8], [0, 16]], A.is_ge, 0.0, 15, -1)
     aff(idb, on, [[-1, 128]], A.is_equal, 0.0, 0, 1)
-    iota(a("cr", *CR["s1"], 1, 2), [[0, 128]], -1024, 1025)
+    iota(a("cr", *CR["s1"], 1, 2), [[0, 128]], 1024 if EP else -1024, -1025 if EP else 1025)
     iota(a("cr", 0, 128, 1, 1), [[0, 8], [1, 16]], 64, 0)
     iota(a("cr", 128, 256, 1, 1), [[0, 8], [-1, 16]], 63, 0)
     iota(a("cr", *CR["xo"], 1, 1), [[256, 8]], 0, 0)
     iota(a("pi", 0, 4), [[0, 4]], 0, 1)
-    for name, c in (("c2k", 2048.0), ("s33", 33.0), ("u", -30720.0), ("cnt", 16.25 / 8), ("c4k", 4096.0), ("u5", -28672.0),
+    iota(a("pi", 8, 24), [[1, 16]], 0, 0)
+    for name, c in (("c2k", 2048.0), ("s33", 33.0), ("u", -30720.0), ("cnt", 16.25 / (1 if KP else 8)), ("c4k", 4096.0), ("u5", -28672.0),
+                    ("m2k", M2K), ("n2k", -M2K), ("m32", M32), ("n32", -M32), ("l32", -32.0),
                     ("big", -8192.0), ("off", -16 * FLOOR)):
         ms(a("cr", *CR[name], 1, 32), c)
     ms(a("cr", CR["off"][0] + 8, CR["off"][0] + 16, 1, 32), -15 * FLOOR - 2048)
     ms(a("xt_s", 0, X0), -1.0)
     cp(a("wtf"), a("wti"))
     ts(a("w2"), blk, a("wtf"), 2.0, A.mult, A.mult)
+    ts(a("w2n"), blk, a("wtf"), -2.0, A.mult, A.mult)
     cp(blk8, a("blk", 0, 128, 16))
     ts(a("b64", 0, 8), blk8, 64.0, None, A.mult)
     ts(a("b64", 8, 16), blk8, -64.0, None, A.mult)
@@ -214,22 +234,26 @@ def rank_program(g, core, T, topo):
     for h in range(2):
         ms(a("z%d" % h, 40, 56), 1.0)
         ms(a("xC%d" % h, 2048, 2064), -1.0)
+        ms(a("mnC%d" % h, 2048, 2064), -1.0)
     ts(a("pi", 4, 8), a("pi", 0, 4), 15, None, A.bitwise_and)
     cp(a("pf", 0, 1), a("pi", 4, 5))
     ts(a("pf", 1, 2), a("pi", 4, 5), -1.0, -1.0, A.mult, A.add)
     tt(a("pf", 2, 4), a("pf", 0, 2), a("pf", 0, 2), A.mult)
-    ts(a("pf", 4, 5), a("pi", 4, 5), 16.0, 4095.0, A.mult, A.add)
+    ts(a("pf", 4, 5), a("pi", 4, 5), 16.0, -1.0, A.mult, A.add)
     ms(a("et"), 0.0)
     for i in range(2):
-        for c0, s1, s2 in ((8 * i, a("pf", i, i + 1), -8192.0), (16 + 8 * i, 1.0, 4096.0), (32, 1.0, -4096.0),
+        for c0, s1, s2 in ((16 + 8 * i, a("pf", i, i + 1), -8192.0), (8 * i, 1.0, 4096.0), (32, 1.0, -4096.0),
                            (40, a("pf", 2 + i, 3 + i), 4096.0), (48, 1.0, 4096.0)):
             ts(a("et", 56 * i + c0, 56 * i + c0 + 8), blk8, s1, s2, A.mult, A.mult)
-    ts(a("et", 120, 128), blk8, -1.0, None, A.mult)
-    ts(a("et", 144, 152), blk8, -4096.0, None, A.mult)
-    mm(*[[(a("p7", 128 * i, 128 * i + 128, 1, 56), a("et", 56 * i, 56 * i + 56), idb)] for i in range(3)])
-    cp(a("em", 0, 384, 1, 56), a("p7", 0, 384, 1, 56), "s")
+    mm(*[[(a("p7", 128 * i, 128 * i + 128, 1, 56), a("et", 56 * i, 56 * i + 56), idb)] for i in range(2)])
+    cp(a("em", 0, 256, 1, 56), a("p7", 0, 256, 1, 56), "s")
+    for i, c in enumerate((-1.0, -4096.0, 4096.0, a("pf", 4, 5))):
+        ts(a("et", 112 + 8 * i, 120 + 8 * i), blk8, c, None, A.mult)
+    ts(a("rr"), a("pi", 8, 24), a("pf", 0, 1), None, A.is_equal)
     for r in range(16):
-        aff(a("xr", 128 * r, 128 * r + 128, 1, 56), a("em", 256, 384, 1, 56), [[0, 8], [1, 16]], A.is_equal, 0.0, -r, 0)
+        ts(a("e4", 32 * r, 32 * r + 32), a("et", 112, 144), a("rr", r, r + 1), None, A.mult)
+    mm(*[[(a("wu", 128 * i, 128 * i + 128), a("e4", 128 * i, 128 * i + 128), idb)] for i in range(4)])
+    cp(a("xr"), a("wu"), "s")
 
     def late_constants():
         cp(a("xt_s", X0 + W, XW), a("xt_s", X0, X0 + 32), "s")
@@ -253,15 +277,33 @@ def rank_program(g, core, T, topo):
         out = a("cps%d" % h, *half(l))
         mm([row(out, c), (out, idb, cards(l, h, t))])
 
-    def e_of(h):
+    def e_of(h, on_s=False):
         H = "%d" % h
         s1, s2 = a("cps" + H, 256, 384), a("cps" + H, 384, 512)
+        if EP:
+            mm([row(s1, "s1", K=2), (s1, a("w2n"), a("d" + H)), row(s1, "m2k"), row(s1, "n2k"), (s1, a("w2"), a("d" + H)), row(s1, "s33")])
+            cp(a("e" + H), s1)
+            return
         mm([row(s1, "s1", K=2), (s1, a("w2"), a("d" + H))], [row(s2, "s33"), (s2, a("w2"), a("d" + H))])
-        ts(a("eq" + H), s1, M2K, M2K, A.add, A.subtract)
+        if on_s:
+            act(a("eq" + H), s1, F.Identity, M2K)
+            act(a("eq" + H), a("eq" + H), F.Identity, -M2K)
+        else:
+            ts(a("eq" + H), s1, M2K, M2K, A.add, A.subtract)
         tt(a("e" + H), s2, a("eq" + H), A.subtract)
 
-    def d_rep(h):
+    def fused(l, h, t):
+        return NF[t].get("%s%d" % (l, h), 0)
+
+    def d_rep(h, t):
         mm(*[[(a("drep%d" % h, j, 512, 4), idb, a("d%d" % h))] for j in range(4)])
+        for c in range(max(fused("O", h, t), fused("C", h, t))):
+            if DS:
+                steps([(a("p7", k, 512, 16), idb, a("d%d" % h, 32 * c, 32 * c + 32)) for k in range(16)])
+                cp(a("ds%d" % h, 512 * c, 512 * c + 512), a("p7"), "s")
+            else:
+                for j in range(4):
+                    cp(a("ds%d" % h, 512 * c + j, 512 * c + 512, 4), a("drep%d" % h, 128 * c, 128 * c + 128), "s")
 
     def f_pre(src, fq, h):
         tt(fq, src, a("e%d" % h), A.mult)
@@ -275,22 +317,25 @@ def rank_program(g, core, T, topo):
 
     last = {"s": None, "v": None}
 
-    def gather(l, h, t, first=False):
+    def gather(l, h, t, first=False, chunks=range(4)):
         n = "%s%d" % (l, h)
-        for lo, hi in ((0, 32), (32, 128)) if first else ((0, 128),):
+        for lo, hi in (((0, 32), (32, 128))[2 * (KP and t > 0):] if first else ((0, 128),)) * (0 in chunks):
             with_k(a("f" + n, lo, hi), a("fq" + n, lo, hi), t)
         win = a("xt_s", WIN, XW if t else X0 + W)
-        for c in range(4):
+        for c in chunks:
+            if c < fused(l, h, t):
+                tt(a("mn" + n, 512 * c, 512 * c + 512), ind(win, a("f" + n, 32 * c, 32 * c + 32)), a("ds%d" % h, 512 * c, 512 * c + 512), A.min)
+                continue
             q = "v" if (l, h, c) in VG[min(t, 1) if t < 4 else 2] else "s"
             i = cp(a("x" + n, 512 * c, 512 * c + 512), ind(win, a("f" + n, 32 * c, 32 * c + 32)), q, last["s"] if q == "s" else None)
             if q == "s":
                 last["s"] = i
 
-    def mins(l, h, parts, by_s=()):
-        n, lo, d = "%s%d" % (l, h), 0, a("d%d" % h)
+    def mins(l, h, t, parts):
+        n, lo, d, by_s = "%s%d" % (l, h), 32 * fused(l, h, t), a("d%d" % h), SMIN[t].get("%s%d" % (l, h), {})
         js = [j for j in range(4) if j not in by_s]
-        for j in by_s:
-            bank = ("p7", "drep0")[j % 2]
+        parts = parts or ((), (32,), (64,), (32, 64), (64, 64))[4 - lo // 32]
+        for j, bank in by_s.items():
             mm([(a(bank), a("idm"), a("x" + n, j, 2048, 4))] + [(a(bank, q, 512, 4), idb, d) for q in range(4)])
             act(a("mn" + n, j, 2048, 4), a(bank), F.Relu)
         for w in parts:
@@ -319,6 +364,14 @@ def rank_program(g, core, T, topo):
 
     def count(t):
         out, c = a("misc", 136, 144), 2 * t + 2
+        if KP:
+            for h in range(2):
+                mm([row(a("wu", 0, 4), "cnt", 4)] * (h == 0)
+                   + [(a("wu", p, p + 2), on, a("z%d" % h, 32 + i, 40, 4)) for p in (2, 1, 0) for i in range(4)]
+                   + [row(a("wu", 2, 3), z, 1) for z in ("m32", "n32", "l32")] * h, opens=h == 0, closes=h == 1)
+            ts(a("fO0"), a("fqO0"), a("wu", 1, 2), a("wu", 2, 3), A.add, A.subtract)
+            cp(a("kc", c, c + 2), a("wu", 1, 3))
+            return
         mm([row(out, "cnt")] + [(out, on, a("z%d" % h, 32, 40)) for h in range(2)])
         add("v", [lambda: g.vector.tensor_reduce(u(a("kc", c, c + 1)), u(out), AX.X, A.add)], [out], [a("kc", c, c + 1)], 64 * CYC)
         ts(a("kc", c + 1, c + 2), a("kc", c, c + 1), M32, M32 + 32, A.add, A.subtract)
@@ -327,20 +380,25 @@ def rank_program(g, core, T, topo):
         H, end = "%d" % h, t == NT - 1
         z, zs, best = "z" + H, a("zs" + H, 0, 128, 1, 56), a("r" + H, 15, 256, 16)
         ts(a("tq" + H), best, M64, M64, A.add, A.subtract)
-        tt(a(z, 0, 16), best, a("tq" + H), A.subtract)
-        tt(a(z, 16, 32), a(z, 0, 16), a(z, 0, 16), A.mult)
+        tt(a(z, 16, 32), best, a("tq" + H), A.subtract)
+        tt(a(z, 0, 16), a(z, 16, 32), a(z, 16, 32), A.mult)
         mm([(a("misc", 0, 128, 1, 56), a(z), idb)])
         cp(zs, a("misc", 0, 128, 1, 56), ZQ)
         em = {l: a("em", *half(l), 1, 56) for l in "OC"}
         if end:
             for l in "OC":
-                c_ps(l, h, t, "c4k")
+                if l not in ON_S[t][h]:
+                    c_ps(l, h, t, "c4k")
         mm(*[[(a("wu", *half(l)), idb, cards(l, h, t)), (a("wu", *half(l)), em[l], zs)] for l in "OC"])
         ts(a("sel" + H), a("wu", 0, 256), 2048.0, None, A.min)
         for l, m in ("CO", "OC"):
             out = a("wu", 256 + half(l)[0], 256 + half(l)[1])
             mm([row(out, "u5" if end else "u"), (out, em[l], zs), (out, blk, a("sel" + H, *half(m)))])
-            tt(a("vv" + H, *half(l)), a("cps" + H, *half(l)), a("sel" + H, *half(l)), A.subtract)
+            if l in ON_S[t][h]:
+                mm([(a("wu", *half(l)), idb, cards(l, h, t)), (a("wu", *half(l)), a("idm"), a("sel" + H, *half(l)))])
+                act(a("vv" + H, *half(l)), a("wu", *half(l)), F.Identity, 4096.0 if end else 2048.0)
+            else:
+                tt(a("vv" + H, *half(l)), a("cps" + H, *half(l)), a("sel" + H, *half(l)), A.subtract)
             new = a("y" + l, 128 * h, 128 * h + 128) if end else cards(l, h, t)
             tt(new, out, a("vv" + H, *half(l)), A.min)
             if end:
@@ -350,19 +408,25 @@ def rank_program(g, core, T, topo):
             else:
                 c_ps("O", h, t)
         xo, dp, d = a("misc", 128, 136), a("misc", 256, 384), a("d" + H)
-        mm([row(xo, "xo")] + [(xo, a("xr", 128 * r, 128 * r + 128, 1, 56), a("zs" + H, r, 128, 16, 56)) for r in range(16)])
-        ts(a("xo" + H), xo, a("pf", 4, 5), 2048.0, A.add, A.min)
-        tt(a("u" + H), ind(a("xC" + H), a("xo" + H)), d, A.is_ge)
+        mm(*[[(a("misc", 192, 224, 1, 32, 32 * q), a(z, 24, 56), a("idb", q, 128, 4))] for q in range(4)])
+        cp(a("z4" + H), a("misc", 192, 224))
+        mm([row(xo, "xo")] + [(xo, a("xr", 128 * i, 128 * i + 128), a("z4" + H, i, 32, 4)) for i in range(4)])
+        ts(a("xo" + H), xo, 2048.0, None, A.min)
+        tt(a("u" + H), ind(a(("mnC" if fused("C", h, t) else "xC") + H), a("xo" + H)), d, A.is_ge)
         mm([(dp, idb, d), (dp, a("idn"), a("u" + H))])
         if end:
             new = a("yD", 128 * h, 128 * h + 128)
             ts(new, dp, 1.0, None, A.max)
             store("s" if h else "y", "sD%d" % h, T.yd[:, 128 * h:128 * h + 128], new)
             return
-        ts(d, dp, 1.0, None, A.max)
-        e_of(h)
+        if "d" in ON_S[t][h]:
+            act(d, dp, F.Relu, -1.0)
+            act(d, d, F.Identity, 1.0)
+        else:
+            ts(d, dp, 1.0, None, A.max)
+        e_of(h, "e" in ON_S[t][h])
         if t + 1 < 4:
-            d_rep(h)
+            d_rep(h, t + 1)
         f_pre(a("cps" + H, 0, 128), a("fqO" + H), h)
 
     def send(t, h):
@@ -377,47 +441,66 @@ def rank_program(g, core, T, topo):
 
     def slots(t, h):
         H = "%d" % h
-        m, gn, mp, df = cards("C", h, t - 4), a("gn" + H), a("p7", 0, 128), a("p7", 128, 256)
-        mm([row(mp, "c2k"), (mp, idb, m)], [(df, idb, m), (df, a("idm"), cards("C", h, t))])
-        ts(gn, df, 0.0, None, A.not_equal)
+        m, gn, mp, mc = cards("C", h, t - 4), a("gn" + H), a("p7", 0, 128), a("misc", 384, 512)
+        mm([row(mp, "c2k"), (mp, idb, m)])
+        mm([(mc, idb, m)])
+        tt(gn, cards("C", h, t), mc, A.not_equal)
         f_pre(mp, a("fqM" + H), h)
         ts(a("fm" + H), a("fqM" + H), -2048.0, None, A.add)
-        grp = [row(a("p7", 128, 512), "big")]
-        for s in range(3):
-            out = a("p7", 128 + 128 * s, 256 + 128 * s)
-            grp += [(out, idb, a("fm" + H)), (out, a("tri", 128 * s, 128 * s + 128), gn)]
-        mm(grp)
+        out = [a("p7", 128 + 128 * s, 256 + 128 * s) for s in range(3)]
+        mm([row(a("p7", 128, 512), "big")] + [(out[s], idb, a("fm" + H)) for s in range(3)], closes=False)
+        mm([(out[s], a("tri", 128 * s, 128 * s + 128), gn) for s in range(3)], opens=False)
         ts(a("cl" + H), a("p7", 128, 512), FLOOR, 2048.0, A.max, A.min)
         out = a("misc", 144 + 24 * h, 168 + 24 * h)
-        mm([row(out, "off")] + [(out, a("sr", 128 * r, 128 * r + 128), a("cl" + H, r, 384, 16)) for r in range(16)])
+        steps([row(out, "off")] + [(out, a("sr", 128 * r, 128 * r + 128), a("cl" + H, r, 384, 16)) for r in range(16)])
 
     def best_gone(t, h):
         H, win = "%d" % h, a("xt_s")
         with_k(a("so" + H), a("misc", 144 + 24 * h, 168 + 24 * h), t)
-        cp(a("yy" + H, 0, 128), ind(win, a("so" + H, 0, 8)), YQ)
+        if YQ[h] == "s":
+            cp(a("y3" + H), ind(win, a("so" + H)), "s")
+            tt(a("misc", 384, 512), a("y3" + H, 0, 128), a("y3" + H, 128, 256), A.max)
+            tt(a("yy" + H, 256, 384), a("misc", 384, 512), a("y3" + H, 256, 384), A.max)
+            return
+        cp(a("yy" + H, 0, 128), ind(win, a("so" + H, 0, 8)))
         for s in (1, 2):
             tt(a("yy" + H, 128 * s, 128 * s + 128), ind(win, a("so" + H, 8 * s, 8 * s + 8)), a("yy" + H, 128 * s - 128, 128 * s), A.max)
 
     def step2(t, h):
         H = "%d" % h
-        B, gn, d = a("yy" + H, 256, 384), a("gn" + H), a("d" + H)
-        n, lo, hi = a("cps" + H, 256, 384), a("up" + H, 0, 128), a("up" + H, 128, 256)
-        ts(lo, d, -8.0, 1.0, A.add, A.max)
-        ts(hi, d, 8.0, 255.0, A.add, A.min)
-        for j in range(4):
-            bank = BANKS[h][j]
-            x, ge = a("xC" + H, j, 2048, 4), a("ge" + H, j, 2048, 4)
-            parts = [[(a(bank, q, 512, 4), idb, B), (a(bank, q, 512, 4), a("sk", 128 * (4 * q + j), 128 * (4 * q + j) + 128), gn)]
-                     for q in range(4)]
-            if j in SCMP[h]:
-                mm([(a(bank), a("idm"), x)] + [z for p in parts for z in p])
-                act(ge, a(bank), F.Relu, 1.0, -1.0)
-            else:
-                mm(*parts)
-                tt(ge, x, a(bank), A.is_ge)
-            mm([(n, idb, lo)] * (j == 0) + [(n, a("id16"), a("ge" + H, k, 2048, 16)) for k in range(j, 16, 4)], opens=j == 0, closes=j == 3)
-        tt(d, n, hi, A.min)
-        d_rep(h)
+        ts(a("up" + H, 0, 128), a("d" + H), -8.0, 1.0, A.add, A.max)
+        ts(a("up" + H, 128, 256), a("d" + H), 8.0, 255.0, A.add, A.min)
+        if OLD2:
+            B, gn, n, d = a("yy" + H, 256, 384), a("gn" + H), a("cps" + H, 256, 384), a("d" + H)
+            for j in range(4):
+                bank = [["drep0", "drep1", "key", "drep1"], ["drep1", "p7", "drep1", "p7"]][h][j]
+                x, ge = a("xC" + H, j, 2048, 4), a("ge" + H, j, 2048, 4)
+                mm([(a(bank, q, 512, 4), a("sk", 128 * (4 * q + j), 128 * (4 * q + j) + 128), gn) for q in range(4)], closes=False)
+                mm([(a(bank, q, 512, 4), idb, B) for q in range(4)] + [(a(bank), a("idm"), x)] * (j in SCMP[h]), opens=False)
+                if j in SCMP[h]:
+                    act(ge, a(bank), F.Relu, 1.0, -1.0)
+                else:
+                    tt(ge, x, a(bank), A.is_ge)
+                mm([(n, idb, a("up" + H, 0, 128))] * (j == 0) + [(n, a("id16"), a("ge" + H, k, 2048, 16)) for k in range(j, 16, 4)], opens=j == 0, closes=j == 3)
+            tt(d, n, a("up" + H, 128, 256), A.min)
+            d_rep(h, t)
+            return
+        for w in range(2):
+            l0, l1 = 64 * w, 64 * w + 64
+            B, gn, n = a("yy" + H, 256 + l0, 256 + l1), a("gn" + H, l0, l1), a("cps" + H, 256 + l0, 256 + l1)
+            for p in range(2):
+                bank, on_s = BANKS[h][2 * w + p], 2 * w + p in SCMP[h]
+                x, ge = a("xC" + H, 16 * l0 + p, 16 * l1, 2), a("ge" + H, 16 * l0 + p, 16 * l1, 2)
+                mm([(a(bank, q, 512, 8), a("sk", 128 * (2 * q + p), 128 * (2 * q + p) + 128), gn) for q in range(8)], closes=False)
+                mm([(a(bank, q, 512, 8), idb, B) for q in range(8)] + [(a(bank), a("idm"), x)] * on_s, opens=False)
+                if on_s:
+                    act(ge, a(bank), F.Relu, 1.0, -1.0)
+                else:
+                    tt(ge, x, a(bank), A.is_ge)
+                mm([(n, idb, a("up" + H, l0, l1))] * (p == 0)
+                   + [(n, a("id16"), a("ge" + H, 16 * l0 + k, 16 * l1, 16)) for k in range(p, 16, 2)], opens=p == 0, closes=p == 1)
+            tt(a("d" + H, l0, l1), n, a("up" + H, 128 + l0, 128 + l1), A.min)
+            mm(*[[(a("drep" + H, 4 * l0 + j, 4 * l1, 4), idb, a("d" + H, l0, l1))] for j in range(4)])
 
     for h in range(2):
         H = "%d" % h
@@ -425,7 +508,7 @@ def rank_program(g, core, T, topo):
         ts(a("o" + H), a("poi", 128 * h, 128 * h + 128), -2048.0, None, A.add)
         ts(cards("C", h, 0), a("pki", 128 * h, 128 * h + 128), -2048.0, None, A.add)
         e_of(h)
-        d_rep(h)
+        d_rep(h, 0)
         c_ps("O", h, 0)
         f_pre(a("cps" + H, 0, 128), a("fqO" + H), h)
     for t in range(NT):
@@ -434,21 +517,21 @@ def rank_program(g, core, T, topo):
                 gather("O", h, t, h == 0)
                 arrive(t, h)
                 gather("C", h, t)
-                mins("O", h, PO[h])
-                mins("C", h, PC[h])
+                mins("O", h, t, None)
+                mins("C", h, t, PC if h and not fused("C", h, t) else None)
                 swap(h)
                 if h == 0:
                     exchange(t, 0)
         else:
             arrive(t, 1)
             slots(t, 1)
-            for l, h in ORDER2:
-                gather(l, h, t, (l, h) == ORDER2[0])
+            for i, (l, h, chunks) in enumerate(ORDER2):
+                gather(l, h, t, i == 0, chunks)
             for h in range(2):
                 best_gone(t, h)
                 step2(t, h)
                 for l in ML[h]:
-                    mins(l, h, P2, SMIN[l] if h else ())
+                    mins(l, h, t, P2)
                 swap(h)
                 if h == 0:
                     exchange(t, 0)
@@ -473,7 +556,7 @@ def rank_program(g, core, T, topo):
     def place(before, behind, weight, release):
         left = [len(b) for b in before]
         ready = {i: release[i] for i in range(n) if left[i] == 0}
-        free, ends, bank, order, extra = {q: 0.0 for q in "vspgyx"}, [0.0] * n, {}, [], {}
+        free, ends, bank, order = {q: 0.0 for q in "vspgyx"}, [0.0] * n, {}, []
         while ready:
             st = {}
             for i, t0 in ready.items():
@@ -482,10 +565,8 @@ def rank_program(g, core, T, topo):
             i0 = min(st, key=st.get)
             i = max((k for k in st if ops[k]["q"] == ops[i0]["q"] and st[k] <= st[i0] + SLACK), key=lambda k: weight[k])
             o = ops[i]
-            extra[i] = set()
             for b in o["banks"]:
-                extra[i] |= {j for q, j in bank.setdefault(b, {}).items() if q != o["q"]}
-                bank[b][o["q"]] = i
+                bank.setdefault(b, {})[o["q"]] = i
             ends[i] = st[i] + o["cost"]
             if o["q"] != "x":
                 free[o["q"]] = ends[i]
@@ -495,22 +576,101 @@ def rank_program(g, core, T, topo):
                 left[k] -= 1
                 if left[k] == 0:
                     ready[k] = max([release[k]] + [ends[j] + lag for j, lag in before[k].items()])
-        return order, ends, extra
+        return order, ends
 
     tails, zero = [o["tail"] for o in ops], [0.0] * n
     weight = [0.0] * n
     for i in range(n - 1, -1, -1):
         weight[i] = ops[i]["cost"] + max([tails[i]] + [weight[k] + lag for k, lag in succ[i].items()])
-    best = None
-    for _ in range(PASSES):
-        order, ends, extra = place(pred, succ, weight, zero)
-        total = max(e + t for e, t in zip(ends, tails))
-        if best is None or total < best[0]:
-            best = (total, order, ends, extra)
-        weight = place(succ, pred, ends, tails)[1]
-    total, order, done, extra = best
+    qs, cs, bs = [o["q"] for o in ops], [o["cost"] for o in ops], [tuple(sorted(o["banks"])) for o in ops]
+    ahead = pred
+    pred = [{j: lag for j, lag in p.items() if j in o["deps"] or o["q"] != "s"} for p, o in zip(pred, ops)]
+    before = [sorted(p.items()) for p in pred]
+
+    name = {}
+    holds = [[name.setdefault(z, len(name)) for z in [q] * (q != "x") + [b + q for b in bk]] for q, bk in zip(qs, bs)]
+    follows = [[(name.setdefault(z, len(name)), lag) for z, lag in [(q, 0.0)] * (q != "x") + [(b + r, HOP + SLATE * (r == "s")) for b in bk for r in "vsp" if r != q]]
+               for q, bk in zip(qs, bs)]
+    lasts = [i for i in range(n) if tails[i]]
+
+    cases = []
+    for f, gt, hop, far in CASES:
+        cases.append(([f * (c + o["gathered"] * (gt - GATHER) * CYC) for c, o in zip(cs, ops)],
+                      [[(j, lag and lag + hop - HOP + (far - FAR) * (qs[j] == "x")) for j, lag in b] for b in before],
+                      [[(z, lag and lag + hop - HOP) for z, lag in b] for b in follows], f))
+
+    def both(order, old=None, lo=0):
+        runs = [timed(order, old and old[2][s], lo, *cases[s][:3]) for s in range(len(cases))]
+        return sum(r[0] / c[3] for r, c in zip(runs, cases)) / len(cases), order, runs
+
+    def timed(order, old=None, lo=0, cs=cs, before=before, follows=follows):
+        ends, why = (old[2][:], old[3][:]) if old else ([0.0] * n + [-1e4], [None] * n)
+        holder = [n] * len(name)
+        for i in order[:lo]:
+            for z in holds[i]:
+                holder[z] = i
+        for i in order[lo:]:
+            t0, w = 0.0, None
+            for j, lag in before[i]:
+                if ends[j] + lag > t0:
+                    t0, w = ends[j] + lag, (j, 0)
+            for z, lag in follows[i]:
+                j = holder[z]
+                if ends[j] + lag > t0:
+                    t0, w = ends[j] + lag, (j, 1)
+            for z in holds[i]:
+                holder[z] = i
+            ends[i], why[i] = t0 + cs[i], w
+        i = max(lasts, key=lambda k: ends[k] + tails[k])
+        total, pairs = ends[i] + tails[i], []
+        while why[i]:
+            pairs += [(why[i][0], i)] * why[i][1]
+            i = why[i][0]
+        return total, order, ends, why, pairs
+
+    def relieve(now, rounds):
+        rng, best = np.random.default_rng(SEED), now
+        for r in range(rounds):
+            total, order, pairs = now[0], now[1], now[2][r % len(cases)][4]
+            p, i = pairs[int(rng.integers(len(pairs)))]
+            lo, hi = order.index(p), order.index(i) + 1
+            lo = max(0, lo - int(rng.integers(12)) * (rng.random() < 0.3))
+            seg, first, rest = order[lo:hi], {i}, {p}
+            for k in seg[::-1]:
+                if k in first:
+                    first.update(pred[k])
+            for k in seg:
+                if not rest.isdisjoint(pred[k]):
+                    rest.add(k)
+            if p in first:
+                continue
+            if rng.random() < 0.5:
+                seg = [k for k in seg if k in first] + [k for k in seg if k not in first]
+            else:
+                seg = [k for k in seg if k not in rest] + [k for k in seg if k in rest]
+            new = both(order[:lo] + seg + order[hi:], now, lo)
+            if new[0] - total <= ALLOW * (1 - r / rounds) * rng.exponential():
+                now = new
+                if r % 64 == 0:
+                    now = both(sorted(new[1], key=lambda k: new[2][0][2][k] - cases[0][0][k]))
+                if now[0] < best[0]:
+                    best = now
+        return best
+
+    if "order" not in PLAN:
+        best = None
+        for _ in range(PASSES):
+            order, ends = place(ahead, succ, weight, zero)
+            if best is None or timed(order)[0] < best[0]:
+                best = timed(order)
+            weight = place(succ, ahead, ends, tails)[1]
+        PLAN["order"] = relieve(both(best[1]), ROUNDS)[1]
+    total, order, done = timed(PLAN["order"])[:3]
+    bank = {}
     for i in order:
-        ops[i]["deps"] = ops[i]["deps"] | extra[i]
+        for b in bs[i]:
+            ops[i]["deps"] = ops[i]["deps"] | {j for q, j in bank.setdefault(b, {}).items() if q != qs[i]}
+            bank[b][qs[i]] = i
 
     pos, known, clock, waits, seen = {}, {q: {} for q in "vspgyx"}, {}, {}, {q: 0 for q in "vspgyx"}
     for i in order:

@@ -1,5 +1,5 @@
 import numpy as np
-from concourse.mybir import AluOpType as A, ActivationFunctionType as F, AxisListType as AX
+from concourse.mybir import AluOpType as A, ActivationFunctionType as F
 
 W = 4096
 NT = 6
@@ -10,32 +10,22 @@ FLOOR = -2560.0
 M32, M64, M2K = 1.5 * 2 ** 28, 1.5 * 2 ** 29, 1.5 * 2 ** 34
 CR = {"key": (0, 256), "c2k": (256, 384), "c4k": (384, 512), "u": (512, 640), "u5": (640, 768), "s1": (768, 896),
       "s33": (896, 1024), "big": (1024, 1408), "xo": (1408, 1416), "cnt": (1416, 1424), "off": (1424, 1448),
-      "m2k": (1448, 1576), "n2k": (1576, 1704), "m32": (1704, 1712), "n32": (1712, 1720), "l32": (1720, 1728)}
-VG = {0: [], 1: [], 2: []}
-NF = [{"O0": 1, "C0": 1}] * 4 + [{}] * 2
-SMIN = [{}] * 4 + [{"O0": {1: "wu"}, "O1": {1: "drep0"}, "C1": {1: "p7"}}] * 2
+      "m2k": (1448, 1576), "n2k": (1576, 1704), "m32": (1704, 1712), "n32": (1712, 1720)}
+NF = [{"O0": 2, "C0": 2}] + [{"O0": 1, "C0": 1}] * 3 + [{}] * 2
+SMIN = [{"O1": {1: "p7"}}] * 4 + [{"O0": {1: "wu"}, "O1": {1: "wu"}, "C1": {1: "p7"}}] * 2
 ORDER2 = [("O", 0, (0,)), ("C", 0, (0, 1, 2, 3)), ("O", 0, (1, 2, 3)), ("O", 1, (0, 1)), ("C", 1, (0, 1, 2, 3)), ("O", 1, (2, 3))]
-YQ = "vv"
-SCMP = [[], []]
-ZQ = "v"
-SLACK = 0.0
-PASSES, ROUNDS, ALLOW, SEED = 6, 30000, 120.0, 0
+PASSES, ROUNDS, ALLOW, SEED = 6, 75000, 70.0, 3
 PLAN = {}
-STEP = 17
-OLD2 = 0
-DS = 0
-KP, EP = 1, 1
-ON_S = [["", ""]] * 6
-BANKS = [["drep0", "drep1", "key", "drep1"], ["drep1", "p7", "drep0", "p7"]]
-ML = ["CO", "CO"]
-PC = (64, 32, 32)
+BANKS = [["drep0", "wu", "key", "wu"], ["drep1", "p7", "wu", "p7"]]
+PC = (64, 48, 16)
+PARTS = ((), (32,), (64,), (32, 64), (64, 64))
 P2 = (64, 64)
 SCRATCH = {
     "xt_s": ("sbuf", [128, XW], "bfloat16"),
     "wti": ("sbuf", [128, 1], "int32"), "wtf": ("sbuf", [128, 1], "float32"),
     "dmi": ("sbuf", [128, 256], "int32"), "poi": ("sbuf", [128, 256], "int32"), "pki": ("sbuf", [128, 256], "int32"),
     "yO": ("sbuf", [128, 256], "float32"), "yC": ("sbuf", [128, 256], "float32"), "yD": ("sbuf", [128, 256], "float32"),
-    "on": ("sbuf", [128, 384], "bfloat16"), "cr": ("sbuf", [128, 1728], "bfloat16"),
+    "on": ("sbuf", [128, 384], "bfloat16"), "cr": ("sbuf", [128, 1856], "bfloat16"),
     "blk8": ("sbuf", [128, 8], "bfloat16"), "b64": ("sbuf", [128, 16], "bfloat16"),
     "blk": ("sbuf", [128, 128], "bfloat16"), "w2": ("sbuf", [128, 128], "bfloat16"), "w2n": ("sbuf", [128, 128], "bfloat16"),
     "idb": ("sbuf", [128, 128], "bfloat16"), "idm": ("sbuf", [128, 128], "bfloat16"),
@@ -43,7 +33,7 @@ SCRATCH = {
     "c512": ("sbuf", [128, 128], "bfloat16"), "nbk": ("sbuf", [128, 128], "bfloat16"),
     "tri": ("sbuf", [128, 640], "bfloat16"),
     "et": ("sbuf", [128, 168], "bfloat16"), "em": ("sbuf", [128, 384], "bfloat16"),
-    "rr": ("sbuf", [128, 16], "float32"), "e4": ("sbuf", [128, 512], "bfloat16"),
+    "e4": ("sbuf", [128, 512], "bfloat16"),
     "xr": ("sbuf", [128, 512], "bfloat16"), "sr": ("sbuf", [128, 2048], "bfloat16"), "sk": ("sbuf", [128, 2048], "bfloat16"),
     "pi": ("sbuf", [128, 24], "int32"), "pf": ("sbuf", [128, 8], "float32"),
     "mkm": ("sbuf", [128, 128], "float32"), "mka": ("sbuf", [128, 128], "float32"),
@@ -57,7 +47,6 @@ for _h in "01":
         "drep" + _h: ("psum", [128, 512], "float32"), "cps" + _h: ("psum", [128, 512], "float32"),
         "o" + _h: ("sbuf", [128, 128], "float16"), "ld" + _h: ("sbuf", [128, 128 * NT], "float16"),
         "d" + _h: ("sbuf", [128, 128], "bfloat16"), "e" + _h: ("sbuf", [128, 128], "float32"),
-        "eq" + _h: ("sbuf", [128, 128], "float32"),
         "r" + _h: ("sbuf", [128, 256], "float32"), "tq" + _h: ("sbuf", [128, 16], "float32"),
         "z" + _h: ("sbuf", [128, 56], "bfloat16"), "zs" + _h: ("sbuf", [128, 128], "bfloat16"),
         "sel" + _h: ("sbuf", [128, 256], "float16"), "vv" + _h: ("sbuf", [128, 256], "float32"),
@@ -65,7 +54,7 @@ for _h in "01":
         "xo" + _h: ("sbuf", [128, 8], "uint16"), "u" + _h: ("sbuf", [128, 128], "bfloat16"),
         "gn" + _h: ("sbuf", [128, 128], "bfloat16"), "fqM" + _h: ("sbuf", [128, 128], "int32"),
         "fm" + _h: ("sbuf", [128, 128], "float16"), "cl" + _h: ("sbuf", [128, 384], "float16"),
-        "y3" + _h: ("sbuf", [128, 384], "bfloat16"), "so" + _h: ("sbuf", [128, 24], "uint16"),
+        "so" + _h: ("sbuf", [128, 24], "uint16"),
         "yy" + _h: ("sbuf", [128, 384], "bfloat16"), "up" + _h: ("sbuf", [128, 256], "bfloat16"),
         "ge" + _h: ("sbuf", [128, 2048], "bfloat16"),
     })
@@ -74,14 +63,14 @@ for _h in "01":
             "fq" + _l + _h: ("sbuf", [128, 128], "int32"), "f" + _l + _h: ("sbuf", [128, 128], "uint16"),
             "x" + _l + _h: ("sbuf", [128, 2064], "bfloat16"), "mn" + _l + _h: ("sbuf", [128, 2064], "bfloat16"),
         })
-LOADS = ["lwt", "ldm0", "lpo0", "lxt", "lpk0", "ldm1", "lpo1", "lpk1"]
+LOADS = ["lwt", "ldm", "lpo", "lpk", "lxt"]
 STORES = ["s%s%d" % (l, h) for l in "OCD" for h in range(2)]
 SEMAPHORES = (["sv", "ss", "sp", "sg", "sent"] + LOADS + STORES
               + ["ar%d%d" % (t, h) for t in range(1, NT) for h in range(2)])
 
-CYC, PCYC, GATHER, HOP, DMA, FAR = 0.83, 0.45, 1.45, 200.0, 2500.0, 3300.0
+CYC, PCYC, GATHER, HOP, DMA, FAR = 0.83, 0.45, 1.45, 200.0, 1800.0, 3300.0
 SFIX, SLATE, PMIN = 60.0, 60.0, 72
-CASES = [(1.0, 1.3, 210.0, 3300.0), (1.35, 1.9, 200.0, 3600.0)]
+CASES = [(1.0, 1.3, 210.0, 2700.0), (1.35, 1.9, 200.0, 3400.0)]
 
 
 def rank_program(g, core, T, topo):
@@ -171,10 +160,6 @@ def rank_program(g, core, T, topo):
         lock = {"rw": [("open " + Wr[0]["b"], 1)]}
         return add("p", calls, R + [lock], Wr + [lock] * (not (opens and closes)), c * PCYC)
 
-    def steps(grp):
-        for i in range(0, len(grp), STEP):
-            mm(grp[i:i + STEP], opens=i == 0, closes=i + STEP >= len(grp))
-
     def row(out, name, n=None, K=1):
         lo, hi = CR[name]
         return (out, a("on", 0, 128, 1, K), a("cr", lo, hi if n is None else lo + n, 1, K))
@@ -182,6 +167,9 @@ def rank_program(g, core, T, topo):
     def iota(out, pattern, base, cm):
         kw = {} if SCRATCH[out["b"]][2] == "int32" else {"allow_small_or_imprecise_dtypes": True}
         return add("g", [lambda: g.iota(u(out), pattern, base, cm, **kw)], [], [out], 130 + 2 * out["n"] * CYC)
+
+    def fill(out, c):
+        return iota(out, [[0, out["n"]]], int(c), 0)
 
     def aff(out, x, pattern, op, fill, base, cm):
         return add("g", [lambda: g.affine_select(u(out), u(x), pattern, op, fill, base, cm)], [x], [out], 170 + 2 * out["n"] * CYC)
@@ -194,30 +182,27 @@ def rank_program(g, core, T, topo):
         return add(q, [lambda: Q[q].dma_start(dst, u(x))], [x], [], 60, sem=(sem, 16), tail=DMA)
 
     load("lwt", a("wti"), T.wt[:], DMA)
-    load("ldm0", a("dmi", 0, 128), T.dm[:, 0:128], DMA)
-    load("lpo0", a("poi", 0, 128), T.po[:, 0:128], DMA + 300)
-    load("lxt", a("xt_s", X0, X0 + W), T.xt[:], DMA + 5500)
-    load("lpk0", a("pki", 0, 128), T.pk[:, 0:128], DMA + 5800)
-    load("ldm1", a("dmi", 128, 256), T.dm[:, 128:256], DMA + 6100)
-    load("lpo1", a("poi", 128, 256), T.po[:, 128:256], DMA + 6400)
-    load("lpk1", a("pki", 128, 256), T.pk[:, 128:256], DMA + 6700)
+    load("ldm", a("dmi"), T.dm[:], DMA + 300)
+    load("lpo", a("poi"), T.po[:], DMA + 600)
+    load("lpk", a("pki"), T.pk[:], DMA + 900)
+    load("lxt", a("xt_s", X0, X0 + W), T.xt[:], DMA + 3500)
 
     on, idb, blk, blk8 = a("on", 0, 128), a("idb"), a("blk"), a("blk8")
     ms(a("on"), 1.0)
     aff(blk, on, [[-16, 8], [0, 16]], A.is_ge, 0.0, 0, 1)
     aff(blk, blk, [[16, 8], [0, 16]], A.is_ge, 0.0, 15, -1)
     aff(idb, on, [[-1, 128]], A.is_equal, 0.0, 0, 1)
-    iota(a("cr", *CR["s1"], 1, 2), [[0, 128]], 1024 if EP else -1024, -1025 if EP else 1025)
+    iota(a("cr", *CR["s1"], 1, 2), [[0, 128]], 1024, -1025)
     iota(a("cr", 0, 128, 1, 1), [[0, 8], [1, 16]], 64, 0)
     iota(a("cr", 128, 256, 1, 1), [[0, 8], [-1, 16]], 63, 0)
     iota(a("cr", *CR["xo"], 1, 1), [[256, 8]], 0, 0)
     iota(a("pi", 0, 4), [[0, 4]], 0, 1)
-    iota(a("pi", 8, 24), [[1, 16]], 0, 0)
-    for name, c in (("c2k", 2048.0), ("s33", 33.0), ("u", -30720.0), ("cnt", 16.25 / (1 if KP else 8)), ("c4k", 4096.0), ("u5", -28672.0),
-                    ("m2k", M2K), ("n2k", -M2K), ("m32", M32), ("n32", -M32), ("l32", -32.0),
+    for name, c in (("c2k", 2048.0), ("s33", 33.0), ("u", -30720.0), ("cnt", 16.25), ("c4k", 4096.0), ("u5", -28672.0),
+                    ("m2k", M2K), ("n2k", -M2K), ("m32", M32), ("n32", -M32),
                     ("big", -8192.0), ("off", -16 * FLOOR)):
-        ms(a("cr", *CR[name], 1, 32), c)
-    ms(a("cr", CR["off"][0] + 8, CR["off"][0] + 16, 1, 32), -15 * FLOOR - 2048)
+        (fill if name in ("u", "u5", "c4k", "big", "off") else ms)(a("cr", *CR[name], 1, 32), c)
+    ms(a("cr", CR["cnt"][0] + 2, CR["cnt"][0] + 3, 1, 32), -15.75)
+    fill(a("cr", CR["off"][0] + 8, CR["off"][0] + 16, 1, 32), -15 * FLOOR - 2048)
     ms(a("xt_s", 0, X0), -1.0)
     cp(a("wtf"), a("wti"))
     ts(a("w2"), blk, a("wtf"), 2.0, A.mult, A.mult)
@@ -226,15 +211,15 @@ def rank_program(g, core, T, topo):
     ts(a("b64", 0, 8), blk8, 64.0, None, A.mult)
     ts(a("b64", 8, 16), blk8, -64.0, None, A.mult)
     for name, c in (("idm", -1.0), ("idn", -4.0), ("id16", 16.0)):
-        ts(a(name), idb, c, None, A.mult)
-    ms(a("mkm"), 1.0)
-    ms(a("mkm", 0, 128, 16), 0.0)
-    ms(a("mka"), 0.0)
-    ms(a("mka", 0, 128, 16), 8388608.0)
+        act(a(name), idb, F.Copy, 0.0, c)
+    fill(a("mkm"), 1)
+    fill(a("mkm", 0, 128, 16), 0)
+    fill(a("mka"), 0)
+    fill(a("mka", 0, 128, 16), 2 ** 23)
     for h in range(2):
-        ms(a("z%d" % h, 40, 56), 1.0)
-        ms(a("xC%d" % h, 2048, 2064), -1.0)
-        ms(a("mnC%d" % h, 2048, 2064), -1.0)
+        fill(a("z%d" % h, 40, 56), 1)
+        fill(a("xC%d" % h, 2048, 2064), -1)
+    fill(a("mnC0", 2048, 2064), -1)
     ts(a("pi", 4, 8), a("pi", 0, 4), 15, None, A.bitwise_and)
     cp(a("pf", 0, 1), a("pi", 4, 5))
     ts(a("pf", 1, 2), a("pi", 4, 5), -1.0, -1.0, A.mult, A.add)
@@ -249,23 +234,22 @@ def rank_program(g, core, T, topo):
     cp(a("em", 0, 256, 1, 56), a("p7", 0, 256, 1, 56), "s")
     for i, c in enumerate((-1.0, -4096.0, 4096.0, a("pf", 4, 5))):
         ts(a("et", 112 + 8 * i, 120 + 8 * i), blk8, c, None, A.mult)
-    ts(a("rr"), a("pi", 8, 24), a("pf", 0, 1), None, A.is_equal)
     for r in range(16):
-        ts(a("e4", 32 * r, 32 * r + 32), a("et", 112, 144), a("rr", r, r + 1), None, A.mult)
+        aff(a("e4", 32 * r, 32 * r + 32), a("et", 112, 144), [[0, 4], [-16, 8]], A.is_equal, 0.0, -r, 1)
     mm(*[[(a("wu", 128 * i, 128 * i + 128), a("e4", 128 * i, 128 * i + 128), idb)] for i in range(4)])
     cp(a("xr"), a("wu"), "s")
 
     def late_constants():
         cp(a("xt_s", X0 + W, XW), a("xt_s", X0, X0 + 32), "s")
-        ms(a("c512"), 512.0)
-        ts(a("nbk"), blk, -8192.0, None, A.mult)
+        fill(a("c512"), 512)
+        act(a("nbk"), blk, F.Copy, 0.0, -8192.0)
         for r in range(16):
             aff(a("sr", 128 * r, 128 * r + 128), blk, [[0, 8], [1, 16]], A.is_equal, 0.0, -r, 0)
             aff(a("sk", 128 * r, 128 * r + 128), a("c512"), [[-16, 8], [0, 16]], A.is_equal, 0.0, -r, 1)
         aff(a("tri", 384, 512), a("nbk"), [[1, 128]], A.is_gt, 0.0, 0, -1)
         aff(a("tri", 512, 640), a("nbk"), [[-1, 128]], A.is_gt, 0.0, 0, 1)
-        for s, (c0, fill) in enumerate(((384, 8192.0), (384, 16384.0), (512, 8192.0))):
-            aff(a("tri", 128 * s, 128 * s + 128), a("tri", c0, c0 + 128), [[1, 128]], A.not_equal, fill, 0, -1)
+        for s, (c0, own) in enumerate(((384, 8192.0), (384, 16384.0), (512, 8192.0))):
+            aff(a("tri", 128 * s, 128 * s + 128), a("tri", c0, c0 + 128), [[1, 128]], A.not_equal, own, 0, -1)
 
     def cards(l, h, t):
         return a("o%d" % h) if l == "O" else a("ld%d" % h, 128 * t, 128 * t + 128)
@@ -277,20 +261,11 @@ def rank_program(g, core, T, topo):
         out = a("cps%d" % h, *half(l))
         mm([row(out, c), (out, idb, cards(l, h, t))])
 
-    def e_of(h, on_s=False):
+    def e_of(h):
         H = "%d" % h
-        s1, s2 = a("cps" + H, 256, 384), a("cps" + H, 384, 512)
-        if EP:
-            mm([row(s1, "s1", K=2), (s1, a("w2n"), a("d" + H)), row(s1, "m2k"), row(s1, "n2k"), (s1, a("w2"), a("d" + H)), row(s1, "s33")])
-            cp(a("e" + H), s1)
-            return
-        mm([row(s1, "s1", K=2), (s1, a("w2"), a("d" + H))], [row(s2, "s33"), (s2, a("w2"), a("d" + H))])
-        if on_s:
-            act(a("eq" + H), s1, F.Identity, M2K)
-            act(a("eq" + H), a("eq" + H), F.Identity, -M2K)
-        else:
-            ts(a("eq" + H), s1, M2K, M2K, A.add, A.subtract)
-        tt(a("e" + H), s2, a("eq" + H), A.subtract)
+        s1 = a("cps" + H, 256, 384)
+        mm([row(s1, "s1", K=2), (s1, a("w2n"), a("d" + H)), row(s1, "m2k"), row(s1, "n2k"), (s1, a("w2"), a("d" + H)), row(s1, "s33")])
+        cp(a("e" + H), s1)
 
     def fused(l, h, t):
         return NF[t].get("%s%d" % (l, h), 0)
@@ -298,12 +273,8 @@ def rank_program(g, core, T, topo):
     def d_rep(h, t):
         mm(*[[(a("drep%d" % h, j, 512, 4), idb, a("d%d" % h))] for j in range(4)])
         for c in range(max(fused("O", h, t), fused("C", h, t))):
-            if DS:
-                steps([(a("p7", k, 512, 16), idb, a("d%d" % h, 32 * c, 32 * c + 32)) for k in range(16)])
-                cp(a("ds%d" % h, 512 * c, 512 * c + 512), a("p7"), "s")
-            else:
-                for j in range(4):
-                    cp(a("ds%d" % h, 512 * c + j, 512 * c + 512, 4), a("drep%d" % h, 128 * c, 128 * c + 128), "s")
+            for j in range(4):
+                cp(a("ds%d" % h, 512 * c + j, 512 * c + 512, 4), a("drep%d" % h, 128 * c, 128 * c + 128), "s")
 
     def f_pre(src, fq, h):
         tt(fq, src, a("e%d" % h), A.mult)
@@ -319,22 +290,25 @@ def rank_program(g, core, T, topo):
 
     def gather(l, h, t, first=False, chunks=range(4)):
         n = "%s%d" % (l, h)
-        for lo, hi in (((0, 32), (32, 128))[2 * (KP and t > 0):] if first else ((0, 128),)) * (0 in chunks):
+        for lo, hi in (((0, 32), (32, 128))[2 * (t > 0):] if first else ((0, 128),)) * (0 in chunks):
             with_k(a("f" + n, lo, hi), a("fq" + n, lo, hi), t)
         win = a("xt_s", WIN, XW if t else X0 + W)
         for c in chunks:
             if c < fused(l, h, t):
                 tt(a("mn" + n, 512 * c, 512 * c + 512), ind(win, a("f" + n, 32 * c, 32 * c + 32)), a("ds%d" % h, 512 * c, 512 * c + 512), A.min)
                 continue
-            q = "v" if (l, h, c) in VG[min(t, 1) if t < 4 else 2] else "s"
-            i = cp(a("x" + n, 512 * c, 512 * c + 512), ind(win, a("f" + n, 32 * c, 32 * c + 32)), q, last["s"] if q == "s" else None)
-            if q == "s":
-                last["s"] = i
+            cuts = (0, 16, 32) if (n, c) == ("C1", 3) and t < 4 else (0, 32)
+            pair = c // 2 * 2 >= fused(l, h, t) and c ^ 1 in chunks and not (n == "C1" and c > 1 and t < 4) and not first
+            if pair:
+                cuts = () if c % 2 else (0, 64)
+            for lo, hi in zip(cuts, cuts[1:]):
+                lo, hi = 32 * c + lo, 32 * c + hi
+                last["s"] = cp(a("x" + n, 16 * lo, 16 * hi), ind(win, a("f" + n, lo, hi)), "s", last["s"])
 
     def mins(l, h, t, parts):
         n, lo, d, by_s = "%s%d" % (l, h), 32 * fused(l, h, t), a("d%d" % h), SMIN[t].get("%s%d" % (l, h), {})
         js = [j for j in range(4) if j not in by_s]
-        parts = parts or ((), (32,), (64,), (32, 64), (64, 64))[4 - lo // 32]
+        parts = parts or PARTS[4 - lo // 32]
         for j, bank in by_s.items():
             mm([(a(bank), a("idm"), a("x" + n, j, 2048, 4))] + [(a(bank, q, 512, 4), idb, d) for q in range(4)])
             act(a("mn" + n, j, 2048, 4), a(bank), F.Relu)
@@ -363,18 +337,13 @@ def rank_program(g, core, T, topo):
         tt(a("z%d" % h, 32, 40), a("r%d" % h, 143, 256, 16), a("r%d" % h, 15, 128, 16), A.is_gt)
 
     def count(t):
-        out, c = a("misc", 136, 144), 2 * t + 2
-        if KP:
-            for h in range(2):
-                mm([row(a("wu", 0, 4), "cnt", 4)] * (h == 0)
-                   + [(a("wu", p, p + 2), on, a("z%d" % h, 32 + i, 40, 4)) for p in (2, 1, 0) for i in range(4)]
-                   + [row(a("wu", 2, 3), z, 1) for z in ("m32", "n32", "l32")] * h, opens=h == 0, closes=h == 1)
-            ts(a("fO0"), a("fqO0"), a("wu", 1, 2), a("wu", 2, 3), A.add, A.subtract)
-            cp(a("kc", c, c + 2), a("wu", 1, 3))
-            return
-        mm([row(out, "cnt")] + [(out, on, a("z%d" % h, 32, 40)) for h in range(2)])
-        add("v", [lambda: g.vector.tensor_reduce(u(a("kc", c, c + 1)), u(out), AX.X, A.add)], [out], [a("kc", c, c + 1)], 64 * CYC)
-        ts(a("kc", c + 1, c + 2), a("kc", c, c + 1), M32, M32 + 32, A.add, A.subtract)
+        for h in range(2):
+            mm([row(a("wu", 0, 4), "cnt", 4)] * (h == 0)
+               + [(a("wu", p, p + 2), on, a("z%d" % h, 32 + i, 40, 4)) for p in (2, 1, 0) for i in range(4)]
+               + [row(a("wu", 2, 3), z, 1) for z in ("m32", "n32")] * h, opens=h == 0, closes=h == 1)
+        for lo in (0, 64):
+            ts(a("fO0", lo, lo + 64), a("fqO0", lo, lo + 64), a("wu", 1, 2), a("wu", 2, 3), A.add, A.subtract)
+        cp(a("kc", 2 * t + 2, 2 * t + 4), a("wu", 1, 3))
 
     def exchange(t, h):
         H, end = "%d" % h, t == NT - 1
@@ -382,23 +351,20 @@ def rank_program(g, core, T, topo):
         ts(a("tq" + H), best, M64, M64, A.add, A.subtract)
         tt(a(z, 16, 32), best, a("tq" + H), A.subtract)
         tt(a(z, 0, 16), a(z, 16, 32), a(z, 16, 32), A.mult)
-        mm([(a("misc", 0, 128, 1, 56), a(z), idb)])
-        cp(zs, a("misc", 0, 128, 1, 56), ZQ)
+        mb = "p7" if end and h else "misc"
+        mm([(a(mb, 0, 128, 1, 56), a(z), idb)])
+        cp(zs, a(mb, 0, 128, 1, 56))
         em = {l: a("em", *half(l), 1, 56) for l in "OC"}
         if end:
             for l in "OC":
-                if l not in ON_S[t][h]:
-                    c_ps(l, h, t, "c4k")
-        mm(*[[(a("wu", *half(l)), idb, cards(l, h, t)), (a("wu", *half(l)), em[l], zs)] for l in "OC"])
-        ts(a("sel" + H), a("wu", 0, 256), 2048.0, None, A.min)
+                c_ps(l, h, t, "c4k")
+        wb = "drep" + H
+        mm([(a(wb, *half(l)), idb, cards(l, h, t)) for l in "OC"] + [(a(wb, *half(l)), em[l], zs) for l in "OC"])
+        ts(a("sel" + H), a(wb, 0, 256), 2048.0, None, A.min)
         for l, m in ("CO", "OC"):
-            out = a("wu", 256 + half(l)[0], 256 + half(l)[1])
+            out = a(wb, 256 + half(l)[0], 256 + half(l)[1])
             mm([row(out, "u5" if end else "u"), (out, em[l], zs), (out, blk, a("sel" + H, *half(m)))])
-            if l in ON_S[t][h]:
-                mm([(a("wu", *half(l)), idb, cards(l, h, t)), (a("wu", *half(l)), a("idm"), a("sel" + H, *half(l)))])
-                act(a("vv" + H, *half(l)), a("wu", *half(l)), F.Identity, 4096.0 if end else 2048.0)
-            else:
-                tt(a("vv" + H, *half(l)), a("cps" + H, *half(l)), a("sel" + H, *half(l)), A.subtract)
+            tt(a("vv" + H, *half(l)), a("cps" + H, *half(l)), a("sel" + H, *half(l)), A.subtract)
             new = a("y" + l, 128 * h, 128 * h + 128) if end else cards(l, h, t)
             tt(new, out, a("vv" + H, *half(l)), A.min)
             if end:
@@ -407,9 +373,9 @@ def rank_program(g, core, T, topo):
                 send(t, h)
             else:
                 c_ps("O", h, t)
-        xo, dp, d = a("misc", 128, 136), a("misc", 256, 384), a("d" + H)
-        mm(*[[(a("misc", 192, 224, 1, 32, 32 * q), a(z, 24, 56), a("idb", q, 128, 4))] for q in range(4)])
-        cp(a("z4" + H), a("misc", 192, 224))
+        xo, dp, d = a(mb, 128, 136), a(mb, 256, 384), a("d" + H)
+        mm(*[[(a(mb, 192, 224, 1, 32, 32 * q), a(z, 24, 56), a("idb", q, 128, 4))] for q in range(4)])
+        cp(a("z4" + H), a(mb, 192, 224))
         mm([row(xo, "xo")] + [(xo, a("xr", 128 * i, 128 * i + 128), a("z4" + H, i, 32, 4)) for i in range(4)])
         ts(a("xo" + H), xo, 2048.0, None, A.min)
         tt(a("u" + H), ind(a(("mnC" if fused("C", h, t) else "xC") + H), a("xo" + H)), d, A.is_ge)
@@ -419,12 +385,8 @@ def rank_program(g, core, T, topo):
             ts(new, dp, 1.0, None, A.max)
             store("s" if h else "y", "sD%d" % h, T.yd[:, 128 * h:128 * h + 128], new)
             return
-        if "d" in ON_S[t][h]:
-            act(d, dp, F.Relu, -1.0)
-            act(d, d, F.Identity, 1.0)
-        else:
-            ts(d, dp, 1.0, None, A.max)
-        e_of(h, "e" in ON_S[t][h])
+        ts(d, dp, 1.0, None, A.max)
+        e_of(h)
         if t + 1 < 4:
             d_rep(h, t + 1)
         f_pre(a("cps" + H, 0, 128), a("fqO" + H), h)
@@ -452,16 +414,11 @@ def rank_program(g, core, T, topo):
         mm([(out[s], a("tri", 128 * s, 128 * s + 128), gn) for s in range(3)], opens=False)
         ts(a("cl" + H), a("p7", 128, 512), FLOOR, 2048.0, A.max, A.min)
         out = a("misc", 144 + 24 * h, 168 + 24 * h)
-        steps([row(out, "off")] + [(out, a("sr", 128 * r, 128 * r + 128), a("cl" + H, r, 384, 16)) for r in range(16)])
+        mm([row(out, "off")] + [(out, a("sr", 128 * r, 128 * r + 128), a("cl" + H, r, 384, 16)) for r in range(16)])
 
     def best_gone(t, h):
         H, win = "%d" % h, a("xt_s")
         with_k(a("so" + H), a("misc", 144 + 24 * h, 168 + 24 * h), t)
-        if YQ[h] == "s":
-            cp(a("y3" + H), ind(win, a("so" + H)), "s")
-            tt(a("misc", 384, 512), a("y3" + H, 0, 128), a("y3" + H, 128, 256), A.max)
-            tt(a("yy" + H, 256, 384), a("misc", 384, 512), a("y3" + H, 256, 384), A.max)
-            return
         cp(a("yy" + H, 0, 128), ind(win, a("so" + H, 0, 8)))
         for s in (1, 2):
             tt(a("yy" + H, 128 * s, 128 * s + 128), ind(win, a("so" + H, 8 * s, 8 * s + 8)), a("yy" + H, 128 * s - 128, 128 * s), A.max)
@@ -470,33 +427,15 @@ def rank_program(g, core, T, topo):
         H = "%d" % h
         ts(a("up" + H, 0, 128), a("d" + H), -8.0, 1.0, A.add, A.max)
         ts(a("up" + H, 128, 256), a("d" + H), 8.0, 255.0, A.add, A.min)
-        if OLD2:
-            B, gn, n, d = a("yy" + H, 256, 384), a("gn" + H), a("cps" + H, 256, 384), a("d" + H)
-            for j in range(4):
-                bank = [["drep0", "drep1", "key", "drep1"], ["drep1", "p7", "drep1", "p7"]][h][j]
-                x, ge = a("xC" + H, j, 2048, 4), a("ge" + H, j, 2048, 4)
-                mm([(a(bank, q, 512, 4), a("sk", 128 * (4 * q + j), 128 * (4 * q + j) + 128), gn) for q in range(4)], closes=False)
-                mm([(a(bank, q, 512, 4), idb, B) for q in range(4)] + [(a(bank), a("idm"), x)] * (j in SCMP[h]), opens=False)
-                if j in SCMP[h]:
-                    act(ge, a(bank), F.Relu, 1.0, -1.0)
-                else:
-                    tt(ge, x, a(bank), A.is_ge)
-                mm([(n, idb, a("up" + H, 0, 128))] * (j == 0) + [(n, a("id16"), a("ge" + H, k, 2048, 16)) for k in range(j, 16, 4)], opens=j == 0, closes=j == 3)
-            tt(d, n, a("up" + H, 128, 256), A.min)
-            d_rep(h, t)
-            return
         for w in range(2):
             l0, l1 = 64 * w, 64 * w + 64
             B, gn, n = a("yy" + H, 256 + l0, 256 + l1), a("gn" + H, l0, l1), a("cps" + H, 256 + l0, 256 + l1)
             for p in range(2):
-                bank, on_s = BANKS[h][2 * w + p], 2 * w + p in SCMP[h]
+                bank = BANKS[h][2 * w + p]
                 x, ge = a("xC" + H, 16 * l0 + p, 16 * l1, 2), a("ge" + H, 16 * l0 + p, 16 * l1, 2)
                 mm([(a(bank, q, 512, 8), a("sk", 128 * (2 * q + p), 128 * (2 * q + p) + 128), gn) for q in range(8)], closes=False)
-                mm([(a(bank, q, 512, 8), idb, B) for q in range(8)] + [(a(bank), a("idm"), x)] * on_s, opens=False)
-                if on_s:
-                    act(ge, a(bank), F.Relu, 1.0, -1.0)
-                else:
-                    tt(ge, x, a(bank), A.is_ge)
+                mm([(a(bank, q, 512, 8), idb, B) for q in range(8)], opens=False)
+                tt(ge, x, a(bank), A.is_ge)
                 mm([(n, idb, a("up" + H, l0, l1))] * (p == 0)
                    + [(n, a("id16"), a("ge" + H, 16 * l0 + k, 16 * l1, 16)) for k in range(p, 16, 2)], opens=p == 0, closes=p == 1)
             tt(a("d" + H, l0, l1), n, a("up" + H, 128 + l0, 128 + l1), A.min)
@@ -530,7 +469,7 @@ def rank_program(g, core, T, topo):
             for h in range(2):
                 best_gone(t, h)
                 step2(t, h)
-                for l in ML[h]:
+                for l in "CO":
                     mins(l, h, t, P2)
                 swap(h)
                 if h == 0:
@@ -563,7 +502,7 @@ def rank_program(g, core, T, topo):
                 o = ops[i]
                 st[i] = max([t0, free[o["q"]]] + [ends[j] + HOP for b in o["banks"] for q, j in bank.get(b, {}).items() if q != o["q"]])
             i0 = min(st, key=st.get)
-            i = max((k for k in st if ops[k]["q"] == ops[i0]["q"] and st[k] <= st[i0] + SLACK), key=lambda k: weight[k])
+            i = max((k for k in st if ops[k]["q"] == ops[i0]["q"] and st[k] <= st[i0]), key=lambda k: weight[k])
             o = ops[i]
             for b in o["banks"]:
                 bank.setdefault(b, {})[o["q"]] = i
@@ -599,13 +538,17 @@ def rank_program(g, core, T, topo):
                       [[(j, lag and lag + hop - HOP + (far - FAR) * (qs[j] == "x")) for j, lag in b] for b in before],
                       [[(z, lag and lag + hop - HOP) for z, lag in b] for b in follows], f))
 
-    def both(order, old=None, lo=0):
-        runs = [timed(order, old and old[2][s], lo, *cases[s][:3]) for s in range(len(cases))]
+    def both(order, old=None, lo=0, limit=0.0, moved=()):
+        runs = []
+        for s, c in enumerate(cases):
+            runs.append(timed(order, old and old[2][s], lo, *c[:3], limit * c[3], moved))
+            if runs[-1] is None:
+                return None
         return sum(r[0] / c[3] for r, c in zip(runs, cases)) / len(cases), order, runs
 
-    def timed(order, old=None, lo=0, cs=cs, before=before, follows=follows):
+    def timed(order, old=None, lo=0, cs=cs, before=before, follows=follows, limit=0.0, moved=()):
         ends, why = (old[2][:], old[3][:]) if old else ([0.0] * n + [-1e4], [None] * n)
-        holder = [n] * len(name)
+        holder, chain = [n] * len(name), old[5] if old else ()
         for i in order[:lo]:
             for z in holds[i]:
                 holder[z] = i
@@ -620,13 +563,17 @@ def rank_program(g, core, T, topo):
                     t0, w = ends[j] + lag, (j, 1)
             for z in holds[i]:
                 holder[z] = i
-            ends[i], why[i] = t0 + cs[i], w
+            t0 += cs[i]
+            if i in chain and t0 > ends[i] + limit and i not in moved:
+                return None
+            ends[i], why[i] = t0, w
         i = max(lasts, key=lambda k: ends[k] + tails[k])
-        total, pairs = ends[i] + tails[i], []
+        total, pairs, chain = ends[i] + tails[i], [], set()
         while why[i]:
+            chain.add(i)
             pairs += [(why[i][0], i)] * why[i][1]
             i = why[i][0]
-        return total, order, ends, why, pairs
+        return total, order, ends, why, pairs, chain
 
     def relieve(now, rounds):
         rng, best = np.random.default_rng(SEED), now
@@ -648,8 +595,9 @@ def rank_program(g, core, T, topo):
                 seg = [k for k in seg if k in first] + [k for k in seg if k not in first]
             else:
                 seg = [k for k in seg if k not in rest] + [k for k in seg if k in rest]
-            new = both(order[:lo] + seg + order[hi:], now, lo)
-            if new[0] - total <= ALLOW * (1 - r / rounds) * rng.exponential():
+            allow = ALLOW * (1 - r / rounds) * rng.exponential()
+            new = both(order[:lo] + seg + order[hi:], now, lo, 2 * allow + 100, set(seg))
+            if new and new[0] - total <= allow:
                 now = new
                 if r % 64 == 0:
                     now = both(sorted(new[1], key=lambda k: new[2][0][2][k] - cases[0][0][k]))
@@ -676,7 +624,7 @@ def rank_program(g, core, T, topo):
     for i in order:
         o = ops[i]
         q = o["q"]
-        seen[q] += 1
+        seen[q] += not o["sem"]
         pos[i] = (o["sem"][0], 1) if o["sem"] else (q, seen[q])
         waits[i] = []
         for j in sorted(o["deps"], key=lambda j: -done[j]):

import numpy as np
from concourse.mybir import AluOpType as A, ActivationFunctionType as F

W = 4096
NT = 6
X0 = 528
WIN = X0 - 16
XW = X0 + W + 32
FLOOR = -2560.0
M32, M64, M2K = 1.5 * 2 ** 28, 1.5 * 2 ** 29, 1.5 * 2 ** 34
CR = {"key": (0, 256), "c2k": (256, 384), "c4k": (384, 512), "u": (512, 640), "u5": (640, 768), "s1": (768, 896),
      "s33": (896, 1024), "big": (1024, 1408), "xo": (1408, 1416), "cnt": (1416, 1424), "off": (1424, 1448),
      "m2k": (1448, 1576), "n2k": (1576, 1704), "m32": (1704, 1712), "n32": (1712, 1720)}
NF = [{"O0": 2, "C0": 2}] + [{"O0": 1, "C0": 1}] * 3 + [{}] * 2
SMIN = [{"O1": {1: "p7"}}] * 4 + [{"O0": {1: "wu"}, "O1": {1: "wu"}, "C1": {1: "p7"}}] * 2
ORDER2 = [("O", 0, (0,)), ("C", 0, (0, 1, 2, 3)), ("O", 0, (1, 2, 3)), ("O", 1, (0, 1)), ("C", 1, (0, 1, 2, 3)), ("O", 1, (2, 3))]
PASSES, ROUNDS, ALLOW, SEED = 6, 75000, 70.0, 3
PLAN = {}
BANKS = [["drep0", "wu", "key", "wu"], ["drep1", "p7", "wu", "p7"]]
PC = (64, 48, 16)
PARTS = ((), (32,), (64,), (32, 64), (64, 64))
P2 = (64, 64)
SCRATCH = {
    "xt_s": ("sbuf", [128, XW], "bfloat16"),
    "wti": ("sbuf", [128, 1], "int32"), "wtf": ("sbuf", [128, 1], "float32"),
    "dmi": ("sbuf", [128, 256], "int32"), "poi": ("sbuf", [128, 256], "int32"), "pki": ("sbuf", [128, 256], "int32"),
    "yO": ("sbuf", [128, 256], "float32"), "yC": ("sbuf", [128, 256], "float32"), "yD": ("sbuf", [128, 256], "float32"),
    "on": ("sbuf", [128, 384], "bfloat16"), "cr": ("sbuf", [128, 1856], "bfloat16"),
    "blk8": ("sbuf", [128, 8], "bfloat16"), "b64": ("sbuf", [128, 16], "bfloat16"),
    "blk": ("sbuf", [128, 128], "bfloat16"), "w2": ("sbuf", [128, 128], "bfloat16"), "w2n": ("sbuf", [128, 128], "bfloat16"),
    "idb": ("sbuf", [128, 128], "bfloat16"), "idm": ("sbuf", [128, 128], "bfloat16"),
    "idn": ("sbuf", [128, 128], "bfloat16"), "id16": ("sbuf", [128, 128], "bfloat16"),
    "c512": ("sbuf", [128, 128], "bfloat16"), "nbk": ("sbuf", [128, 128], "bfloat16"),
    "tri": ("sbuf", [128, 640], "bfloat16"),
    "et": ("sbuf", [128, 168], "bfloat16"), "em": ("sbuf", [128, 384], "bfloat16"),
    "e4": ("sbuf", [128, 512], "bfloat16"),
    "xr": ("sbuf", [128, 512], "bfloat16"), "sr": ("sbuf", [128, 2048], "bfloat16"), "sk": ("sbuf", [128, 2048], "bfloat16"),
    "pi": ("sbuf", [128, 24], "int32"), "pf": ("sbuf", [128, 8], "float32"),
    "mkm": ("sbuf", [128, 128], "float32"), "mka": ("sbuf", [128, 128], "float32"),
    "ds0": ("sbuf", [128, 2048], "bfloat16"), "ds1": ("sbuf", [128, 2048], "bfloat16"),
    "kc": ("sbuf", [128, 16], "float32"),
    "key": ("psum", [128, 512], "float32"), "wu": ("psum", [128, 512], "float32"),
    "misc": ("psum", [128, 512], "float32"), "p7": ("psum", [128, 512], "float32"),
}
for _h in "01":
    SCRATCH.update({
        "drep" + _h: ("psum", [128, 512], "float32"), "cps" + _h: ("psum", [128, 512], "float32"),
        "o" + _h: ("sbuf", [128, 128], "float16"), "ld" + _h: ("sbuf", [128, 128 * NT], "float16"),
        "d" + _h: ("sbuf", [128, 128], "bfloat16"), "e" + _h: ("sbuf", [128, 128], "float32"),
        "r" + _h: ("sbuf", [128, 256], "float32"), "tq" + _h: ("sbuf", [128, 16], "float32"),
        "z" + _h: ("sbuf", [128, 56], "bfloat16"), "zs" + _h: ("sbuf", [128, 128], "bfloat16"),
        "sel" + _h: ("sbuf", [128, 256], "float16"), "vv" + _h: ("sbuf", [128, 256], "float32"),
        "z4" + _h: ("sbuf", [128, 32], "bfloat16"),
        "xo" + _h: ("sbuf", [128, 8], "uint16"), "u" + _h: ("sbuf", [128, 128], "bfloat16"),
        "gn" + _h: ("sbuf", [128, 128], "bfloat16"), "fqM" + _h: ("sbuf", [128, 128], "int32"),
        "fm" + _h: ("sbuf", [128, 128], "float16"), "cl" + _h: ("sbuf", [128, 384], "float16"),
        "so" + _h: ("sbuf", [128, 24], "uint16"),
        "yy" + _h: ("sbuf", [128, 384], "bfloat16"), "up" + _h: ("sbuf", [128, 256], "bfloat16"),
        "ge" + _h: ("sbuf", [128, 2048], "bfloat16"),
    })
    for _l in "OC":
        SCRATCH.update({
            "fq" + _l + _h: ("sbuf", [128, 128], "int32"), "f" + _l + _h: ("sbuf", [128, 128], "uint16"),
            "x" + _l + _h: ("sbuf", [128, 2064], "bfloat16"), "mn" + _l + _h: ("sbuf", [128, 2064], "bfloat16"),
        })
LOADS = ["lwt", "ldm", "lpo", "lpk", "lxt"]
STORES = ["s%s%d" % (l, h) for l in "OCD" for h in range(2)]
SEMAPHORES = (["sv", "ss", "sp", "sg", "sent"] + LOADS + STORES
              + ["ar%d%d" % (t, h) for t in range(1, NT) for h in range(2)])

CYC, PCYC, GATHER, HOP, DMA, FAR = 0.83, 0.45, 1.45, 200.0, 1800.0, 3300.0
SFIX, SLATE, PMIN = 60.0, 60.0, 72
CASES = [(1.0, 1.3, 210.0, 2700.0), (1.35, 1.9, 200.0, 3400.0)]


def rank_program(g, core, T, topo):
    rank = T.rank_of(core)
    if rank is None:
        return
    nxt = T.cores[(rank + 1) % len(T.cores)]
    prv = T.cores[(rank - 1) % len(T.cores)]
    rid, pid = topo.addr(nxt)[0], topo.addr(nxt)[1]
    mask = topo.mask(core, nxt)
    nout, nin = len(topo.engines(core, nxt)), len(topo.engines(prv, core))
    Q = {"v": g.vector, "s": g.scalar, "p": g.tensor, "g": g, "y": g.sync}
    S = {"v": T.sem.sv, "s": T.sem.ss, "p": T.sem.sp, "g": T.sem.sg}

    ops, acc = [], {}

    def a(name, lo=0, hi=None, step=1, P=128, p0=0):
        hi = SCRATCH[name][1][1] if hi is None else hi
        cols = range(lo, hi, step)
        bits = ((1 << hi) - (1 << lo)) if step == 1 else sum(1 << c for c in cols)
        return {"ap": T[name][p0:p0 + P, lo:hi:step], "rw": [(name, bits)], "n": len(cols), "b": name}

    def ind(win, off):
        return {"ap": win["ap"].indirect(off["ap"]), "rw": win["rw"] + off["rw"], "n": 16 * off["n"], "b": win["b"], "ind": 1}

    def add(q, calls, R, Wr, cost, sem=None, tail=0.0, after=None):
        i, deps = len(ops), set()
        Rl = [z for x in R if isinstance(x, dict) for z in x["rw"]]
        Wl = [z for x in Wr for z in x["rw"]]
        for n, bits in Rl:
            deps.update(j for j, b, w in acc.get(n, []) if w and b & bits)
        for n, bits in Wl:
            deps.update(j for j, b, w in acc.get(n, []) if b & bits)
        for n, bits in Wl:
            acc[n] = [(j, b & ~bits, w) for j, b, w in acc.get(n, []) if b & ~bits] + [(i, bits, True)]
        for n, bits in Rl:
            acc.setdefault(n, []).append((i, bits, False))
        deps.discard(i)
        ops.append({"q": q, "gathered": sum(x["n"] for x in R if isinstance(x, dict) and "ind" in x), "calls": calls, "deps": deps, "cost": cost, "sem": sem, "tail": tail,
                    "after": set() if after is None else {after},
                    "banks": {n for n, b in Rl + Wl if n in SCRATCH and SCRATCH[n][0] == "psum"}})
        return i

    def u(x):
        return x["ap"] if isinstance(x, dict) else x

    def two(*xs):
        return all(SCRATCH[x["b"]][2] in ("bfloat16", "float16", "uint16") for x in xs)

    def cost(q, out, ins, per):
        if any("ind" in x for x in ins):
            return (50 if q == "v" else 65) + out["n"] * GATHER * CYC
        return max(64, max(x["n"] for x in [out] + ins) * per) * CYC

    def tt(out, x, y, op, after=None):
        per = 1 if "psum" in (SCRATCH[x["b"]][0], SCRATCH[y["b"]][0]) else 2
        return add("v", [lambda: g.vector.tensor_tensor(u(out), u(x), u(y), op)], [x, y], [out], cost("v", out, [x], per), after=after)

    def ts(out, x, s1, s2, *op):
        return add("v", [lambda: g.vector.tensor_scalar(u(out), u(x), u(s1), u(s2), *op)], [x, s1, s2], [out],
                   cost("v", out, [x], 0.5 if two(out, x) else 1))

    def cp(out, x, q="v", after=None):
        if q == "s":
            return act(out, x, F.Copy, after=after)
        return add("v", [lambda: g.vector.tensor_copy(u(out), u(x))], [x], [out], cost("v", out, [x], 0.5 if two(out, x) else 1), after=after)

    def ms(out, c):
        return add("v", [lambda: g.vector.memset(u(out), c)], [], [out], cost("v", out, [], 0.5 if two(out) else 1))

    def scan(out, d0, d1, op0, op1):
        return add("v", [lambda: g.vector.tensor_tensor_scan(u(out), u(d0), u(d1), 0.0, op0, op1)], [d0, d1], [out], cost("v", out, [d1], 1))

    def act(out, x, f, bias=0.0, scale=1.0, after=None):
        return add("s", [lambda: g.scalar.activation(u(out), u(x), f, bias, scale)], [x], [out],
                   cost("s", out, [x], 1) + (0 if "ind" in x else SFIX), tail=SLATE, after=after)

    def mm(*groups, opens=True, closes=True):
        calls, R, Wr, c = [], [], [], 0
        for grp in groups:
            for i, (o, l, r) in enumerate(grp):
                st, sp = opens and i == 0, closes and i == len(grp) - 1
                calls.append(lambda o=o, l=l, r=r, st=st, sp=sp: g.tensor.matmul(u(o), u(l), u(r), st, sp))
                R += [l, r]
                Wr.append(o)
                c += max(PMIN, r["n"])
        lock = {"rw": [("open " + Wr[0]["b"], 1)]}
        return add("p", calls, R + [lock], Wr + [lock] * (not (opens and closes)), c * PCYC)

    def row(out, name, n=None, K=1):
        lo, hi = CR[name]
        return (out, a("on", 0, 128, 1, K), a("cr", lo, hi if n is None else lo + n, 1, K))

    def iota(out, pattern, base, cm):
        kw = {} if SCRATCH[out["b"]][2] == "int32" else {"allow_small_or_imprecise_dtypes": True}
        return add("g", [lambda: g.iota(u(out), pattern, base, cm, **kw)], [], [out], 130 + 2 * out["n"] * CYC)

    def fill(out, c):
        return iota(out, [[0, out["n"]]], int(c), 0)

    def aff(out, x, pattern, op, fill, base, cm):
        return add("g", [lambda: g.affine_select(u(out), u(x), pattern, op, fill, base, cm)], [x], [out], 170 + 2 * out["n"] * CYC)

    def load(sem, out, src, t):
        return add("y", [lambda: g.sync.dma_start(u(out), src)], [], [out], 60, sem=(sem, 16), tail=t,
                   after=len(ops) - 1 if ops else None)

    def store(q, sem, dst, x):
        return add(q, [lambda: Q[q].dma_start(dst, u(x))], [x], [], 60, sem=(sem, 16), tail=DMA)

    load("lwt", a("wti"), T.wt[:], DMA)
    load("ldm", a("dmi"), T.dm[:], DMA + 300)
    load("lpo", a("poi"), T.po[:], DMA + 600)
    load("lpk", a("pki"), T.pk[:], DMA + 900)
    load("lxt", a("xt_s", X0, X0 + W), T.xt[:], DMA + 3500)

    on, idb, blk, blk8 = a("on", 0, 128), a("idb"), a("blk"), a("blk8")
    ms(a("on"), 1.0)
    aff(blk, on, [[-16, 8], [0, 16]], A.is_ge, 0.0, 0, 1)
    aff(blk, blk, [[16, 8], [0, 16]], A.is_ge, 0.0, 15, -1)
    aff(idb, on, [[-1, 128]], A.is_equal, 0.0, 0, 1)
    iota(a("cr", *CR["s1"], 1, 2), [[0, 128]], 1024, -1025)
    iota(a("cr", 0, 128, 1, 1), [[0, 8], [1, 16]], 64, 0)
    iota(a("cr", 128, 256, 1, 1), [[0, 8], [-1, 16]], 63, 0)
    iota(a("cr", *CR["xo"], 1, 1), [[256, 8]], 0, 0)
    iota(a("pi", 0, 4), [[0, 4]], 0, 1)
    for name, c in (("c2k", 2048.0), ("s33", 33.0), ("u", -30720.0), ("cnt", 16.25), ("c4k", 4096.0), ("u5", -28672.0),
                    ("m2k", M2K), ("n2k", -M2K), ("m32", M32), ("n32", -M32),
                    ("big", -8192.0), ("off", -16 * FLOOR)):
        (fill if name in ("u", "u5", "c4k", "big", "off") else ms)(a("cr", *CR[name], 1, 32), c)
    ms(a("cr", CR["cnt"][0] + 2, CR["cnt"][0] + 3, 1, 32), -15.75)
    fill(a("cr", CR["off"][0] + 8, CR["off"][0] + 16, 1, 32), -15 * FLOOR - 2048)
    ms(a("xt_s", 0, X0), -1.0)
    cp(a("wtf"), a("wti"))
    ts(a("w2"), blk, a("wtf"), 2.0, A.mult, A.mult)
    ts(a("w2n"), blk, a("wtf"), -2.0, A.mult, A.mult)
    cp(blk8, a("blk", 0, 128, 16))
    ts(a("b64", 0, 8), blk8, 64.0, None, A.mult)
    ts(a("b64", 8, 16), blk8, -64.0, None, A.mult)
    for name, c in (("idm", -1.0), ("idn", -4.0), ("id16", 16.0)):
        act(a(name), idb, F.Copy, 0.0, c)
    fill(a("mkm"), 1)
    fill(a("mkm", 0, 128, 16), 0)
    fill(a("mka"), 0)
    fill(a("mka", 0, 128, 16), 2 ** 23)
    for h in range(2):
        fill(a("z%d" % h, 40, 56), 1)
        fill(a("xC%d" % h, 2048, 2064), -1)
    fill(a("mnC0", 2048, 2064), -1)
    ts(a("pi", 4, 8), a("pi", 0, 4), 15, None, A.bitwise_and)
    cp(a("pf", 0, 1), a("pi", 4, 5))
    ts(a("pf", 1, 2), a("pi", 4, 5), -1.0, -1.0, A.mult, A.add)
    tt(a("pf", 2, 4), a("pf", 0, 2), a("pf", 0, 2), A.mult)
    ts(a("pf", 4, 5), a("pi", 4, 5), 16.0, -1.0, A.mult, A.add)
    ms(a("et"), 0.0)
    for i in range(2):
        for c0, s1, s2 in ((16 + 8 * i, a("pf", i, i + 1), -8192.0), (8 * i, 1.0, 4096.0), (32, 1.0, -4096.0),
                           (40, a("pf", 2 + i, 3 + i), 4096.0), (48, 1.0, 4096.0)):
            ts(a("et", 56 * i + c0, 56 * i + c0 + 8), blk8, s1, s2, A.mult, A.mult)
    mm(*[[(a("p7", 128 * i, 128 * i + 128, 1, 56), a("et", 56 * i, 56 * i + 56), idb)] for i in range(2)])
    cp(a("em", 0, 256, 1, 56), a("p7", 0, 256, 1, 56), "s")
    for i, c in enumerate((-1.0, -4096.0, 4096.0, a("pf", 4, 5))):
        ts(a("et", 112 + 8 * i, 120 + 8 * i), blk8, c, None, A.mult)
    for r in range(16):
        aff(a("e4", 32 * r, 32 * r + 32), a("et", 112, 144), [[0, 4], [-16, 8]], A.is_equal, 0.0, -r, 1)
    mm(*[[(a("wu", 128 * i, 128 * i + 128), a("e4", 128 * i, 128 * i + 128), idb)] for i in range(4)])
    cp(a("xr"), a("wu"), "s")

    def late_constants():
        cp(a("xt_s", X0 + W, XW), a("xt_s", X0, X0 + 32), "s")
        fill(a("c512"), 512)
        act(a("nbk"), blk, F.Copy, 0.0, -8192.0)
        for r in range(16):
            aff(a("sr", 128 * r, 128 * r + 128), blk, [[0, 8], [1, 16]], A.is_equal, 0.0, -r, 0)
            aff(a("sk", 128 * r, 128 * r + 128), a("c512"), [[-16, 8], [0, 16]], A.is_equal, 0.0, -r, 1)
        aff(a("tri", 384, 512), a("nbk"), [[1, 128]], A.is_gt, 0.0, 0, -1)
        aff(a("tri", 512, 640), a("nbk"), [[-1, 128]], A.is_gt, 0.0, 0, 1)
        for s, (c0, own) in enumerate(((384, 8192.0), (384, 16384.0), (512, 8192.0))):
            aff(a("tri", 128 * s, 128 * s + 128), a("tri", c0, c0 + 128), [[1, 128]], A.not_equal, own, 0, -1)

    def cards(l, h, t):
        return a("o%d" % h) if l == "O" else a("ld%d" % h, 128 * t, 128 * t + 128)

    def half(l):
        return (0, 128) if l == "O" else (128, 256)

    def c_ps(l, h, t, c="c2k"):
        out = a("cps%d" % h, *half(l))
        mm([row(out, c), (out, idb, cards(l, h, t))])

    def e_of(h):
        H = "%d" % h
        s1 = a("cps" + H, 256, 384)
        mm([row(s1, "s1", K=2), (s1, a("w2n"), a("d" + H)), row(s1, "m2k"), row(s1, "n2k"), (s1, a("w2"), a("d" + H)), row(s1, "s33")])
        cp(a("e" + H), s1)

    def fused(l, h, t):
        return NF[t].get("%s%d" % (l, h), 0)

    def d_rep(h, t):
        mm(*[[(a("drep%d" % h, j, 512, 4), idb, a("d%d" % h))] for j in range(4)])
        for c in range(max(fused("O", h, t), fused("C", h, t))):
            for j in range(4):
                cp(a("ds%d" % h, 512 * c + j, 512 * c + 512, 4), a("drep%d" % h, 128 * c, 128 * c + 128), "s")

    def f_pre(src, fq, h):
        tt(fq, src, a("e%d" % h), A.mult)
        ts(fq, fq, 5, 4095, A.arith_shift_right, A.bitwise_and)

    def with_k(out, x, t):
        if t == 0:
            ts(out, x, 16.0, None, A.add)
        else:
            ts(out, x, a("kc", 2 * t, 2 * t + 1), a("kc", 2 * t + 1, 2 * t + 2), A.add, A.subtract)

    last = {"s": None, "v": None}

    def gather(l, h, t, first=False, chunks=range(4)):
        n = "%s%d" % (l, h)
        for lo, hi in (((0, 32), (32, 128))[2 * (t > 0):] if first else ((0, 128),)) * (0 in chunks):
            with_k(a("f" + n, lo, hi), a("fq" + n, lo, hi), t)
        win = a("xt_s", WIN, XW if t else X0 + W)
        for c in chunks:
            if c < fused(l, h, t):
                tt(a("mn" + n, 512 * c, 512 * c + 512), ind(win, a("f" + n, 32 * c, 32 * c + 32)), a("ds%d" % h, 512 * c, 512 * c + 512), A.min)
                continue
            cuts = (0, 16, 32) if (n, c) == ("C1", 3) and t < 4 else (0, 32)
            pair = c // 2 * 2 >= fused(l, h, t) and c ^ 1 in chunks and not (n == "C1" and c > 1 and t < 4) and not first
            if pair:
                cuts = () if c % 2 else (0, 64)
            for lo, hi in zip(cuts, cuts[1:]):
                lo, hi = 32 * c + lo, 32 * c + hi
                last["s"] = cp(a("x" + n, 16 * lo, 16 * hi), ind(win, a("f" + n, lo, hi)), "s", last["s"])

    def mins(l, h, t, parts):
        n, lo, d, by_s = "%s%d" % (l, h), 32 * fused(l, h, t), a("d%d" % h), SMIN[t].get("%s%d" % (l, h), {})
        js = [j for j in range(4) if j not in by_s]
        parts = parts or PARTS[4 - lo // 32]
        for j, bank in by_s.items():
            mm([(a(bank), a("idm"), a("x" + n, j, 2048, 4))] + [(a(bank, q, 512, 4), idb, d) for q in range(4)])
            act(a("mn" + n, j, 2048, 4), a(bank), F.Relu)
        for w in parts:
            for j in js:
                tt(a("mn" + n, 16 * lo + j, 16 * (lo + w), 4), a("x" + n, 16 * lo + j, 16 * (lo + w), 4),
                   a("drep%d" % h, 4 * lo, 4 * (lo + w)), A.min)
            lo += w
        c0 = 256 * h + half(l)[0]
        out = a("key", c0, c0 + 128)
        for i, j in enumerate(js[:1] + list(by_s) + js[1:]):
            grp = [(out, a("on", 0, 128, 1, 1), a("cr", *half(l), 1, 1))] * (i == 0)
            for k in range(j, 16, 4):
                key = a("key", c0 + k, c0 + 128, 16)
                if j in by_s:
                    grp += [(key, d, a("b64", 0, 8)), (key, a("mn" + n, k, 2048, 16), a("b64", 8, 16))]
                else:
                    grp += [(key, a("mn" + n, k, 2048, 16), a("b64", 0, 8))]
            mm(grp, opens=i == 0, closes=i == 3)
        if l == "O":
            scan(a("r%d" % h, 0, 128), a("mka"), out, A.add, A.min)
        else:
            scan(a("r%d" % h, 128, 256), a("mkm"), out, A.mult, A.max)

    def swap(h):
        tt(a("z%d" % h, 32, 40), a("r%d" % h, 143, 256, 16), a("r%d" % h, 15, 128, 16), A.is_gt)

    def count(t):
        for h in range(2):
            mm([row(a("wu", 0, 4), "cnt", 4)] * (h == 0)
               + [(a("wu", p, p + 2), on, a("z%d" % h, 32 + i, 40, 4)) for p in (2, 1, 0) for i in range(4)]
               + [row(a("wu", 2, 3), z, 1) for z in ("m32", "n32")] * h, opens=h == 0, closes=h == 1)
        for lo in (0, 64):
            ts(a("fO0", lo, lo + 64), a("fqO0", lo, lo + 64), a("wu", 1, 2), a("wu", 2, 3), A.add, A.subtract)
        cp(a("kc", 2 * t + 2, 2 * t + 4), a("wu", 1, 3))

    def exchange(t, h):
        H, end = "%d" % h, t == NT - 1
        z, zs, best = "z" + H, a("zs" + H, 0, 128, 1, 56), a("r" + H, 15, 256, 16)
        ts(a("tq" + H), best, M64, M64, A.add, A.subtract)
        tt(a(z, 16, 32), best, a("tq" + H), A.subtract)
        tt(a(z, 0, 16), a(z, 16, 32), a(z, 16, 32), A.mult)
        mb = "p7" if end and h else "misc"
        mm([(a(mb, 0, 128, 1, 56), a(z), idb)])
        cp(zs, a(mb, 0, 128, 1, 56))
        em = {l: a("em", *half(l), 1, 56) for l in "OC"}
        if end:
            for l in "OC":
                c_ps(l, h, t, "c4k")
        wb = "drep" + H
        mm([(a(wb, *half(l)), idb, cards(l, h, t)) for l in "OC"] + [(a(wb, *half(l)), em[l], zs) for l in "OC"])
        ts(a("sel" + H), a(wb, 0, 256), 2048.0, None, A.min)
        for l, m in ("CO", "OC"):
            out = a(wb, 256 + half(l)[0], 256 + half(l)[1])
            mm([row(out, "u5" if end else "u"), (out, em[l], zs), (out, blk, a("sel" + H, *half(m)))])
            tt(a("vv" + H, *half(l)), a("cps" + H, *half(l)), a("sel" + H, *half(l)), A.subtract)
            new = a("y" + l, 128 * h, 128 * h + 128) if end else cards(l, h, t)
            tt(new, out, a("vv" + H, *half(l)), A.min)
            if end:
                store("y", "s%s%d" % (l, h), T["y" + l.lower()][:, 128 * h:128 * h + 128], new)
            elif l == "C":
                send(t, h)
            else:
                c_ps("O", h, t)
        xo, dp, d = a(mb, 128, 136), a(mb, 256, 384), a("d" + H)
        mm(*[[(a(mb, 192, 224, 1, 32, 32 * q), a(z, 24, 56), a("idb", q, 128, 4))] for q in range(4)])
        cp(a("z4" + H), a(mb, 192, 224))
        mm([row(xo, "xo")] + [(xo, a("xr", 128 * i, 128 * i + 128), a("z4" + H, i, 32, 4)) for i in range(4)])
        ts(a("xo" + H), xo, 2048.0, None, A.min)
        tt(a("u" + H), ind(a(("mnC" if fused("C", h, t) else "xC") + H), a("xo" + H)), d, A.is_ge)
        mm([(dp, idb, d), (dp, a("idn"), a("u" + H))])
        if end:
            new = a("yD", 128 * h, 128 * h + 128)
            ts(new, dp, 1.0, None, A.max)
            store("s" if h else "y", "sD%d" % h, T.yd[:, 128 * h:128 * h + 128], new)
            return
        ts(d, dp, 1.0, None, A.max)
        e_of(h)
        if t + 1 < 4:
            d_rep(h, t + 1)
        f_pre(a("cps" + H, 0, 128), a("fqO" + H), h)

    def send(t, h):
        src, dst = cards("C", h, t), cards("C", h, t + 1)
        sem = "ar%d%d" % (t + 1, h)
        i = add("g", [lambda: g.remote_dma(u(dst), u(src), T.sem[sem], T.sem.sent, pid, rid, mask)], [src], [], 60, sem=("sent", 0))
        add("x", [], [], [dst], 0, sem=(sem, nin), tail=FAR + (2000 if t + h == 0 else 0), after=i)

    def arrive(t, h):
        c_ps("C", h, t)
        f_pre(a("cps%d" % h, 128, 256), a("fqC%d" % h), h)

    def slots(t, h):
        H = "%d" % h
        m, gn, mp, mc = cards("C", h, t - 4), a("gn" + H), a("p7", 0, 128), a("misc", 384, 512)
        mm([row(mp, "c2k"), (mp, idb, m)])
        mm([(mc, idb, m)])
        tt(gn, cards("C", h, t), mc, A.not_equal)
        f_pre(mp, a("fqM" + H), h)
        ts(a("fm" + H), a("fqM" + H), -2048.0, None, A.add)
        out = [a("p7", 128 + 128 * s, 256 + 128 * s) for s in range(3)]
        mm([row(a("p7", 128, 512), "big")] + [(out[s], idb, a("fm" + H)) for s in range(3)], closes=False)
        mm([(out[s], a("tri", 128 * s, 128 * s + 128), gn) for s in range(3)], opens=False)
        ts(a("cl" + H), a("p7", 128, 512), FLOOR, 2048.0, A.max, A.min)
        out = a("misc", 144 + 24 * h, 168 + 24 * h)
        mm([row(out, "off")] + [(out, a("sr", 128 * r, 128 * r + 128), a("cl" + H, r, 384, 16)) for r in range(16)])

    def best_gone(t, h):
        H, win = "%d" % h, a("xt_s")
        with_k(a("so" + H), a("misc", 144 + 24 * h, 168 + 24 * h), t)
        cp(a("yy" + H, 0, 128), ind(win, a("so" + H, 0, 8)))
        for s in (1, 2):
            tt(a("yy" + H, 128 * s, 128 * s + 128), ind(win, a("so" + H, 8 * s, 8 * s + 8)), a("yy" + H, 128 * s - 128, 128 * s), A.max)

    def step2(t, h):
        H = "%d" % h
        ts(a("up" + H, 0, 128), a("d" + H), -8.0, 1.0, A.add, A.max)
        ts(a("up" + H, 128, 256), a("d" + H), 8.0, 255.0, A.add, A.min)
        for w in range(2):
            l0, l1 = 64 * w, 64 * w + 64
            B, gn, n = a("yy" + H, 256 + l0, 256 + l1), a("gn" + H, l0, l1), a("cps" + H, 256 + l0, 256 + l1)
            for p in range(2):
                bank = BANKS[h][2 * w + p]
                x, ge = a("xC" + H, 16 * l0 + p, 16 * l1, 2), a("ge" + H, 16 * l0 + p, 16 * l1, 2)
                mm([(a(bank, q, 512, 8), a("sk", 128 * (2 * q + p), 128 * (2 * q + p) + 128), gn) for q in range(8)], closes=False)
                mm([(a(bank, q, 512, 8), idb, B) for q in range(8)], opens=False)
                tt(ge, x, a(bank), A.is_ge)
                mm([(n, idb, a("up" + H, l0, l1))] * (p == 0)
                   + [(n, a("id16"), a("ge" + H, 16 * l0 + k, 16 * l1, 16)) for k in range(p, 16, 2)], opens=p == 0, closes=p == 1)
            tt(a("d" + H, l0, l1), n, a("up" + H, 128 + l0, 128 + l1), A.min)
            mm(*[[(a("drep" + H, 4 * l0 + j, 4 * l1, 4), idb, a("d" + H, l0, l1))] for j in range(4)])

    for h in range(2):
        H = "%d" % h
        cp(a("d" + H), a("dmi", 128 * h, 128 * h + 128))
        ts(a("o" + H), a("poi", 128 * h, 128 * h + 128), -2048.0, None, A.add)
        ts(cards("C", h, 0), a("pki", 128 * h, 128 * h + 128), -2048.0, None, A.add)
        e_of(h)
        d_rep(h, 0)
        c_ps("O", h, 0)
        f_pre(a("cps" + H, 0, 128), a("fqO" + H), h)
    for t in range(NT):
        if t < 4:
            for h in range(2):
                gather("O", h, t, h == 0)
                arrive(t, h)
                gather("C", h, t)
                mins("O", h, t, None)
                mins("C", h, t, PC if h and not fused("C", h, t) else None)
                swap(h)
                if h == 0:
                    exchange(t, 0)
        else:
            arrive(t, 1)
            slots(t, 1)
            for i, (l, h, chunks) in enumerate(ORDER2):
                gather(l, h, t, i == 0, chunks)
            for h in range(2):
                best_gone(t, h)
                step2(t, h)
                for l in "CO":
                    mins(l, h, t, P2)
                swap(h)
                if h == 0:
                    exchange(t, 0)
        if t < NT - 1:
            count(t)
        if t == 0:
            late_constants()
        if 3 <= t < NT - 1:
            arrive(t + 1, 0)
            slots(t + 1, 0)
        exchange(t, 1)

    n = len(ops)
    pred, succ = [{} for _ in range(n)], [{} for _ in range(n)]
    for i, o in enumerate(ops):
        for j in o["deps"] | o["after"]:
            lag = 0.0
            if j in o["deps"] and o["q"] != "x" and not o["q"] == ops[j]["q"] == "p":
                lag = ops[j]["tail"] + HOP
            pred[i][j] = succ[j][i] = lag

    def place(before, behind, weight, release):
        left = [len(b) for b in before]
        ready = {i: release[i] for i in range(n) if left[i] == 0}
        free, ends, bank, order = {q: 0.0 for q in "vspgyx"}, [0.0] * n, {}, []
        while ready:
            st = {}
            for i, t0 in ready.items():
                o = ops[i]
                st[i] = max([t0, free[o["q"]]] + [ends[j] + HOP for b in o["banks"] for q, j in bank.get(b, {}).items() if q != o["q"]])
            i0 = min(st, key=st.get)
            i = max((k for k in st if ops[k]["q"] == ops[i0]["q"] and st[k] <= st[i0]), key=lambda k: weight[k])
            o = ops[i]
            for b in o["banks"]:
                bank.setdefault(b, {})[o["q"]] = i
            ends[i] = st[i] + o["cost"]
            if o["q"] != "x":
                free[o["q"]] = ends[i]
            order.append(i)
            del ready[i]
            for k in behind[i]:
                left[k] -= 1
                if left[k] == 0:
                    ready[k] = max([release[k]] + [ends[j] + lag for j, lag in before[k].items()])
        return order, ends

    tails, zero = [o["tail"] for o in ops], [0.0] * n
    weight = [0.0] * n
    for i in range(n - 1, -1, -1):
        weight[i] = ops[i]["cost"] + max([tails[i]] + [weight[k] + lag for k, lag in succ[i].items()])
    qs, cs, bs = [o["q"] for o in ops], [o["cost"] for o in ops], [tuple(sorted(o["banks"])) for o in ops]
    ahead = pred
    pred = [{j: lag for j, lag in p.items() if j in o["deps"] or o["q"] != "s"} for p, o in zip(pred, ops)]
    before = [sorted(p.items()) for p in pred]

    name = {}
    holds = [[name.setdefault(z, len(name)) for z in [q] * (q != "x") + [b + q for b in bk]] for q, bk in zip(qs, bs)]
    follows = [[(name.setdefault(z, len(name)), lag) for z, lag in [(q, 0.0)] * (q != "x") + [(b + r, HOP + SLATE * (r == "s")) for b in bk for r in "vsp" if r != q]]
               for q, bk in zip(qs, bs)]
    lasts = [i for i in range(n) if tails[i]]

    cases = []
    for f, gt, hop, far in CASES:
        cases.append(([f * (c + o["gathered"] * (gt - GATHER) * CYC) for c, o in zip(cs, ops)],
                      [[(j, lag and lag + hop - HOP + (far - FAR) * (qs[j] == "x")) for j, lag in b] for b in before],
                      [[(z, lag and lag + hop - HOP) for z, lag in b] for b in follows], f))

    def both(order, old=None, lo=0, limit=0.0, moved=()):
        runs = []
        for s, c in enumerate(cases):
            runs.append(timed(order, old and old[2][s], lo, *c[:3], limit * c[3], moved))
            if runs[-1] is None:
                return None
        return sum(r[0] / c[3] for r, c in zip(runs, cases)) / len(cases), order, runs

    def timed(order, old=None, lo=0, cs=cs, before=before, follows=follows, limit=0.0, moved=()):
        ends, why = (old[2][:], old[3][:]) if old else ([0.0] * n + [-1e4], [None] * n)
        holder, chain = [n] * len(name), old[5] if old else ()
        for i in order[:lo]:
            for z in holds[i]:
                holder[z] = i
        for i in order[lo:]:
            t0, w = 0.0, None
            for j, lag in before[i]:
                if ends[j] + lag > t0:
                    t0, w = ends[j] + lag, (j, 0)
            for z, lag in follows[i]:
                j = holder[z]
                if ends[j] + lag > t0:
                    t0, w = ends[j] + lag, (j, 1)
            for z in holds[i]:
                holder[z] = i
            t0 += cs[i]
            if i in chain and t0 > ends[i] + limit and i not in moved:
                return None
            ends[i], why[i] = t0, w
        i = max(lasts, key=lambda k: ends[k] + tails[k])
        total, pairs, chain = ends[i] + tails[i], [], set()
        while why[i]:
            chain.add(i)
            pairs += [(why[i][0], i)] * why[i][1]
            i = why[i][0]
        return total, order, ends, why, pairs, chain

    def relieve(now, rounds):
        rng, best = np.random.default_rng(SEED), now
        for r in range(rounds):
            total, order, pairs = now[0], now[1], now[2][r % len(cases)][4]
            p, i = pairs[int(rng.integers(len(pairs)))]
            lo, hi = order.index(p), order.index(i) + 1
            lo = max(0, lo - int(rng.integers(12)) * (rng.random() < 0.3))
            seg, first, rest = order[lo:hi], {i}, {p}
            for k in seg[::-1]:
                if k in first:
                    first.update(pred[k])
            for k in seg:
                if not rest.isdisjoint(pred[k]):
                    rest.add(k)
            if p in first:
                continue
            if rng.random() < 0.5:
                seg = [k for k in seg if k in first] + [k for k in seg if k not in first]
            else:
                seg = [k for k in seg if k not in rest] + [k for k in seg if k in rest]
            allow = ALLOW * (1 - r / rounds) * rng.exponential()
            new = both(order[:lo] + seg + order[hi:], now, lo, 2 * allow + 100, set(seg))
            if new and new[0] - total <= allow:
                now = new
                if r % 64 == 0:
                    now = both(sorted(new[1], key=lambda k: new[2][0][2][k] - cases[0][0][k]))
                if now[0] < best[0]:
                    best = now
        return best

    if "order" not in PLAN:
        best = None
        for _ in range(PASSES):
            order, ends = place(ahead, succ, weight, zero)
            if best is None or timed(order)[0] < best[0]:
                best = timed(order)
            weight = place(succ, ahead, ends, tails)[1]
        PLAN["order"] = relieve(both(best[1]), ROUNDS)[1]
    total, order, done = timed(PLAN["order"])[:3]
    bank = {}
    for i in order:
        for b in bs[i]:
            ops[i]["deps"] = ops[i]["deps"] | {j for q, j in bank.setdefault(b, {}).items() if q != qs[i]}
            bank[b][qs[i]] = i

    pos, known, clock, waits, seen = {}, {q: {} for q in "vspgyx"}, {}, {}, {q: 0 for q in "vspgyx"}
    for i in order:
        o = ops[i]
        q = o["q"]
        seen[q] += not o["sem"]
        pos[i] = (o["sem"][0], 1) if o["sem"] else (q, seen[q])
        waits[i] = []
        for j in sorted(o["deps"], key=lambda j: -done[j]):
            c, m = pos[j]
            if q != "x" and not (q == c == "p") and known[q].get(c, 0) < m:
                waits[i].append(j)
                known[q][c] = m
                for c2, m2 in clock[j].items():
                    known[q][c2] = max(known[q].get(c2, 0), m2)
        clock[i] = dict(known[q]) if q != "x" else {}
    final = {ops[i]["q"]: i for i in order if not ops[i]["sem"]}
    wanted = {j for w in waits.values() for j in w} | set(final.values())
    cnt, val = {q: 0 for q in S}, {}
    for i in order:
        o = ops[i]
        q = o["q"]
        for j in waits[i]:
            Q[q].wait_ge(*val[j])
        call = None
        for fn in o["calls"]:
            call = fn()
        if o["sem"]:
            val[i] = (T.sem[o["sem"][0]], o["sem"][1])
            if o["sem"][1] and call is not None:
                call.then_inc(*val[i])
        elif i in wanted:
            cnt[q] += 1
            call.then_inc(S[q], 1)
            val[i] = (S[q], cnt[q])
    for q in S:
        g.wait_ge(S[q], cnt[q])
    g.wait_ge(T.sem.sent, nout * 2 * (NT - 1))
    for sem in LOADS + STORES:
        g.wait_ge(T.sem[sem], 16)
    for t in range(1, NT):
        for h in range(2):
            g.wait_ge(T.sem["ar%d%d" % (t, h)], nin)
